import numpy as np
import ml_dtypes


def mxq(x, axis, fmt="e4m3"):
    dtype, down = {"e4m3": (ml_dtypes.float8_e4m3fn, 7), "e5m2": (ml_dtypes.float8_e5m2, 14)}[fmt]
    v = np.moveaxis(np.asarray(x, np.float32).astype(ml_dtypes.bfloat16).astype(np.float64), axis, -1)
    blocks = v.reshape(v.shape[:-1] + (-1, 32))
    amax = np.abs(blocks).max(-1, keepdims=True)
    byte = np.maximum(np.where(amax > 0, np.frexp(amax)[1] - 1 + 127, 0) - down, 1)
    scale = np.exp2(byte - 127.0)
    codes = (blocks / scale).astype(np.float32).astype(dtype).astype(np.float64)
    return np.moveaxis((codes * scale).reshape(v.shape), -1, axis)


WIDE = False


def mx_kscale(k):
    if not WIDE:
        return np.ones(k)
    levels = np.array([10, -10, 5, -5, 0])
    if k % 512:
        return np.exp2(np.random.permutation(np.resize(levels, k // 32))).repeat(32)
    a = np.empty((k // 512, 16))
    for p in range(k // 512):
        a[p, :8] = np.random.permutation(np.resize(levels, 8))
        for g in range(8):
            far = levels[np.abs(levels - a[p, g]) >= 10]
            a[p, g + 8] = far[np.random.randint(len(far))]
    return np.exp2(a.ravel()).repeat(32)


def f64(x):
    return np.asarray(x).astype(np.float64)


def striped(idx):
    return np.tile(idx.reshape(-1, 16).T, (8, 1)).astype(np.uint16)


def unstriped(offs):
    return offs[:16].T.reshape(-1).astype(np.int64)


def striped8(idx):
    return np.concatenate([x.reshape(-1, 16).T for x in idx]).astype(np.uint16)


def runs(offs, k):
    lists = np.stack([offs[16 * r : 16 * r + 16].T.reshape(-1) for r in range(8)]).astype(np.int64)
    return lists[np.arange(k) % 512 // 64]


def pack_weight(w):
    k, n = w.shape
    w = f64(np.asarray(w, np.float32).astype(ml_dtypes.bfloat16)).reshape(k // 32, 32, n)
    amax = np.abs(w).max(1)
    byte = np.clip(np.where(amax > 0, np.frexp(amax)[1] - 1 + 127 - 7, 1), 1, 254)
    scaled = (w * np.exp2(127.0 - byte)[:, None, :]).reshape(k, n).astype(np.float32)
    words = np.ascontiguousarray(scaled.reshape(k // 512, 128, 4, n).transpose(0, 1, 3, 2)).astype(ml_dtypes.float8_e4m3fn).view(np.uint8)
    return words, np.ascontiguousarray(byte.astype(np.uint8).reshape(k // 512, 16, n))


def unpack_weight(words, scales):
    g, p, n, _ = words.shape
    vals = np.ascontiguousarray(words).view(ml_dtypes.float8_e4m3fn).astype(np.float64) * np.repeat(np.exp2(scales.astype(np.float64) - 127.0), 8, axis=1)[..., None]
    return vals.transpose(0, 1, 3, 2).reshape(g * 512, n)

def planes(y):
    n, m = y.shape
    v = y.astype(np.float32).astype(ml_dtypes.bfloat16).astype(np.float64).reshape(n // 32, 32, m)
    top = np.abs(v).max(1)
    byte = np.clip(np.where(top > 0, np.frexp(top)[1] - 1 + 127 - 7, 1), 1, 254)
    codes = (v * np.exp2(127.0 - byte)[:, None, :]).reshape(n, m).astype(np.float32).astype(ml_dtypes.float8_e4m3fn).view(np.uint8)
    words = codes.reshape(n // 512, 128, 4, m).transpose(0, 1, 3, 2)
    return np.ascontiguousarray(words), np.ascontiguousarray(byte.astype(np.uint8).reshape(n // 512, 16, m))


K, T, S, N, H = 512, 2048, 512, 512, 512


def setup_inputs():
    n = np.random.standard_normal
    s = mx_kscale(K)[:, None]
    u = mx_kscale(H)
    packed_xT = pack_weight(n((K, T)) * s)
    packed_w1 = pack_weight(n((K, H)) / np.sqrt(K) / s)
    packed_w2 = pack_weight(n((H, N)) / np.sqrt(H) / u[:, None])
    return {
        "x_words": packed_xT[0],
        "x_scales": packed_xT[1],
        "w1_words": packed_w1[0],
        "w1_scales": packed_w1[1],
        "cj1": (0.7 * n((H, S))).astype(np.float32),
        "cj2": (0.7 * n((H, S))).astype(np.float32),
        "gn": (np.random.uniform(0.5, 1.5, (H, 1)) * u[:, None]).astype(np.float32),
        "w2_words": packed_w2[0],
        "w2_scales": packed_w2[1],
        "offs": striped(np.random.permutation(T)[:S]),
        "p1": striped8(np.stack([np.random.permutation(S) for _ in range(8)])),
        "p2": striped8(np.stack([np.random.permutation(S) for _ in range(8)])),
    }


def reference(x_words, x_scales, w1_words, w1_scales, cj1, cj2, gn, w2_words, w2_scales, offs, p1, p2):
    xq = unpack_weight(x_words, x_scales)[:, unstriped(offs)]
    y = unpack_weight(w1_words, w1_scales).T @ xq
    h = np.tanh(y + f64(cj1) * (y[np.arange(H)[:, None], runs(p1, H)]) + f64(cj2) * (y[np.arange(H)[:, None], runs(p2, H)]))
    z = f64(gn) * (np.tanh(y + f64(cj1) * (h[np.arange(H)[:, None], runs(p1, H)]) + f64(cj2) * (h[np.arange(H)[:, None], runs(p2, H)])))
    out_0 = unpack_weight(w2_words, w2_scales).T @ mxq(z, 0, "e4m3")
    return (out_0,) + planes(out_0)

@@ -1,0 +1,240 @@
+from contextlib import ExitStack
+
+import concourse.mybir as mybir
+from concourse.masks import make_identity
+
+F32 = mybir.dt.float32
+BF16 = mybir.dt.bfloat16
+I32 = mybir.dt.int32
+U32 = mybir.dt.uint32
+U16 = mybir.dt.uint16
+U8 = mybir.dt.uint8
+FP8X4 = mybir.dt.float8_e4m3fn_x4
+ACT = mybir.ActivationFunctionType
+ALU = mybir.AluOpType
+
+P = 128
+T = 2048
+S = 512
+PACK = 4
+JB = 128
+NJB = S // JB
+WIN = 2 * S
+W1_ROW = 4
+W2_ROW = 8
+FLOPS = 2 * 2 * 512 * 512 * 512
+R1_MULT = ["fused","fused","fused","fused"]
+R1_SUM = ["v","v","v","v"]
+WARM = True
+
+
+def tile_picked_mfield_none_po_kernel(
+    tc, x_words, x_scales, w1_words, w1_scales, cj1, cj2, gn, w2_words, w2_scales, offs, p1, p2, out_0, out_1, out_2
+):
+    nc = tc.nc
+    with ExitStack() as ctx:
+        keep = ctx.enter_context(tc.tile_pool(name="keep", bufs=1))
+        psum = ctx.enter_context(tc.psum_pool(name="psum", bufs=1))
+
+        def sb(name, shape, dtype):
+            return keep.tile(shape, dtype, name=name, align_bytes=64)
+
+        bank = [psum.tile([P, S], F32, name="bank%d" % k) for k in range(4)]
+
+        def words_of(dram):
+            return dram[0].rearrange("p n t -> p (n t)").bitcast(I32)
+
+        def load_scales(queue, tile, dram, q):
+            rows = dram[0][4 * q : 4 * q + 4, :].bitcast(I32)
+            queue.dma_start(out=tile[32 * q : 32 * q + 32, :].bitcast(I32), in_=rows.unsqueeze(0).to_broadcast([8, 4, rows.shape[1]]))
+
+        xs = sb("xs", [P, T], U8)
+        w1s = sb("w1s", [P, S], U8)
+        w2s = sb("w2s", [P, S], U8)
+        xw = sb("xw", [P, T], U32)
+        w1w = sb("w1w", [P, S], I32)
+        w2w = sb("w2w", [P, S], I32)
+        offs_t = keep.tile([P, S // 16], U16, name="offs_t")
+        p1_t = keep.tile([P, S // 16], U16, name="p1_t")
+        p2_t = keep.tile([P, S // 16], U16, name="p2_t")
+        c1 = [sb("c1_%d" % t, [P, S], F32) for t in range(PACK)]
+        c2 = [sb("c2_%d" % t, [P, S], F32) for t in range(PACK)]
+        gn_t = sb("gn_t", [P, PACK], F32)
+        cj1_v = cj1.rearrange("(p t) j -> p t j", t=PACK)
+        cj2_v = cj2.rearrange("(p t) j -> p t j", t=PACK)
+
+        nc.sync.dma_start(offs_t[:], offs)
+        load_scales(nc.sync, xs, x_scales, 0)
+        load_scales(nc.sync, xs, x_scales, 1)
+        load_scales(nc.sync, xs, x_scales, 2)
+        load_scales(nc.sync, xs, x_scales, 3)
+        nc.sync.dma_start(out=w1w[:], in_=words_of(w1_words))
+        load_scales(nc.sync, w1s, w1_scales, 0)
+        nc.sync.dma_start(out=xw[:].bitcast(I32), in_=words_of(x_words))
+        load_scales(nc.sync, w1s, w1_scales, 1)
+        load_scales(nc.sync, w1s, w1_scales, 2)
+        load_scales(nc.sync, w1s, w1_scales, 3)
+        nc.sync.dma_start(p1_t[:], p1)
+        nc.sync.dma_start(out=c1[0][:], in_=cj1_v[:, 0, :])
+        nc.sync.dma_start(p2_t[:], p2)
+        nc.sync.dma_start(out=c2[0][:], in_=cj2_v[:, 0, :])
+        nc.sync.dma_start(out=w2w[:], in_=words_of(w2_words))
+        load_scales(nc.sync, w2s, w2_scales, 0)
+        load_scales(nc.sync, w2s, w2_scales, 1)
+        load_scales(nc.sync, w2s, w2_scales, 2)
+        load_scales(nc.sync, w2s, w2_scales, 3)
+        nc.sync.dma_start(out=c1[1][:], in_=cj1_v[:, 1, :])
+        nc.sync.dma_start(out=c2[1][:], in_=cj2_v[:, 1, :])
+        nc.sync.dma_start(out=c1[2][:], in_=cj1_v[:, 2, :])
+        nc.sync.dma_start(out=c2[2][:], in_=cj2_v[:, 2, :])
+        nc.sync.dma_start(out=c1[3][:], in_=cj1_v[:, 3, :])
+        nc.sync.dma_start(out=c2[3][:], in_=cj2_v[:, 3, :])
+        nc.sync.dma_start(out=gn_t[:], in_=gn.rearrange("(p t) o -> p (t o)", t=PACK))
+
+        ident = sb("ident", [P, P], F32)
+        make_identity(nc, ident[:])
+
+        ywin = [sb("ywin%d" % t, [P, WIN], F32) for t in range(PACK)]
+        awin = [sb("awin%d" % t, [P, WIN if t < 3 else S], F32) for t in range(PACK)]
+        for t in range(PACK):
+            nc.vector.memset(ywin[t][:, S:WIN], 0.0)
+        for t in range(3):
+            nc.vector.memset(awin[t][:, S:WIN], 0.0)
+        if WARM:
+            warm = sb("warm", [P, 1], F32)
+            nc.scalar.activation(warm[:], ywin[0][:, S : S + 1], ACT.Sigmoid)
+
+        def deal(name, words, scales):
+            dw = sb(name + "_w", [P, S], I32)
+            ds = sb(name + "_s", [P, S], U8)
+            nc.vector.tensor_copy(out=dw[:].rearrange("p (t m) -> p t m", t=PACK), in_=words[:].rearrange("p (m t) -> p t m", t=PACK))
+            nc.vector.tensor_copy(out=ds[:].rearrange("p (t m) -> p t m", t=PACK), in_=scales[:].rearrange("p (m t) -> p t m", t=PACK))
+            return dw, ds
+
+        xsg = sb("xsg", [P, S], U8)
+        xg = sb("xg", [P, S], U32)
+        nc.vector.tensor_copy(out=xsg[:], in_=xs[:].indirect(offs_t[:]))
+        w1dw, w1ds = deal("w1d", w1w, w1s)
+        nc.vector.tensor_copy(out=xg[:], in_=xw[:].indirect(offs_t[:]))
+
+        for t in range(PACK):
+            cols = slice(t * P, (t + 1) * P)
+            nc.tensor.matmul_mx(
+                out=bank[t][:], lhsT=w1dw[:, cols].bitcast(FP8X4), lhsT_scale=w1ds[:, cols],
+                rhs=xg[:].bitcast(FP8X4), rhs_scale=xsg[:], start=True, stop=True,
+            )
+            nc.scalar.activation(ywin[t][:, 0:S], bank[t][:], ACT.Copy, scale=0.5)
+        w2dw, w2ds = deal("w2d", w2w, w2s)
+
+        lists = (p1_t, p2_t)
+        cj = (c1, c2)
+        g = [[sb("g%d_%d" % (t, n), [P, S], F32) for n in range(2)] for t in range(PACK)]
+        got = [[sb("got%d_%d" % (t, n), [P, S], F32) for n in range(2)] for t in range(PACK)]
+        sig = [[sb("sig%d_%d" % (t, n), [P, S], F32) for n in range(2)] for t in range(PACK)]
+        m = [[sb("m%d_%d" % (t, n), [P, S], F32) for n in range(2)] for t in range(PACK)]
+        at = [sb("at%d" % t, [P, S], F32) for t in range(PACK)]
+        tt = [sb("tt%d" % t, [P, S], F32) for t in range(PACK)]
+        zb = [psum.tile([P, PACK, JB], F32, name="zb%d" % b) for b in range(NJB)]
+        a_bank = [bank[k] for k in [0,0,0,0]]
+        b_bank = [bank[k] for k in [0,0,0,0]]
+
+        def blk(b):
+            return slice(b * JB, (b + 1) * JB)
+
+        def turn(dst, term, first, last):
+            for b in range(NJB):
+                nc.tensor.matmul(
+                    out=dst[:, blk(b)], lhsT=term[:, blk(b)], rhs=ident[:], is_transpose=True,
+                    start=(first and b == 0), stop=(last and b == NJB - 1),
+                )
+
+        def exit_copy(engine, out, in_):
+            if engine == "s":
+                nc.scalar.copy(out=out, in_=in_)
+            else:
+                nc.vector.tensor_copy(out=out, in_=in_)
+
+        def step(kind, t, n=0, h=(0, 4)):
+            if kind == "g":
+                if R1_MULT[t] == "fused":
+                    nc.vector.tensor_tensor(out=g[t][n][:], in0=ywin[t][:].indirect(lists[n][:]), in1=cj[n][t][:], op=ALU.mult)
+                else:
+                    nc.vector.tensor_copy(out=got[t][n][:], in_=ywin[t][:].indirect(lists[n][:]))
+                    nc.gpsimd.tensor_tensor(out=g[t][n][:], in0=got[t][n][:], in1=cj[n][t][:], op=ALU.mult)
+                if R1_SUM[t] == "pe":
+                    if n == 0:
+                        turn(a_bank[t], ywin[t], True, False)
+                    turn(a_bank[t], g[t][n], False, n == 1)
+            elif kind == "add":
+                nc.vector.tensor_tensor(out=at[t][:], in0=g[t][0][:], in1=ywin[t][:, 0:S], op=ALU.add)
+                nc.vector.tensor_tensor(out=awin[t][:, 0:S], in0=at[t][:], in1=g[t][1][:], op=ALU.add)
+            elif kind == "at":
+                exit_copy(n, at[t][:], a_bank[t][:])
+                for b in range(NJB):
+                    nc.tensor.transpose(a_bank[t][:, blk(b)], at[t][:, blk(b)], ident[:])
+            elif kind == "ab":
+                exit_copy(n, awin[t][:, 0:S], a_bank[t][:])
+            elif kind == "sig":
+                b0, b1 = h
+                nc.scalar.activation(sig[t][n][:, b0 * JB : b1 * JB], awin[t][:].indirect(lists[n][:, b0 * 8 : b1 * 8]), ACT.Sigmoid, scale=4.0)
+            elif kind == "by":
+                for k, (tl, b) in enumerate(n):
+                    nc.tensor.matmul(out=bank[t][:, blk(k)], lhsT=ywin[tl][:, blk(b)], rhs=ident[:], is_transpose=True, start=(k == 0), stop=False)
+                    place[(tl, b)] = (t, k)
+                left[t] = 2 * len(n)
+            elif kind == "m":
+                b0, b1 = h
+                js = slice(b0 * JB, b1 * JB)
+                nc.vector.scalar_tensor_tensor(out=m[t][n][:, js], in0=sig[t][n][:, js], scalar=-0.5, in1=cj[n][t][:, js], op0=ALU.add, op1=ALU.mult)
+                for b in range(b0, b1):
+                    bk, k = place[(t, b)]
+                    left[bk] = left[bk] - 1
+                    nc.tensor.matmul(out=bank[bk][:, blk(k)], lhsT=m[t][n][:, blk(b)], rhs=ident[:], is_transpose=True, start=False, stop=(left[bk] == 0))
+            elif kind == "th":
+                width = len(n) * JB
+                tanh_t = sb("tanh_%d_%d_%d" % (t, n[0][0], n[0][1]), [P, width], F32)
+                nc.scalar.activation(tanh_t[:], bank[t][:, 0:width], ACT.Tanh, scale=2.0)
+                for k, (tl, b) in enumerate(n):
+                    nc.tensor.transpose(zb[b][:, tl, :], tanh_t[:, blk(k)], ident[:])
+            elif kind == "gn":
+                nc.vector.tensor_tensor(
+                    out=z16[t][:], in0=zb[t][:].rearrange("p t j -> p j t"),
+                    in1=gn_t[:].unsqueeze(1).to_broadcast([P, JB, PACK]), op=ALU.mult,
+                )
+            elif kind == "qz":
+                nc.vector.quantize_mx(out=zc[t][:].bitcast(FP8X4), scales=zs[t][:], in_=z16[t][:].rearrange("p j t -> p (j t)"))
+                ob = o_bank[t][:].rearrange("p (t j) -> p t j", t=PACK)
+                for k in range(PACK):
+                    nc.tensor.matmul_mx(
+                        out=ob[:, k, :], lhsT=w2dw[:, blk(k)].bitcast(FP8X4), lhsT_scale=w2ds[:, blk(k)],
+                        rhs=zc[t][:].bitcast(FP8X4), rhs_scale=zs[t][:], start=True, stop=True,
+                    )
+                nc.scalar.copy(out=ot[t][:], in_=ob)
+                nc.sync.dma_start(out=out_v[:, :, blk(t)], in_=ot[t][:])
+            elif kind == "o":
+                if n == "s":
+                    nc.scalar.copy(out=o16[t][:], in_=o_bank[t][:].rearrange("p (t j) -> p j t", t=PACK))
+                else:
+                    nc.vector.tensor_copy(out=o16[t][:], in_=ot[t][:].rearrange("p t j -> p j t"))
+            else:
+                nc.vector.quantize_mx(out=oc[:, blk(t)].bitcast(FP8X4), scales=osc[:, blk(t)], in_=o16[t][:].rearrange("p j t -> p (j t)"))
+
+        place = {}
+        left = {}
+        o_bank = [bank[k] for k in [2,3,0,1]]
+        oc = sb("oc", [P, S], U32)
+        osc = sb("osc", [P, S], U8)
+        out_v = out_0.rearrange("(p t) j -> p t j", t=PACK)
+        out_w = out_1[0].rearrange("p n t -> p (n t)").bitcast(I32)
+        z16 = [sb("z16_%d" % b, [P, JB, PACK], BF16) for b in range(NJB)]
+        zc = [sb("zc%d" % b, [P, JB], U32) for b in range(NJB)]
+        zs = [sb("zs%d" % b, [P, JB], U8) for b in range(NJB)]
+        ot = [sb("ot%d" % b, [P, PACK, JB], F32) for b in range(NJB)]
+        o16 = [sb("o16_%d" % b, [P, JB, PACK], BF16) for b in range(NJB)]
+
+        for item in [["by",0,[[0,0],[0,1],[0,2],[0,3]]],["by",1,[[1,0],[1,1],[1,2],[1,3]]],["by",2,[[2,0],[2,1],[2,2],[2,3]]],["by",3,[[3,0],[3,1]]],["g",0,0],["g",0,1],["add",0],["sig",0,0],["sig",0,1],["g",1,0],["g",1,1],["add",1],["sig",1,0],["sig",1,1],["m",0,0],["m",0,1],["th",0,[[0,0],[0,1],[0,2],[0,3]]],["g",2,0],["g",2,1],["add",2],["sig",2,0],["sig",2,1],["m",1,0],["m",1,1],["th",1,[[1,0],[1,1],[1,2],[1,3]]],["g",3,0],["g",3,1],["add",3],["sig",3,0,[0,2]],["sig",3,1,[0,2]],["sig",3,0,[2,3]],["sig",3,1,[2,3]],["sig",3,0,[3,4]],["sig",3,1,[3,4]],["by",0,[[3,2]]],["by",1,[[3,3]]],["m",2,0],["m",2,1],["th",2,[[2,0],[2,1],[2,2],[2,3]]],["m",3,0,[0,2]],["m",3,1,[0,2]],["th",3,[[3,0],[3,1]]],["m",3,0,[2,3]],["m",3,1,[2,3]],["th",0,[[3,2]]],["m",3,0,[3,4]],["m",3,1,[3,4]],["th",1,[[3,3]]],["gn",0],["qz",0],["gn",1],["qz",1],["gn",2],["qz",2],["gn",3],["qz",3],["o",0,"v"],["qo",0],["o",1,"v"],["qo",1],["o",2,"v"],["qo",2],["o",3,"v"],["qo",3]]:
+            step(*item)
+
+        nc.sync.dma_start(out=out_w, in_=oc[:].bitcast(I32))
+        for q in range(4):
+            nc.scalar.dma_start(out=out_2[0][4 * q : 4 * q + 4, :].bitcast(I32), in_=osc[32 * q : 32 * q + 4, :].bitcast(I32))

@@ -24,8 +24,8 @@ W1_ROW = 4
 W2_ROW = 8
 FLOPS = 2 * 2 * 512 * 512 * 512
 R1_MULT = ["fused","fused","fused","fused"]
-R1_SUM = ["v","v","v","v"]
-WARM = True
+R1_SUM = ["v","pe","v","v"]
+WARM = False
 
 
 def tile_picked_mfield_none_po_kernel(
@@ -45,20 +45,24 @@ def tile_picked_mfield_none_po_kernel(
             return dram[0].rearrange("p n t -> p (n t)").bitcast(I32)
 
         def load_scales(queue, tile, dram, q):
-            rows = dram[0][4 * q : 4 * q + 4, :].bitcast(I32)
-            queue.dma_start(out=tile[32 * q : 32 * q + 32, :].bitcast(I32), in_=rows.unsqueeze(0).to_broadcast([8, 4, rows.shape[1]]))
+            queue.dma_start(out=tile[32 * q : 32 * q + 4, :].bitcast(I32), in_=dram[0][4 * q : 4 * q + 4, :].bitcast(I32))
 
         xs = sb("xs", [P, T], U8)
         w1s = sb("w1s", [P, S], U8)
         w2s = sb("w2s", [P, S], U8)
+        for plane in (xs, w1s, w2s):
+            nc.gpsimd.memset(plane[:].bitcast(I32), 0)
         xw = sb("xw", [P, T], U32)
         w1w = sb("w1w", [P, S], I32)
         w2w = sb("w2w", [P, S], I32)
         offs_t = keep.tile([P, S // 16], U16, name="offs_t")
         p1_t = keep.tile([P, S // 16], U16, name="p1_t")
         p2_t = keep.tile([P, S // 16], U16, name="p2_t")
-        c1 = [sb("c1_%d" % t, [P, S], F32) for t in range(PACK)]
-        c2 = [sb("c2_%d" % t, [P, S], F32) for t in range(PACK)]
+        ywin = [sb("ywin%d" % t, [P, WIN], F32) for t in range(PACK)]
+        awin = [sb("awin%d" % t, [P, WIN], F32) for t in range(PACK)]
+        c2_last = sb("c2_last", [P, S], F32)
+        c1 = [awin[t][:, S:WIN] for t in range(PACK)]
+        c2 = [ywin[t + 1][:, S:WIN] for t in range(PACK - 1)] + [c2_last[:]]
         gn_t = sb("gn_t", [P, PACK], F32)
         cj1_v = cj1.rearrange("(p t) j -> p t j", t=PACK)
         cj2_v = cj2.rearrange("(p t) j -> p t j", t=PACK)
@@ -75,46 +79,41 @@ def tile_picked_mfield_none_po_kernel(
         load_scales(nc.sync, w1s, w1_scales, 2)
         load_scales(nc.sync, w1s, w1_scales, 3)
         nc.sync.dma_start(p1_t[:], p1)
-        nc.sync.dma_start(out=c1[0][:], in_=cj1_v[:, 0, :])
+        nc.sync.dma_start(out=c1[0], in_=cj1_v[:, 0, :])
         nc.sync.dma_start(p2_t[:], p2)
-        nc.sync.dma_start(out=c2[0][:], in_=cj2_v[:, 0, :])
+        nc.sync.dma_start(out=c2[0], in_=cj2_v[:, 0, :])
+        nc.sync.dma_start(out=c1[1], in_=cj1_v[:, 1, :])
+        nc.sync.dma_start(out=c2[1], in_=cj2_v[:, 1, :])
+        nc.sync.dma_start(out=c1[2], in_=cj1_v[:, 2, :])
+        nc.sync.dma_start(out=c2[2], in_=cj2_v[:, 2, :])
+        nc.sync.dma_start(out=c1[3], in_=cj1_v[:, 3, :])
+        nc.sync.dma_start(out=c2[3], in_=cj2_v[:, 3, :])
+        nc.sync.dma_start(out=gn_t[:], in_=gn.rearrange("(p t) o -> p (t o)", t=PACK))
         nc.sync.dma_start(out=w2w[:], in_=words_of(w2_words))
         load_scales(nc.sync, w2s, w2_scales, 0)
         load_scales(nc.sync, w2s, w2_scales, 1)
         load_scales(nc.sync, w2s, w2_scales, 2)
         load_scales(nc.sync, w2s, w2_scales, 3)
-        nc.sync.dma_start(out=c1[1][:], in_=cj1_v[:, 1, :])
-        nc.sync.dma_start(out=c2[1][:], in_=cj2_v[:, 1, :])
-        nc.sync.dma_start(out=c1[2][:], in_=cj1_v[:, 2, :])
-        nc.sync.dma_start(out=c2[2][:], in_=cj2_v[:, 2, :])
-        nc.sync.dma_start(out=c1[3][:], in_=cj1_v[:, 3, :])
-        nc.sync.dma_start(out=c2[3][:], in_=cj2_v[:, 3, :])
-        nc.sync.dma_start(out=gn_t[:], in_=gn.rearrange("(p t) o -> p (t o)", t=PACK))
 
         ident = sb("ident", [P, P], F32)
         make_identity(nc, ident[:])
 
-        ywin = [sb("ywin%d" % t, [P, WIN], F32) for t in range(PACK)]
-        awin = [sb("awin%d" % t, [P, WIN if t < 3 else S], F32) for t in range(PACK)]
-        for t in range(PACK):
-            nc.vector.memset(ywin[t][:, S:WIN], 0.0)
-        for t in range(3):
-            nc.vector.memset(awin[t][:, S:WIN], 0.0)
+        nc.vector.memset(ywin[0][:, S:WIN], 0.0)
         if WARM:
             warm = sb("warm", [P, 1], F32)
             nc.scalar.activation(warm[:], ywin[0][:, S : S + 1], ACT.Sigmoid)
 
-        def deal(name, words, scales):
+        def deal(name, words, scales, scale_engine):
             dw = sb(name + "_w", [P, S], I32)
             ds = sb(name + "_s", [P, S], U8)
             nc.vector.tensor_copy(out=dw[:].rearrange("p (t m) -> p t m", t=PACK), in_=words[:].rearrange("p (m t) -> p t m", t=PACK))
-            nc.vector.tensor_copy(out=ds[:].rearrange("p (t m) -> p t m", t=PACK), in_=scales[:].rearrange("p (m t) -> p t m", t=PACK))
+            scale_engine.tensor_copy(out=ds[:].rearrange("p (t m) -> p t m", t=PACK), in_=scales[:].rearrange("p (m t) -> p t m", t=PACK))
             return dw, ds
 
         xsg = sb("xsg", [P, S], U8)
         xg = sb("xg", [P, S], U32)
         nc.vector.tensor_copy(out=xsg[:], in_=xs[:].indirect(offs_t[:]))
-        w1dw, w1ds = deal("w1d", w1w, w1s)
+        w1dw, w1ds = deal("w1d", w1w, w1s, nc.gpsimd)
         nc.vector.tensor_copy(out=xg[:], in_=xw[:].indirect(offs_t[:]))
 
         for t in range(PACK):
@@ -124,7 +123,7 @@ def tile_picked_mfield_none_po_kernel(
                 rhs=xg[:].bitcast(FP8X4), rhs_scale=xsg[:], start=True, stop=True,
             )
             nc.scalar.activation(ywin[t][:, 0:S], bank[t][:], ACT.Copy, scale=0.5)
-        w2dw, w2ds = deal("w2d", w2w, w2s)
+        dealt = []
 
         lists = (p1_t, p2_t)
         cj = (c1, c2)
@@ -135,7 +134,7 @@ def tile_picked_mfield_none_po_kernel(
         at = [sb("at%d" % t, [P, S], F32) for t in range(PACK)]
         tt = [sb("tt%d" % t, [P, S], F32) for t in range(PACK)]
         zb = [psum.tile([P, PACK, JB], F32, name="zb%d" % b) for b in range(NJB)]
-        a_bank = [bank[k] for k in [0,0,0,0]]
+        a_bank = [bank[k] for k in [0,1,2,0]]
         b_bank = [bank[k] for k in [0,0,0,0]]
 
         def blk(b):
@@ -157,17 +156,20 @@ def tile_picked_mfield_none_po_kernel(
         def step(kind, t, n=0, h=(0, 4)):
             if kind == "g":
                 if R1_MULT[t] == "fused":
-                    nc.vector.tensor_tensor(out=g[t][n][:], in0=ywin[t][:].indirect(lists[n][:]), in1=cj[n][t][:], op=ALU.mult)
+                    nc.vector.tensor_tensor(out=g[t][n][:], in0=ywin[t][:].indirect(lists[n][:]), in1=cj[n][t], op=ALU.mult)
                 else:
                     nc.vector.tensor_copy(out=got[t][n][:], in_=ywin[t][:].indirect(lists[n][:]))
-                    nc.gpsimd.tensor_tensor(out=g[t][n][:], in0=got[t][n][:], in1=cj[n][t][:], op=ALU.mult)
+                    nc.gpsimd.tensor_tensor(out=g[t][n][:], in0=got[t][n][:], in1=cj[n][t], op=ALU.mult)
                 if R1_SUM[t] == "pe":
                     if n == 0:
                         turn(a_bank[t], ywin[t], True, False)
                     turn(a_bank[t], g[t][n], False, n == 1)
             elif kind == "add":
-                nc.vector.tensor_tensor(out=at[t][:], in0=g[t][0][:], in1=ywin[t][:, 0:S], op=ALU.add)
-                nc.vector.tensor_tensor(out=awin[t][:, 0:S], in0=at[t][:], in1=g[t][1][:], op=ALU.add)
+                halves = (slice(0, S // 2), slice(S // 2, S))
+                for js in halves:
+                    nc.vector.tensor_tensor(out=at[t][:, js], in0=g[t][0][:, js], in1=ywin[t][:, js], op=ALU.add)
+                for js in halves:
+                    nc.vector.tensor_tensor(out=awin[t][:, js], in0=at[t][:, js], in1=g[t][1][:, js], op=ALU.add)
             elif kind == "at":
                 exit_copy(n, at[t][:], a_bank[t][:])
                 for b in range(NJB):
@@ -196,6 +198,8 @@ def tile_picked_mfield_none_po_kernel(
                 nc.scalar.activation(tanh_t[:], bank[t][:, 0:width], ACT.Tanh, scale=2.0)
                 for k, (tl, b) in enumerate(n):
                     nc.tensor.transpose(zb[b][:, tl, :], tanh_t[:, blk(k)], ident[:])
+            elif kind == "deal":
+                dealt.extend(deal("w2d", w2w, w2s, nc.vector))
             elif kind == "gn":
                 nc.vector.tensor_tensor(
                     out=z16[t][:], in0=zb[t][:].rearrange("p t j -> p j t"),
@@ -206,7 +210,7 @@ def tile_picked_mfield_none_po_kernel(
                 ob = o_bank[t][:].rearrange("p (t j) -> p t j", t=PACK)
                 for k in range(PACK):
                     nc.tensor.matmul_mx(
-                        out=ob[:, k, :], lhsT=w2dw[:, blk(k)].bitcast(FP8X4), lhsT_scale=w2ds[:, blk(k)],
+                        out=ob[:, k, :], lhsT=dealt[0][:, blk(k)].bitcast(FP8X4), lhsT_scale=dealt[1][:, blk(k)],
                         rhs=zc[t][:].bitcast(FP8X4), rhs_scale=zs[t][:], start=True, stop=True,
                     )
                 nc.scalar.copy(out=ot[t][:], in_=ob)
@@ -218,10 +222,13 @@ def tile_picked_mfield_none_po_kernel(
                     nc.vector.tensor_copy(out=o16[t][:], in_=ot[t][:].rearrange("p t j -> p j t"))
             else:
                 nc.vector.quantize_mx(out=oc[:, blk(t)].bitcast(FP8X4), scales=osc[:, blk(t)], in_=o16[t][:].rearrange("p j t -> p (j t)"))
+                if t % 2 == 1:
+                    js = slice((t - 1) * JB, (t + 1) * JB)
+                    nc.sync.dma_start(out=out_w[:, js], in_=oc[:, js].bitcast(I32))
 
         place = {}
         left = {}
-        o_bank = [bank[k] for k in [2,3,0,1]]
+        o_bank = [bank[k] for k in [2,1,0,3]]
         oc = sb("oc", [P, S], U32)
         osc = sb("osc", [P, S], U8)
         out_v = out_0.rearrange("(p t) j -> p t j", t=PACK)
@@ -232,9 +239,8 @@ def tile_picked_mfield_none_po_kernel(
         ot = [sb("ot%d" % b, [P, PACK, JB], F32) for b in range(NJB)]
         o16 = [sb("o16_%d" % b, [P, JB, PACK], BF16) for b in range(NJB)]
 
-        for item in [["by",0,[[0,0],[0,1],[0,2],[0,3]]],["by",1,[[1,0],[1,1],[1,2],[1,3]]],["by",2,[[2,0],[2,1],[2,2],[2,3]]],["by",3,[[3,0],[3,1]]],["g",0,0],["g",0,1],["add",0],["sig",0,0],["sig",0,1],["g",1,0],["g",1,1],["add",1],["sig",1,0],["sig",1,1],["m",0,0],["m",0,1],["th",0,[[0,0],[0,1],[0,2],[0,3]]],["g",2,0],["g",2,1],["add",2],["sig",2,0],["sig",2,1],["m",1,0],["m",1,1],["th",1,[[1,0],[1,1],[1,2],[1,3]]],["g",3,0],["g",3,1],["add",3],["sig",3,0,[0,2]],["sig",3,1,[0,2]],["sig",3,0,[2,3]],["sig",3,1,[2,3]],["sig",3,0,[3,4]],["sig",3,1,[3,4]],["by",0,[[3,2]]],["by",1,[[3,3]]],["m",2,0],["m",2,1],["th",2,[[2,0],[2,1],[2,2],[2,3]]],["m",3,0,[0,2]],["m",3,1,[0,2]],["th",3,[[3,0],[3,1]]],["m",3,0,[2,3]],["m",3,1,[2,3]],["th",0,[[3,2]]],["m",3,0,[3,4]],["m",3,1,[3,4]],["th",1,[[3,3]]],["gn",0],["qz",0],["gn",1],["qz",1],["gn",2],["qz",2],["gn",3],["qz",3],["o",0,"v"],["qo",0],["o",1,"v"],["qo",1],["o",2,"v"],["qo",2],["o",3,"v"],["qo",3]]:
+        for item in [["by",0,[[0,0],[0,1],[0,2],[0,3]]],["by",2,[[1,0],[1,1],[2,0],[2,1]]],["by",3,[[3,2],[3,3]]],["g",0,0],["g",0,1],["add",0],["sig",0,0],["sig",0,1],["g",1,0],["g",1,1],["at",1,"s"],["ab",1,"s"],["by",1,[[3,0],[3,1]]],["sig",1,0],["sig",1,1],["g",2,0],["g",2,1],["m",0,0],["m",0,1],["add",2],["th",0,[[0,0],[0,1],[0,2],[0,3]]],["by",0,[[1,2],[1,3],[2,2],[2,3]]],["sig",2,0],["sig",2,1],["g",3,0],["g",3,1],["add",3],["sig",3,0,[0,2]],["sig",3,1,[0,2]],["m",1,0,[0,2]],["m",1,1,[0,2]],["m",2,0,[0,2]],["m",2,1,[0,2]],["th",2,[[1,0],[1,1],[2,0],[2,1]]],["sig",3,0,[2,4]],["sig",3,1,[2,4]],["m",3,0,[0,2]],["m",3,1,[0,2]],["th",1,[[3,0],[3,1]]],["m",1,0,[2,4]],["m",1,1,[2,4]],["m",2,0,[2,4]],["m",2,1,[2,4]],["th",0,[[1,2],[1,3],[2,2],[2,3]]],["m",3,0,[2,4]],["m",3,1,[2,4]],["th",3,[[3,2],[3,3]]],["deal",0],["gn",0],["qz",0],["gn",1],["qz",1],["gn",2],["qz",2],["gn",3],["qz",3],["o",0,"v"],["qo",0],["o",1,"v"],["qo",1],["o",2,"v"],["qo",2],["o",3,"v"],["qo",3]]:
             step(*item)
 
-        nc.sync.dma_start(out=out_w, in_=oc[:].bitcast(I32))
         for q in range(4):
-            nc.scalar.dma_start(out=out_2[0][4 * q : 4 * q + 4, :].bitcast(I32), in_=osc[32 * q : 32 * q + 4, :].bitcast(I32))
+            (nc.scalar if q < 3 else nc.sync).dma_start(out=out_2[0][4 * q : 4 * q + 4, :].bitcast(I32), in_=osc[32 * q : 32 * q + 4, :].bitcast(I32))

@@ -25,6 +25,7 @@ W2_ROW = 8
 FLOPS = 2 * 2 * 512 * 512 * 512
 R1_MULT = ["fused","fused","fused","fused"]
 R1_SUM = ["v","pe","v","v"]
+SIG_HOME = {(3, 1, 2): (2, 1, -2)}
 WARM = False
 
 
@@ -114,9 +115,19 @@ def tile_picked_mfield_none_po_kernel(
         xg = sb("xg", [P, S], U32)
         nc.vector.tensor_copy(out=xsg[:], in_=xs[:].indirect(offs_t[:]))
         w1dw, w1ds = deal("w1d", w1w, w1s, nc.gpsimd)
-        nc.vector.tensor_copy(out=xg[:], in_=xw[:].indirect(offs_t[:]))
+        zb = [psum.tile([P, PACK, JB], F32, name="zb%d" % b) for b in range(NJB)]
+        half = S // 2
+        for k in range(2):
+            nc.vector.tensor_copy(out=xg[:, k * half : (k + 1) * half], in_=xw[:].indirect(offs_t[:, k * 16 : (k + 1) * 16]))
+        for k, dst in enumerate((zb[0][:].rearrange("p t j -> p (t j)"), bank[0][:])):
+            js = slice(k * half, (k + 1) * half)
+            nc.tensor.matmul_mx(
+                out=dst[:, 0:half], lhsT=w1dw[:, 0:P].bitcast(FP8X4), lhsT_scale=w1ds[:, 0:P],
+                rhs=xg[:, js].bitcast(FP8X4), rhs_scale=xsg[:, js], start=True, stop=True,
+            )
+            nc.scalar.activation(ywin[0][:, js], dst[:, 0:half], ACT.Copy, scale=0.5)
 
-        for t in range(PACK):
+        for t in range(1, PACK):
             cols = slice(t * P, (t + 1) * P)
             nc.tensor.matmul_mx(
                 out=bank[t][:], lhsT=w1dw[:, cols].bitcast(FP8X4), lhsT_scale=w1ds[:, cols],
@@ -133,12 +144,17 @@ def tile_picked_mfield_none_po_kernel(
         m = [[sb("m%d_%d" % (t, n), [P, S], F32) for n in range(2)] for t in range(PACK)]
         at = [sb("at%d" % t, [P, S], F32) for t in range(PACK)]
         tt = [sb("tt%d" % t, [P, S], F32) for t in range(PACK)]
-        zb = [psum.tile([P, PACK, JB], F32, name="zb%d" % b) for b in range(NJB)]
         a_bank = [bank[k] for k in [0,1,2,0]]
         b_bank = [bank[k] for k in [0,0,0,0]]
 
         def blk(b):
             return slice(b * JB, (b + 1) * JB)
+
+        def sig_at(t, n, b0, b1):
+            if (t, n, b0) in SIG_HOME:
+                t2, n2, shift = SIG_HOME[(t, n, b0)]
+                return m[t2][n2][:, (b0 + shift) * JB : (b1 + shift) * JB]
+            return sig[t][n][:, b0 * JB : b1 * JB]
 
         def turn(dst, term, first, last):
             for b in range(NJB):
@@ -178,7 +194,7 @@ def tile_picked_mfield_none_po_kernel(
                 exit_copy(n, awin[t][:, 0:S], a_bank[t][:])
             elif kind == "sig":
                 b0, b1 = h
-                nc.scalar.activation(sig[t][n][:, b0 * JB : b1 * JB], awin[t][:].indirect(lists[n][:, b0 * 8 : b1 * 8]), ACT.Sigmoid, scale=4.0)
+                nc.scalar.activation(sig_at(t, n, b0, b1), awin[t][:].indirect(lists[n][:, b0 * 8 : b1 * 8]), ACT.Sigmoid, scale=4.0)
             elif kind == "by":
                 for k, (tl, b) in enumerate(n):
                     nc.tensor.matmul(out=bank[t][:, blk(k)], lhsT=ywin[tl][:, blk(b)], rhs=ident[:], is_transpose=True, start=(k == 0), stop=False)
@@ -187,7 +203,7 @@ def tile_picked_mfield_none_po_kernel(
             elif kind == "m":
                 b0, b1 = h
                 js = slice(b0 * JB, b1 * JB)
-                nc.vector.scalar_tensor_tensor(out=m[t][n][:, js], in0=sig[t][n][:, js], scalar=-0.5, in1=cj[n][t][:, js], op0=ALU.add, op1=ALU.mult)
+                nc.vector.scalar_tensor_tensor(out=m[t][n][:, js], in0=sig_at(t, n, b0, b1), scalar=-0.5, in1=cj[n][t][:, js], op0=ALU.add, op1=ALU.mult)
                 for b in range(b0, b1):
                     bk, k = place[(t, b)]
                     left[bk] = left[bk] - 1
@@ -200,6 +216,12 @@ def tile_picked_mfield_none_po_kernel(
                     nc.tensor.transpose(zb[b][:, tl, :], tanh_t[:, blk(k)], ident[:])
             elif kind == "deal":
                 dealt.extend(deal("w2d", w2w, w2s, nc.vector))
+            elif kind == "heat":
+                for k in range(2):
+                    nc.tensor.matmul_mx(
+                        out=bank[t][:], lhsT=w1dw[:, 0:P].bitcast(FP8X4), lhsT_scale=w1ds[:, 0:P],
+                        rhs=xg[:].bitcast(FP8X4), rhs_scale=xsg[:], start=True, stop=True,
+                    )
             elif kind == "gn":
                 nc.vector.tensor_tensor(
                     out=z16[t][:], in0=zb[t][:].rearrange("p t j -> p j t"),
@@ -217,14 +239,13 @@ def tile_picked_mfield_none_po_kernel(
                 nc.sync.dma_start(out=out_v[:, :, blk(t)], in_=ot[t][:])
             elif kind == "o":
                 if n == "s":
-                    nc.scalar.copy(out=o16[t][:], in_=o_bank[t][:].rearrange("p (t j) -> p j t", t=PACK))
+                    nc.scalar.copy(out=o16[t], in_=o_bank[t][:].rearrange("p (t j) -> p j t", t=PACK))
                 else:
-                    nc.vector.tensor_copy(out=o16[t][:], in_=ot[t][:].rearrange("p t j -> p j t"))
+                    nc.vector.tensor_copy(out=o16[t], in_=ot[t][:].rearrange("p t j -> p j t"))
             else:
-                nc.vector.quantize_mx(out=oc[:, blk(t)].bitcast(FP8X4), scales=osc[:, blk(t)], in_=o16[t][:].rearrange("p j t -> p (j t)"))
-                if t % 2 == 1:
-                    js = slice((t - 1) * JB, (t + 1) * JB)
-                    nc.sync.dma_start(out=out_w[:, js], in_=oc[:, js].bitcast(I32))
+                js = slice(2 * t * JB, 2 * (t + 1) * JB)
+                nc.vector.quantize_mx(out=oc[:, js].bitcast(FP8X4), scales=osc[:, js], in_=o16_pair[t][:].rearrange("p j t -> p (j t)"))
+                nc.sync.dma_start(out=out_w[:, js], in_=oc[:, js].bitcast(I32))
 
         place = {}
         left = {}
@@ -237,9 +258,10 @@ def tile_picked_mfield_none_po_kernel(
         zc = [sb("zc%d" % b, [P, JB], U32) for b in range(NJB)]
         zs = [sb("zs%d" % b, [P, JB], U8) for b in range(NJB)]
         ot = [sb("ot%d" % b, [P, PACK, JB], F32) for b in range(NJB)]
-        o16 = [sb("o16_%d" % b, [P, JB, PACK], BF16) for b in range(NJB)]
+        o16_pair = [sb("o16_%d" % k, [P, 2 * JB, PACK], BF16) for k in range(2)]
+        o16 = [o16_pair[b // 2][:, (b % 2) * JB : (b % 2 + 1) * JB, :] for b in range(NJB)]
 
-        for item in [["by",0,[[0,0],[0,1],[0,2],[0,3]]],["by",2,[[1,0],[1,1],[2,0],[2,1]]],["by",3,[[3,2],[3,3]]],["g",0,0],["g",0,1],["add",0],["sig",0,0],["sig",0,1],["g",1,0],["g",1,1],["at",1,"s"],["ab",1,"s"],["by",1,[[3,0],[3,1]]],["sig",1,0],["sig",1,1],["g",2,0],["g",2,1],["m",0,0],["m",0,1],["add",2],["th",0,[[0,0],[0,1],[0,2],[0,3]]],["by",0,[[1,2],[1,3],[2,2],[2,3]]],["sig",2,0],["sig",2,1],["g",3,0],["g",3,1],["add",3],["sig",3,0,[0,2]],["sig",3,1,[0,2]],["m",1,0,[0,2]],["m",1,1,[0,2]],["m",2,0,[0,2]],["m",2,1,[0,2]],["th",2,[[1,0],[1,1],[2,0],[2,1]]],["sig",3,0,[2,4]],["sig",3,1,[2,4]],["m",3,0,[0,2]],["m",3,1,[0,2]],["th",1,[[3,0],[3,1]]],["m",1,0,[2,4]],["m",1,1,[2,4]],["m",2,0,[2,4]],["m",2,1,[2,4]],["th",0,[[1,2],[1,3],[2,2],[2,3]]],["m",3,0,[2,4]],["m",3,1,[2,4]],["th",3,[[3,2],[3,3]]],["deal",0],["gn",0],["qz",0],["gn",1],["qz",1],["gn",2],["qz",2],["gn",3],["qz",3],["o",0,"v"],["qo",0],["o",1,"v"],["qo",1],["o",2,"v"],["qo",2],["o",3,"v"],["qo",3]]:
+        for item in [["by",0,[[0,0],[0,1],[0,2],[0,3]]],["by",2,[[1,0],[1,1],[2,0],[2,1]]],["by",3,[[3,2],[3,3]]],["g",0,0],["g",0,1],["add",0],["sig",0,0],["sig",0,1],["g",1,0],["g",1,1],["at",1,"s"],["ab",1,"s"],["by",1,[[3,0],[3,1]]],["sig",1,0],["sig",1,1],["g",2,0],["g",2,1],["m",0,0],["m",0,1],["add",2],["th",0,[[0,0],[0,1],[0,2],[0,3]]],["by",0,[[1,2],[1,3],[2,2],[2,3]]],["sig",2,0],["sig",2,1],["g",3,0],["g",3,1],["add",3],["sig",3,0,[0,2]],["sig",3,1,[0,2]],["m",1,0,[0,2]],["m",1,1,[0,2]],["m",2,0,[0,2]],["m",2,1,[0,2]],["th",2,[[1,0],[1,1],[2,0],[2,1]]],["sig",3,0,[2,4]],["sig",3,1,[2,4]],["m",3,0,[0,2]],["m",3,1,[0,2]],["th",1,[[3,0],[3,1]]],["m",1,0,[2,4]],["m",1,1,[2,4]],["m",2,0,[2,4]],["m",2,1,[2,4]],["th",0,[[1,2],[1,3],[2,2],[2,3]]],["m",3,0,[2,4]],["m",3,1,[2,4]],["th",3,[[3,2],[3,3]]],["deal",0],["gn",0],["qz",0],["gn",1],["qz",1],["gn",2],["qz",2],["gn",3],["qz",3],["o",0,"v"],["o",1,"v"],["qo",0],["o",2,"v"],["o",3,"v"],["qo",1]]:
             step(*item)
 
         for q in range(4):

@@ -261,7 +261,7 @@ def tile_picked_mfield_none_po_kernel(
         o16_pair = [sb("o16_%d" % k, [P, 2 * JB, PACK], BF16) for k in range(2)]
         o16 = [o16_pair[b // 2][:, (b % 2) * JB : (b % 2 + 1) * JB, :] for b in range(NJB)]
 
-        for item in [["by",0,[[0,0],[0,1],[0,2],[0,3]]],["by",2,[[1,0],[1,1],[2,0],[2,1]]],["by",3,[[3,2],[3,3]]],["g",0,0],["g",0,1],["add",0],["sig",0,0],["sig",0,1],["g",1,0],["g",1,1],["at",1,"s"],["ab",1,"s"],["by",1,[[3,0],[3,1]]],["sig",1,0],["sig",1,1],["g",2,0],["g",2,1],["m",0,0],["m",0,1],["add",2],["th",0,[[0,0],[0,1],[0,2],[0,3]]],["by",0,[[1,2],[1,3],[2,2],[2,3]]],["sig",2,0],["sig",2,1],["g",3,0],["g",3,1],["add",3],["sig",3,0,[0,2]],["sig",3,1,[0,2]],["m",1,0,[0,2]],["m",1,1,[0,2]],["m",2,0,[0,2]],["m",2,1,[0,2]],["th",2,[[1,0],[1,1],[2,0],[2,1]]],["sig",3,0,[2,4]],["sig",3,1,[2,4]],["m",3,0,[0,2]],["m",3,1,[0,2]],["th",1,[[3,0],[3,1]]],["m",1,0,[2,4]],["m",1,1,[2,4]],["m",2,0,[2,4]],["m",2,1,[2,4]],["th",0,[[1,2],[1,3],[2,2],[2,3]]],["m",3,0,[2,4]],["m",3,1,[2,4]],["th",3,[[3,2],[3,3]]],["deal",0],["gn",0],["qz",0],["gn",1],["qz",1],["gn",2],["qz",2],["gn",3],["qz",3],["o",0,"v"],["o",1,"v"],["qo",0],["o",2,"v"],["o",3,"v"],["qo",1]]:
+        for item in [["by",0,[[0,0],[0,1],[0,2],[0,3]]],["by",2,[[1,0],[1,1],[2,0],[2,1]]],["by",3,[[3,2],[3,3]]],["g",0,0],["g",0,1],["add",0],["sig",0,0],["sig",0,1],["g",1,0],["g",1,1],["at",1,"s"],["ab",1,"s"],["by",1,[[3,0],[3,1]]],["sig",1,0],["sig",1,1],["g",2,0],["g",2,1],["m",0,0],["m",0,1],["add",2],["th",0,[[0,0],[0,1],[0,2],[0,3]]],["heat",0],["by",0,[[1,2],[1,3],[2,2],[2,3]]],["sig",2,0],["sig",2,1],["g",3,0],["g",3,1],["add",3],["sig",3,0,[0,2]],["sig",3,1,[0,2]],["m",1,0,[0,2]],["m",1,1,[0,2]],["m",2,0,[0,2]],["m",2,1,[0,2]],["th",2,[[1,0],[1,1],[2,0],[2,1]]],["sig",3,0,[2,4]],["sig",3,1,[2,4]],["m",3,0,[0,2]],["m",3,1,[0,2]],["th",1,[[3,0],[3,1]]],["m",1,0,[2,4]],["m",1,1,[2,4]],["m",2,0,[2,4]],["m",2,1,[2,4]],["th",0,[[1,2],[1,3],[2,2],[2,3]]],["m",3,0,[2,4]],["m",3,1,[2,4]],["th",3,[[3,2],[3,3]]],["deal",0],["gn",0],["qz",0],["gn",1],["qz",1],["gn",2],["qz",2],["gn",3],["qz",3],["o",0,"v"],["o",1,"v"],["qo",0],["o",2,"v"],["o",3,"v"],["qo",1]]:
             step(*item)
 
         for q in range(4):

@@ -19,14 +19,15 @@ S = 512
 PACK = 4
 JB = 128
 NJB = S // JB
-WIN = 2 * S
-W1_ROW = 4
-W2_ROW = 8
+HALF = S // 2
+SUM = {1: (4, 5), 2: (1, 2)}
+BACK = {1: (6, 7), 2: (1, 2)}
+GROUPS = [(0, [(0, 0), (0, 1), (0, 2), (0, 3)]), (3, [(1, 0), (1, 1), (1, 2), (1, 3)]), (0, [(2, 0), (2, 1), (3, 0), (3, 1)]), (1, [(2, 2), (2, 3), (3, 2), (3, 3)])]
+ZB = (4, 5, 6, 7)
+OB = (2, 3, 0, 1)
+V_PLANES = (3,)
 FLOPS = 2 * 2 * 512 * 512 * 512
-R1_MULT = ["fused","fused","fused","fused"]
-R1_SUM = ["v","pe","v","v"]
-SIG_HOME = {(3, 1, 2): (2, 1, -2)}
-WARM = False
+PE_PLANES = (1, 2)
 
 
 def tile_picked_mfield_none_po_kernel(
@@ -40,7 +41,16 @@ def tile_picked_mfield_none_po_kernel(
         def sb(name, shape, dtype):
             return keep.tile(shape, dtype, name=name, align_bytes=64)
 
-        bank = [psum.tile([P, S], F32, name="bank%d" % k) for k in range(4)]
+        bank = [psum.tile([P, S], F32, name="bank%d" % k) for k in range(8)]
+
+        def blk(b):
+            return slice(b * JB, (b + 1) * JB)
+
+        def half(h):
+            return slice(h * HALF, (h + 1) * HALF)
+
+        def entries(h):
+            return slice(h * HALF // 16, (h + 1) * HALF // 16)
 
         def words_of(dram):
             return dram[0].rearrange("p n t -> p (n t)").bitcast(I32)
@@ -59,55 +69,41 @@ def tile_picked_mfield_none_po_kernel(
         offs_t = keep.tile([P, S // 16], U16, name="offs_t")
         p1_t = keep.tile([P, S // 16], U16, name="p1_t")
         p2_t = keep.tile([P, S // 16], U16, name="p2_t")
-        ywin = [sb("ywin%d" % t, [P, WIN], F32) for t in range(PACK)]
-        awin = [sb("awin%d" % t, [P, WIN], F32) for t in range(PACK)]
-        c2_last = sb("c2_last", [P, S], F32)
-        c1 = [awin[t][:, S:WIN] for t in range(PACK)]
-        c2 = [ywin[t + 1][:, S:WIN] for t in range(PACK - 1)] + [c2_last[:]]
+        lists = (p1_t, p2_t)
+        cpl = [sb("cpl%d" % t, [P, 2, S], F32) for t in range(PACK)]
         gn_t = sb("gn_t", [P, PACK], F32)
-        cj1_v = cj1.rearrange("(p t) j -> p t j", t=PACK)
-        cj2_v = cj2.rearrange("(p t) j -> p t j", t=PACK)
+        cj_v = [c.rearrange("(p t) j -> p t j", t=PACK) for c in (cj1, cj2)]
 
         nc.sync.dma_start(offs_t[:], offs)
-        load_scales(nc.sync, xs, x_scales, 0)
-        load_scales(nc.sync, xs, x_scales, 1)
-        load_scales(nc.sync, xs, x_scales, 2)
-        load_scales(nc.sync, xs, x_scales, 3)
+        for q in range(4):
+            load_scales(nc.sync, xs, x_scales, q)
         nc.sync.dma_start(out=w1w[:], in_=words_of(w1_words))
         load_scales(nc.sync, w1s, w1_scales, 0)
         nc.sync.dma_start(out=xw[:].bitcast(I32), in_=words_of(x_words))
-        load_scales(nc.sync, w1s, w1_scales, 1)
-        load_scales(nc.sync, w1s, w1_scales, 2)
-        load_scales(nc.sync, w1s, w1_scales, 3)
+        for q in range(1, 4):
+            load_scales(nc.sync, w1s, w1_scales, q)
         nc.sync.dma_start(p1_t[:], p1)
-        nc.sync.dma_start(out=c1[0], in_=cj1_v[:, 0, :])
+        nc.sync.dma_start(out=cpl[0][:, 0, :], in_=cj_v[0][:, 0, :])
         nc.sync.dma_start(p2_t[:], p2)
-        nc.sync.dma_start(out=c2[0], in_=cj2_v[:, 0, :])
-        nc.sync.dma_start(out=c1[1], in_=cj1_v[:, 1, :])
-        nc.sync.dma_start(out=c2[1], in_=cj2_v[:, 1, :])
-        nc.sync.dma_start(out=c1[2], in_=cj1_v[:, 2, :])
-        nc.sync.dma_start(out=c2[2], in_=cj2_v[:, 2, :])
-        nc.sync.dma_start(out=c1[3], in_=cj1_v[:, 3, :])
-        nc.sync.dma_start(out=c2[3], in_=cj2_v[:, 3, :])
+        nc.sync.dma_start(out=cpl[0][:, 1, :], in_=cj_v[1][:, 0, :])
+        for t in range(1, PACK):
+            for n in range(2):
+                nc.sync.dma_start(out=cpl[t][:, n, :], in_=cj_v[n][:, t, :])
         nc.sync.dma_start(out=gn_t[:], in_=gn.rearrange("(p t) o -> p (t o)", t=PACK))
         nc.sync.dma_start(out=w2w[:], in_=words_of(w2_words))
-        load_scales(nc.sync, w2s, w2_scales, 0)
-        load_scales(nc.sync, w2s, w2_scales, 1)
-        load_scales(nc.sync, w2s, w2_scales, 2)
-        load_scales(nc.sync, w2s, w2_scales, 3)
+        for q in range(4):
+            load_scales(nc.sync, w2s, w2_scales, q)
 
         ident = sb("ident", [P, P], F32)
         make_identity(nc, ident[:])
 
-        nc.vector.memset(ywin[0][:, S:WIN], 0.0)
-        if WARM:
-            warm = sb("warm", [P, 1], F32)
-            nc.scalar.activation(warm[:], ywin[0][:, S : S + 1], ACT.Sigmoid)
+        warm = sb("warm", [P, 1], F32)
+        nc.scalar.activation(warm[:], ident[:, 0:1], ACT.Sigmoid)
 
         def deal(name, words, scales, scale_engine):
             dw = sb(name + "_w", [P, S], I32)
             ds = sb(name + "_s", [P, S], U8)
-            nc.vector.tensor_copy(out=dw[:].rearrange("p (t m) -> p t m", t=PACK), in_=words[:].rearrange("p (m t) -> p t m", t=PACK))
+            nc.vector.tensor_copy(out=dw[:].rearrange("p (t c i) -> p c t i", t=PACK, i=4), in_=words[:].rearrange("p (c i t) -> p c t i", t=PACK, i=4))
             scale_engine.tensor_copy(out=ds[:].rearrange("p (t m) -> p t m", t=PACK), in_=scales[:].rearrange("p (m t) -> p t m", t=PACK))
             return dw, ds
 
@@ -115,154 +111,200 @@ def tile_picked_mfield_none_po_kernel(
         xg = sb("xg", [P, S], U32)
         nc.vector.tensor_copy(out=xsg[:], in_=xs[:].indirect(offs_t[:]))
         w1dw, w1ds = deal("w1d", w1w, w1s, nc.gpsimd)
-        zb = [psum.tile([P, PACK, JB], F32, name="zb%d" % b) for b in range(NJB)]
-        half = S // 2
-        for k in range(2):
-            nc.vector.tensor_copy(out=xg[:, k * half : (k + 1) * half], in_=xw[:].indirect(offs_t[:, k * 16 : (k + 1) * 16]))
-        for k, dst in enumerate((zb[0][:].rearrange("p t j -> p (t j)"), bank[0][:])):
-            js = slice(k * half, (k + 1) * half)
+        for h in range(2):
+            nc.vector.tensor_copy(out=xg[:, half(h)], in_=xw[:].indirect(offs_t[:, entries(h)]))
+
+        y = [sb("y%d" % t, [P, S], F32) for t in range(PACK)]
+
+        def first_product(t, dst, js):
             nc.tensor.matmul_mx(
-                out=dst[:, 0:half], lhsT=w1dw[:, 0:P].bitcast(FP8X4), lhsT_scale=w1ds[:, 0:P],
+                out=dst, lhsT=w1dw[:, blk(t)].bitcast(FP8X4), lhsT_scale=w1ds[:, blk(t)],
                 rhs=xg[:, js].bitcast(FP8X4), rhs_scale=xsg[:, js], start=True, stop=True,
             )
-            nc.scalar.activation(ywin[0][:, js], dst[:, 0:half], ACT.Copy, scale=0.5)
+            nc.scalar.activation(y[t][:, js], dst, ACT.Copy, scale=(1.0 if t in V_PLANES else 0.5))
 
+        for h in range(2):
+            first_product(0, bank[(4, 5, 6, 7, 3)[h]][:, 0:HALF], half(h))
         for t in range(1, PACK):
-            cols = slice(t * P, (t + 1) * P)
-            nc.tensor.matmul_mx(
-                out=bank[t][:], lhsT=w1dw[:, cols].bitcast(FP8X4), lhsT_scale=w1ds[:, cols],
-                rhs=xg[:].bitcast(FP8X4), rhs_scale=xsg[:], start=True, stop=True,
-            )
-            nc.scalar.activation(ywin[t][:, 0:S], bank[t][:], ACT.Copy, scale=0.5)
-        dealt = []
+            first_product(t, bank[(4, 5, 6, 7, 3)[t + 1]][:], slice(0, S))
 
-        lists = (p1_t, p2_t)
-        cj = (c1, c2)
         g = [[sb("g%d_%d" % (t, n), [P, S], F32) for n in range(2)] for t in range(PACK)]
-        got = [[sb("got%d_%d" % (t, n), [P, S], F32) for n in range(2)] for t in range(PACK)]
-        sig = [[sb("sig%d_%d" % (t, n), [P, S], F32) for n in range(2)] for t in range(PACK)]
-        m = [[sb("m%d_%d" % (t, n), [P, S], F32) for n in range(2)] for t in range(PACK)]
-        at = [sb("at%d" % t, [P, S], F32) for t in range(PACK)]
-        tt = [sb("tt%d" % t, [P, S], F32) for t in range(PACK)]
-        a_bank = [bank[k] for k in [0,1,2,0]]
-        b_bank = [bank[k] for k in [0,0,0,0]]
-
-        def blk(b):
-            return slice(b * JB, (b + 1) * JB)
-
-        def sig_at(t, n, b0, b1):
-            if (t, n, b0) in SIG_HOME:
-                t2, n2, shift = SIG_HOME[(t, n, b0)]
-                return m[t2][n2][:, (b0 + shift) * JB : (b1 + shift) * JB]
-            return sig[t][n][:, b0 * JB : b1 * JB]
-
-        def turn(dst, term, first, last):
-            for b in range(NJB):
-                nc.tensor.matmul(
-                    out=dst[:, blk(b)], lhsT=term[:, blk(b)], rhs=ident[:], is_transpose=True,
-                    start=(first and b == 0), stop=(last and b == NJB - 1),
-                )
-
-        def exit_copy(engine, out, in_):
-            if engine == "s":
-                nc.scalar.copy(out=out, in_=in_)
-            else:
-                nc.vector.tensor_copy(out=out, in_=in_)
-
-        def step(kind, t, n=0, h=(0, 4)):
-            if kind == "g":
-                if R1_MULT[t] == "fused":
-                    nc.vector.tensor_tensor(out=g[t][n][:], in0=ywin[t][:].indirect(lists[n][:]), in1=cj[n][t], op=ALU.mult)
-                else:
-                    nc.vector.tensor_copy(out=got[t][n][:], in_=ywin[t][:].indirect(lists[n][:]))
-                    nc.gpsimd.tensor_tensor(out=g[t][n][:], in0=got[t][n][:], in1=cj[n][t], op=ALU.mult)
-                if R1_SUM[t] == "pe":
-                    if n == 0:
-                        turn(a_bank[t], ywin[t], True, False)
-                    turn(a_bank[t], g[t][n], False, n == 1)
-            elif kind == "add":
-                halves = (slice(0, S // 2), slice(S // 2, S))
-                for js in halves:
-                    nc.vector.tensor_tensor(out=at[t][:, js], in0=g[t][0][:, js], in1=ywin[t][:, js], op=ALU.add)
-                for js in halves:
-                    nc.vector.tensor_tensor(out=awin[t][:, js], in0=at[t][:, js], in1=g[t][1][:, js], op=ALU.add)
-            elif kind == "at":
-                exit_copy(n, at[t][:], a_bank[t][:])
-                for b in range(NJB):
-                    nc.tensor.transpose(a_bank[t][:, blk(b)], at[t][:, blk(b)], ident[:])
-            elif kind == "ab":
-                exit_copy(n, awin[t][:, 0:S], a_bank[t][:])
-            elif kind == "sig":
-                b0, b1 = h
-                nc.scalar.activation(sig_at(t, n, b0, b1), awin[t][:].indirect(lists[n][:, b0 * 8 : b1 * 8]), ACT.Sigmoid, scale=4.0)
-            elif kind == "by":
-                for k, (tl, b) in enumerate(n):
-                    nc.tensor.matmul(out=bank[t][:, blk(k)], lhsT=ywin[tl][:, blk(b)], rhs=ident[:], is_transpose=True, start=(k == 0), stop=False)
-                    place[(tl, b)] = (t, k)
-                left[t] = 2 * len(n)
-            elif kind == "m":
-                b0, b1 = h
-                js = slice(b0 * JB, b1 * JB)
-                nc.vector.scalar_tensor_tensor(out=m[t][n][:, js], in0=sig_at(t, n, b0, b1), scalar=-0.5, in1=cj[n][t][:, js], op0=ALU.add, op1=ALU.mult)
-                for b in range(b0, b1):
-                    bk, k = place[(t, b)]
-                    left[bk] = left[bk] - 1
-                    nc.tensor.matmul(out=bank[bk][:, blk(k)], lhsT=m[t][n][:, blk(b)], rhs=ident[:], is_transpose=True, start=False, stop=(left[bk] == 0))
-            elif kind == "th":
-                width = len(n) * JB
-                tanh_t = sb("tanh_%d_%d_%d" % (t, n[0][0], n[0][1]), [P, width], F32)
-                nc.scalar.activation(tanh_t[:], bank[t][:, 0:width], ACT.Tanh, scale=2.0)
-                for k, (tl, b) in enumerate(n):
-                    nc.tensor.transpose(zb[b][:, tl, :], tanh_t[:, blk(k)], ident[:])
-            elif kind == "deal":
-                dealt.extend(deal("w2d", w2w, w2s, nc.vector))
-            elif kind == "heat":
-                for k in range(2):
-                    nc.tensor.matmul_mx(
-                        out=bank[t][:], lhsT=w1dw[:, 0:P].bitcast(FP8X4), lhsT_scale=w1ds[:, 0:P],
-                        rhs=xg[:].bitcast(FP8X4), rhs_scale=xsg[:], start=True, stop=True,
-                    )
-            elif kind == "gn":
-                nc.vector.tensor_tensor(
-                    out=z16[t][:], in0=zb[t][:].rearrange("p t j -> p j t"),
-                    in1=gn_t[:].unsqueeze(1).to_broadcast([P, JB, PACK]), op=ALU.mult,
-                )
-            elif kind == "qz":
-                nc.vector.quantize_mx(out=zc[t][:].bitcast(FP8X4), scales=zs[t][:], in_=z16[t][:].rearrange("p j t -> p (j t)"))
-                ob = o_bank[t][:].rearrange("p (t j) -> p t j", t=PACK)
-                for k in range(PACK):
-                    nc.tensor.matmul_mx(
-                        out=ob[:, k, :], lhsT=dealt[0][:, blk(k)].bitcast(FP8X4), lhsT_scale=dealt[1][:, blk(k)],
-                        rhs=zc[t][:].bitcast(FP8X4), rhs_scale=zs[t][:], start=True, stop=True,
-                    )
-                nc.scalar.copy(out=ot[t][:], in_=ob)
-                nc.sync.dma_start(out=out_v[:, :, blk(t)], in_=ot[t][:])
-            elif kind == "o":
-                if n == "s":
-                    nc.scalar.copy(out=o16[t], in_=o_bank[t][:].rearrange("p (t j) -> p j t", t=PACK))
-                else:
-                    nc.vector.tensor_copy(out=o16[t], in_=ot[t][:].rearrange("p t j -> p j t"))
-            else:
-                js = slice(2 * t * JB, 2 * (t + 1) * JB)
-                nc.vector.quantize_mx(out=oc[:, js].bitcast(FP8X4), scales=osc[:, js], in_=o16_pair[t][:].rearrange("p j t -> p (j t)"))
-                nc.sync.dma_start(out=out_w[:, js], in_=oc[:, js].bitcast(I32))
-
+        part = [sb("part%d" % t, [P, S], F32) for t in range(PACK)]
+        a = [sb("a%d" % t, [P, S], F32) for t in range(PACK)]
+        sig = [sb("sig%d" % t, [P, 2, S], F32) for t in range(PACK)]
+        m = [sb("m%d" % t, [P, 2, S], F32) for t in range(PACK)]
+        zb = [bank[k] for k in ZB]
+        o_bank = [bank[k] for k in OB]
+        th = [sb("th%d" % k, [P, S], F32) for k in range(len(GROUPS))]
         place = {}
         left = {}
-        o_bank = [bank[k] for k in [2,1,0,3]]
-        oc = sb("oc", [P, S], U32)
-        osc = sb("osc", [P, S], U8)
-        out_v = out_0.rearrange("(p t) j -> p t j", t=PACK)
-        out_w = out_1[0].rearrange("p n t -> p (n t)").bitcast(I32)
         z16 = [sb("z16_%d" % b, [P, JB, PACK], BF16) for b in range(NJB)]
         zc = [sb("zc%d" % b, [P, JB], U32) for b in range(NJB)]
         zs = [sb("zs%d" % b, [P, JB], U8) for b in range(NJB)]
         ot = [sb("ot%d" % b, [P, PACK, JB], F32) for b in range(NJB)]
-        o16_pair = [sb("o16_%d" % k, [P, 2 * JB, PACK], BF16) for k in range(2)]
-        o16 = [o16_pair[b // 2][:, (b % 2) * JB : (b % 2 + 1) * JB, :] for b in range(NJB)]
+        o16_pair = [sb("o16_%d" % k, [P, HALF, PACK], BF16) for k in range(2)]
+        oc = sb("oc", [P, S], U32)
+        osc = sb("osc", [P, S], U8)
+        out_v = out_0.rearrange("(p t) j -> p t j", t=PACK)
+        out_w = out_1[0].rearrange("p n t -> p (n t)").bitcast(I32)
 
-        for item in [["by",0,[[0,0],[0,1],[0,2],[0,3]]],["by",2,[[1,0],[1,1],[2,0],[2,1]]],["by",3,[[3,2],[3,3]]],["g",0,0],["g",0,1],["add",0],["sig",0,0],["sig",0,1],["g",1,0],["g",1,1],["at",1,"s"],["ab",1,"s"],["by",1,[[3,0],[3,1]]],["sig",1,0],["sig",1,1],["g",2,0],["g",2,1],["m",0,0],["m",0,1],["add",2],["th",0,[[0,0],[0,1],[0,2],[0,3]]],["heat",0],["by",0,[[1,2],[1,3],[2,2],[2,3]]],["sig",2,0],["sig",2,1],["g",3,0],["g",3,1],["add",3],["sig",3,0,[0,2]],["sig",3,1,[0,2]],["m",1,0,[0,2]],["m",1,1,[0,2]],["m",2,0,[0,2]],["m",2,1,[0,2]],["th",2,[[1,0],[1,1],[2,0],[2,1]]],["sig",3,0,[2,4]],["sig",3,1,[2,4]],["m",3,0,[0,2]],["m",3,1,[0,2]],["th",1,[[3,0],[3,1]]],["m",1,0,[2,4]],["m",1,1,[2,4]],["m",2,0,[2,4]],["m",2,1,[2,4]],["th",0,[[1,2],[1,3],[2,2],[2,3]]],["m",3,0,[2,4]],["m",3,1,[2,4]],["th",3,[[3,2],[3,3]]],["deal",0],["gn",0],["qz",0],["gn",1],["qz",1],["gn",2],["qz",2],["gn",3],["qz",3],["o",0,"v"],["o",1,"v"],["qo",0],["o",2,"v"],["o",3,"v"],["qo",1]]:
-            step(*item)
+        def turn(dst, src, start, stop):
+            nc.tensor.matmul(out=dst, lhsT=src, rhs=ident[:], is_transpose=True, start=start, stop=stop)
+
+        def gather1(t, n, h):
+            nc.vector.tensor_tensor(out=g[t][n][:, half(h)], in0=y[t][:].indirect(lists[n][:, entries(h)]), in1=cpl[t][:, n, half(h)], op=ALU.mult)
+            if t in PE_PLANES:
+                dst = bank[SUM[t][h]]
+                if n == 0:
+                    for b in (2 * h, 2 * h + 1):
+                        turn(dst[:, blk(b)], y[t][:, blk(b)], b == 2 * h, False)
+                for b in (2 * h, 2 * h + 1):
+                    turn(dst[:, blk(b)], g[t][n][:, blk(b)], False, n == 1 and b == 2 * h + 1)
+
+        def round1(t):
+            for h in range(2):
+                for n in range(2):
+                    gather1(t, n, h)
+            if t not in PE_PLANES:
+                for dst, lhs, rhs in ((part[t], y[t], g[t][0]), (a[t], part[t], g[t][1])):
+                    for h in range(2):
+                        nc.vector.tensor_tensor(out=dst[:, half(h)], in0=lhs[:, half(h)], in1=rhs[:, half(h)], op=ALU.add)
+
+        def sum_out(t, h):
+            if t in V_PLANES:
+                nc.scalar.activation(part[t][:, half(h)], bank[SUM[t][h]][:, half(h)], ACT.Tanh)
+            else:
+                nc.scalar.copy(out=part[t][:, half(h)], in_=bank[SUM[t][h]][:, half(h)])
+            for b in (2 * h, 2 * h + 1):
+                turn(bank[BACK[t][h]][:, blk(b)], part[t][:, blk(b)], True, True)
+
+        def sum_back(t, h):
+            nc.scalar.copy(out=a[t][:, half(h)], in_=bank[BACK[t][h]][:, half(h)])
+
+        def gather2(t, b0, b1):
+            for n in range(2):
+                nc.scalar.activation(sig[t][:, n, b0 * JB : b1 * JB], a[t][:].indirect(lists[n][:, b0 * 8 : b1 * 8]), ACT.Sigmoid, scale=4.0)
+
+        hw = {t: (a[t] if t in PE_PLANES else sb("h%d" % t, [P, S], F32)) for t in V_PLANES}
+
+        def state(t):
+            nc.scalar.activation(hw[t][:], a[t][:], ACT.Tanh)
+
+        def fused(t, b0, b1):
+            js = slice(b0 * JB, b1 * JB)
+            for n in range(2):
+                nc.vector.tensor_tensor(out=m[t][:, n, js], in0=hw[t][:].indirect(lists[n][:, b0 * 8 : b1 * 8]), in1=cpl[t][:, n, js], op=ALU.mult)
+                for b in range(b0, b1):
+                    k, i = place[(t, b)]
+                    left[k] = left[k] - 1
+                    turn(bank[GROUPS[k][0]][:, blk(i)], m[t][:, n, blk(b)], False, left[k] == 0)
+
+        def open_acc(k):
+            bk, slots = GROUPS[k]
+            left[k] = 2 * len(slots)
+            for i, (t, b) in enumerate(slots):
+                place[(t, b)] = (k, i)
+                turn(bank[bk][:, blk(i)], y[t][:, blk(b)], i == 0, False)
+
+        def couple(t, b0, b1):
+            js = slice(b0 * JB, b1 * JB)
+            nc.vector.scalar_tensor_tensor(out=m[t][:, :, js], in0=sig[t][:, :, js], scalar=-0.5, in1=cpl[t][:, :, js], op0=ALU.add, op1=ALU.mult)
+            for b in range(b0, b1):
+                k, i = place[(t, b)]
+                for n in range(2):
+                    left[k] = left[k] - 1
+                    turn(bank[GROUPS[k][0]][:, blk(i)], m[t][:, n, blk(b)], False, left[k] == 0)
+
+        def tanh(k):
+            bk, slots = GROUPS[k]
+            for via in (False, True):
+                own = [i for i, (t, b) in enumerate(slots) if (t in V_PLANES) == via]
+                if own:
+                    js = slice(own[0] * JB, (own[-1] + 1) * JB)
+                    nc.scalar.activation(th[k][:, js], bank[bk][:, js], ACT.Tanh, scale=(1.0 if via else 2.0))
+            for i, (t, b) in enumerate(slots):
+                turn(zb[b][:, blk(t)], th[k][:, blk(i)], True, True)
+
+        def gain(b):
+            nc.vector.tensor_tensor(
+                out=z16[b][:], in0=zb[b][:].rearrange("p (t j) -> p j t", t=PACK),
+                in1=gn_t[:].unsqueeze(1).to_broadcast([P, JB, PACK]), op=ALU.mult,
+            )
+
+        def second_product(b):
+            nc.vector.quantize_mx(out=zc[b][:].bitcast(FP8X4), scales=zs[b][:], in_=z16[b][:].rearrange("p j t -> p (j t)"))
+            ob = o_bank[b][:].rearrange("p (t j) -> p t j", t=PACK)
+            for t in range(PACK):
+                nc.tensor.matmul_mx(
+                    out=ob[:, t, :], lhsT=w2dw[:, blk(t)].bitcast(FP8X4), lhsT_scale=w2ds[:, blk(t)],
+                    rhs=zc[b][:].bitcast(FP8X4), rhs_scale=zs[b][:], start=True, stop=True,
+                )
+
+        def result(b):
+            nc.scalar.copy(out=ot[b][:], in_=o_bank[b][:].rearrange("p (t j) -> p t j", t=PACK))
+            nc.sync.dma_start(out=out_v[:, :, blk(b)], in_=ot[b][:])
+
+        def round_out(b):
+            nc.vector.tensor_copy(out=o16_pair[b // 2][:, blk(b % 2), :], in_=ot[b][:].rearrange("p t j -> p j t"))
+
+        def planes(k):
+            nc.vector.quantize_mx(out=oc[:, half(k)].bitcast(FP8X4), scales=osc[:, half(k)], in_=o16_pair[k][:].rearrange("p j t -> p (j t)"))
+            nc.sync.dma_start(out=out_w[:, half(k)], in_=oc[:, half(k)].bitcast(I32))
+
+        round1(0)
+        open_acc(0)
+        open_acc(1)
+        round1(1)
+        sum_out(1, 0)
+        sum_back(1, 0)
+        sum_out(1, 1)
+        sum_back(1, 1)
+        gather2(0, 0, 2)
+        gather2(0, 2, 4)
+        round1(2)
+        sum_out(2, 0)
+        sum_back(2, 0)
+        sum_out(2, 1)
+        sum_back(2, 1)
+        open_acc(3)
+        couple(0, 0, 2)
+        couple(0, 2, 4)
+        gather2(1, 0, 2)
+        gather2(1, 2, 4)
+        round1(3)
+        state(3)
+        tanh(0)
+        open_acc(2)
+        couple(1, 0, 2)
+        couple(1, 2, 4)
+        gather2(2, 0, 2)
+        gather2(2, 2, 4)
+        tanh(1)
+        fused(3, 0, 2)
+        couple(2, 0, 2)
+        tanh(2)
+        fused(3, 2, 4)
+        couple(2, 2, 4)
+        tanh(3)
+        w2dw, w2ds = deal("w2d", w2w, w2s, nc.vector)
+        gain(0)
+        gain(1)
+        second_product(0)
+        second_product(1)
+        gain(2)
+        gain(3)
+        second_product(2)
+        second_product(3)
+        result(0)
+        result(1)
+        result(2)
+        result(3)
+        round_out(0)
+        round_out(1)
+        planes(0)
+        round_out(2)
+        round_out(3)
+        planes(1)
 
         for q in range(4):
             (nc.scalar if q < 3 else nc.sync).dma_start(out=out_2[0][4 * q : 4 * q + 4, :].bitcast(I32), in_=osc[32 * q : 32 * q + 4, :].bitcast(I32))

@@ -20,14 +20,14 @@ PACK = 4
 JB = 128
 NJB = S // JB
 HALF = S // 2
-SUM = {1: (4, 5), 2: (1, 2)}
-BACK = {1: (6, 7), 2: (1, 2)}
-GROUPS = [(0, [(0, 0), (0, 1), (0, 2), (0, 3)]), (3, [(1, 0), (1, 1), (1, 2), (1, 3)]), (0, [(2, 0), (2, 1), (3, 0), (3, 1)]), (1, [(2, 2), (2, 3), (3, 2), (3, 3)])]
+SUM = {0: (4, 5), 2: (4, 5)}
+BACK = {0: (0, 3), 2: (1, 2)}
+GROUPS = [(0, [(0, 0), (0, 1), (0, 2), (0, 3)]), (3, [(1, 0), (1, 1), (1, 2), (1, 3)]), (0, [(2, 0), (2, 1), (2, 2), (2, 3)]), (1, [(3, 0), (3, 1)]), (2, [(3, 2), (3, 3)])]
 ZB = (4, 5, 6, 7)
-OB = (2, 3, 0, 1)
+OB = (3, 0, 1, 2)
 V_PLANES = (3,)
 FLOPS = 2 * 2 * 512 * 512 * 512
-PE_PLANES = (1, 2)
+PE_PLANES = (0, 2)
 
 
 def tile_picked_mfield_none_po_kernel(
@@ -124,9 +124,9 @@ def tile_picked_mfield_none_po_kernel(
             nc.scalar.activation(y[t][:, js], dst, ACT.Copy, scale=(1.0 if t in V_PLANES else 0.5))
 
         for h in range(2):
-            first_product(0, bank[(4, 5, 6, 7, 3)[h]][:, 0:HALF], half(h))
+            first_product(0, bank[(1, 2, 6, 7, 0)[h]][:, 0:HALF], half(h))
         for t in range(1, PACK):
-            first_product(t, bank[(4, 5, 6, 7, 3)[t + 1]][:], slice(0, S))
+            first_product(t, bank[(1, 2, 6, 7, 0)[t + 1]][:], slice(0, S))
 
         g = [[sb("g%d_%d" % (t, n), [P, S], F32) for n in range(2)] for t in range(PACK)]
         part = [sb("part%d" % t, [P, S], F32) for t in range(PACK)]
@@ -138,11 +138,12 @@ def tile_picked_mfield_none_po_kernel(
         th = [sb("th%d" % k, [P, S], F32) for k in range(len(GROUPS))]
         place = {}
         left = {}
-        z16 = [sb("z16_%d" % b, [P, JB, PACK], BF16) for b in range(NJB)]
+        z16_pair = [keep.tile([P, HALF, PACK], BF16, name="z16_%d" % k, tag="pair16_%d" % k, align_bytes=64) for k in range(2)]
+        z16 = [z16_pair[b // 2][:, blk(b % 2), :] for b in range(NJB)]
         zc = [sb("zc%d" % b, [P, JB], U32) for b in range(NJB)]
         zs = [sb("zs%d" % b, [P, JB], U8) for b in range(NJB)]
         ot = [sb("ot%d" % b, [P, PACK, JB], F32) for b in range(NJB)]
-        o16_pair = [sb("o16_%d" % k, [P, HALF, PACK], BF16) for k in range(2)]
+        o16_pair = {}
         oc = sb("oc", [P, S], U32)
         osc = sb("osc", [P, S], U8)
         out_v = out_0.rearrange("(p t) j -> p t j", t=PACK)
@@ -227,12 +228,12 @@ def tile_picked_mfield_none_po_kernel(
 
         def gain(b):
             nc.vector.tensor_tensor(
-                out=z16[b][:], in0=zb[b][:].rearrange("p (t j) -> p j t", t=PACK),
+                out=z16[b], in0=zb[b][:].rearrange("p (t j) -> p j t", t=PACK),
                 in1=gn_t[:].unsqueeze(1).to_broadcast([P, JB, PACK]), op=ALU.mult,
             )
 
         def second_product(b):
-            nc.vector.quantize_mx(out=zc[b][:].bitcast(FP8X4), scales=zs[b][:], in_=z16[b][:].rearrange("p j t -> p (j t)"))
+            nc.vector.quantize_mx(out=zc[b][:].bitcast(FP8X4), scales=zs[b][:], in_=z16[b].rearrange("p j t -> p (j t)"))
             ob = o_bank[b][:].rearrange("p (t j) -> p t j", t=PACK)
             for t in range(PACK):
                 nc.tensor.matmul_mx(
@@ -245,6 +246,8 @@ def tile_picked_mfield_none_po_kernel(
             nc.sync.dma_start(out=out_v[:, :, blk(b)], in_=ot[b][:])
 
         def round_out(b):
+            if b % 2 == 0:
+                o16_pair[b // 2] = keep.tile([P, HALF, PACK], BF16, name="o16_%d" % (b // 2), tag="pair16_%d" % (1 - b // 2), align_bytes=64)
             nc.vector.tensor_copy(out=o16_pair[b // 2][:, blk(b % 2), :], in_=ot[b][:].rearrange("p t j -> p j t"))
 
         def planes(k):
@@ -252,13 +255,11 @@ def tile_picked_mfield_none_po_kernel(
             nc.sync.dma_start(out=out_w[:, half(k)], in_=oc[:, half(k)].bitcast(I32))
 
         round1(0)
-        open_acc(0)
-        open_acc(1)
+        sum_out(0, 0)
+        sum_back(0, 0)
+        sum_out(0, 1)
+        sum_back(0, 1)
         round1(1)
-        sum_out(1, 0)
-        sum_back(1, 0)
-        sum_out(1, 1)
-        sum_back(1, 1)
         gather2(0, 0, 2)
         gather2(0, 2, 4)
         round1(2)
@@ -266,26 +267,30 @@ def tile_picked_mfield_none_po_kernel(
         sum_back(2, 0)
         sum_out(2, 1)
         sum_back(2, 1)
-        open_acc(3)
-        couple(0, 0, 2)
-        couple(0, 2, 4)
+        open_acc(0)
+        open_acc(1)
         gather2(1, 0, 2)
         gather2(1, 2, 4)
+        couple(0, 0, 2)
+        couple(0, 2, 4)
         round1(3)
-        state(3)
+        gather2(2, 0, 2)
         tanh(0)
+        gather2(2, 2, 4)
+        state(3)
         open_acc(2)
+        open_acc(3)
+        open_acc(4)
         couple(1, 0, 2)
         couple(1, 2, 4)
-        gather2(2, 0, 2)
-        gather2(2, 2, 4)
         tanh(1)
-        fused(3, 0, 2)
         couple(2, 0, 2)
-        tanh(2)
-        fused(3, 2, 4)
         couple(2, 2, 4)
+        tanh(2)
+        fused(3, 0, 2)
         tanh(3)
+        fused(3, 2, 4)
+        tanh(4)
         w2dw, w2ds = deal("w2d", w2w, w2s, nc.vector)
         gain(0)
         gain(1)

@@ -17,17 +17,21 @@ P = 128
 T = 2048
 S = 512
 PACK = 4
+LAST = PACK - 1
 JB = 128
 NJB = S // JB
 HALF = S // 2
-SUM = {0: (4, 5), 2: (4, 5)}
-BACK = {0: (0, 3), 2: (1, 2)}
-GROUPS = [(0, [(0, 0), (0, 1), (0, 2), (0, 3)]), (3, [(1, 0), (1, 1), (1, 2), (1, 3)]), (0, [(2, 0), (2, 1), (2, 2), (2, 3)]), (1, [(3, 0), (3, 1)]), (2, [(3, 2), (3, 3)])]
-ZB = (4, 5, 6, 7)
-OB = (3, 0, 1, 2)
-V_PLANES = (3,)
+GROUP = 16
+QUADS = 4
 FLOPS = 2 * 2 * 512 * 512 * 512
-PE_PLANES = (0, 2)
+
+Y_BANKS = (1, 2, 6, 7, 0)
+TURNED = (0, 2)
+SUM_BANKS = (4, 5)
+BACK_BANKS = {0: (0, 3), 2: (1, 2)}
+Z_BANKS = (4, 5, 6, 7)
+OUT_BANKS = (3, 0, 1, 2)
+ROUND2 = ((0, 0, (0, 1, 2, 3)), (3, 1, (0, 1, 2, 3)), (0, 2, (0, 1, 2, 3)), (1, LAST, (0, 1)), (2, LAST, (2, 3)))
 
 
 def tile_picked_mfield_none_po_kernel(
@@ -38,8 +42,8 @@ def tile_picked_mfield_none_po_kernel(
         keep = ctx.enter_context(tc.tile_pool(name="keep", bufs=1))
         psum = ctx.enter_context(tc.psum_pool(name="psum", bufs=1))
 
-        def sb(name, shape, dtype):
-            return keep.tile(shape, dtype, name=name, align_bytes=64)
+        def sb(name, shape, dtype, tag=None):
+            return keep.tile(shape, dtype, name=name, tag=tag or name, align_bytes=64)
 
         bank = [psum.tile([P, S], F32, name="bank%d" % k) for k in range(8)]
 
@@ -49,50 +53,56 @@ def tile_picked_mfield_none_po_kernel(
         def half(h):
             return slice(h * HALF, (h + 1) * HALF)
 
+        def blocks_of(h):
+            return (2 * h, 2 * h + 1)
+
         def entries(h):
-            return slice(h * HALF // 16, (h + 1) * HALF // 16)
+            return slice(h * HALF // GROUP, (h + 1) * HALF // GROUP)
 
         def words_of(dram):
             return dram[0].rearrange("p n t -> p (n t)").bitcast(I32)
 
-        def load_scales(queue, tile, dram, q):
-            queue.dma_start(out=tile[32 * q : 32 * q + 4, :].bitcast(I32), in_=dram[0][4 * q : 4 * q + 4, :].bitcast(I32))
+        def scale_rows(tile, dram, q):
+            return tile[32 * q : 32 * q + 4, :].bitcast(I32), dram[0][4 * q : 4 * q + 4, :].bitcast(I32)
+
+        def load_scales(tile, dram, q):
+            rows, source = scale_rows(tile, dram, q)
+            nc.sync.dma_start(out=rows, in_=source)
 
         xs = sb("xs", [P, T], U8)
         w1s = sb("w1s", [P, S], U8)
         w2s = sb("w2s", [P, S], U8)
-        for plane in (xs, w1s, w2s):
-            nc.gpsimd.memset(plane[:].bitcast(I32), 0)
+        for scales in (xs, w1s, w2s):
+            nc.gpsimd.memset(scales[:].bitcast(I32), 0)
         xw = sb("xw", [P, T], U32)
         w1w = sb("w1w", [P, S], I32)
         w2w = sb("w2w", [P, S], I32)
-        offs_t = keep.tile([P, S // 16], U16, name="offs_t")
-        p1_t = keep.tile([P, S // 16], U16, name="p1_t")
-        p2_t = keep.tile([P, S // 16], U16, name="p2_t")
+        offs_t = keep.tile([P, S // GROUP], U16, name="offs_t")
+        p1_t = keep.tile([P, S // GROUP], U16, name="p1_t")
+        p2_t = keep.tile([P, S // GROUP], U16, name="p2_t")
         lists = (p1_t, p2_t)
         cpl = [sb("cpl%d" % t, [P, 2, S], F32) for t in range(PACK)]
         gn_t = sb("gn_t", [P, PACK], F32)
         cj_v = [c.rearrange("(p t) j -> p t j", t=PACK) for c in (cj1, cj2)]
 
         nc.sync.dma_start(offs_t[:], offs)
-        for q in range(4):
-            load_scales(nc.sync, xs, x_scales, q)
+        for q in range(QUADS):
+            load_scales(xs, x_scales, q)
         nc.sync.dma_start(out=w1w[:], in_=words_of(w1_words))
-        load_scales(nc.sync, w1s, w1_scales, 0)
+        load_scales(w1s, w1_scales, 0)
         nc.sync.dma_start(out=xw[:].bitcast(I32), in_=words_of(x_words))
-        for q in range(1, 4):
-            load_scales(nc.sync, w1s, w1_scales, q)
-        nc.sync.dma_start(p1_t[:], p1)
-        nc.sync.dma_start(out=cpl[0][:, 0, :], in_=cj_v[0][:, 0, :])
-        nc.sync.dma_start(p2_t[:], p2)
-        nc.sync.dma_start(out=cpl[0][:, 1, :], in_=cj_v[1][:, 0, :])
+        for q in range(1, QUADS):
+            load_scales(w1s, w1_scales, q)
+        for n, (tile, source) in enumerate(((p1_t, p1), (p2_t, p2))):
+            nc.sync.dma_start(tile[:], source)
+            nc.sync.dma_start(out=cpl[0][:, n, :], in_=cj_v[n][:, 0, :])
         for t in range(1, PACK):
             for n in range(2):
                 nc.sync.dma_start(out=cpl[t][:, n, :], in_=cj_v[n][:, t, :])
         nc.sync.dma_start(out=gn_t[:], in_=gn.rearrange("(p t) o -> p (t o)", t=PACK))
         nc.sync.dma_start(out=w2w[:], in_=words_of(w2_words))
-        for q in range(4):
-            load_scales(nc.sync, w2s, w2_scales, q)
+        for q in range(QUADS):
+            load_scales(w2s, w2_scales, q)
 
         ident = sb("ident", [P, P], F32)
         make_identity(nc, ident[:])
@@ -100,17 +110,24 @@ def tile_picked_mfield_none_po_kernel(
         warm = sb("warm", [P, 1], F32)
         nc.scalar.activation(warm[:], ident[:, 0:1], ACT.Sigmoid)
 
-        def deal(name, words, scales, scale_engine):
+        def deal(name, words, scales, pieces):
             dw = sb(name + "_w", [P, S], I32)
             ds = sb(name + "_s", [P, S], U8)
-            nc.vector.tensor_copy(out=dw[:].rearrange("p (t c i) -> p c t i", t=PACK, i=4), in_=words[:].rearrange("p (c i t) -> p c t i", t=PACK, i=4))
-            scale_engine.tensor_copy(out=ds[:].rearrange("p (t m) -> p t m", t=PACK), in_=scales[:].rearrange("p (m t) -> p t m", t=PACK))
+            nc.vector.tensor_copy(
+                out=dw[:].rearrange("p (t c i) -> p c t i", t=PACK, i=4),
+                in_=words[:].rearrange("p (c i t) -> p c t i", t=PACK, i=4),
+            )
+            for engine, ts in pieces:
+                engine.tensor_copy(
+                    out=ds[:].rearrange("p (t m) -> p t m", t=PACK)[:, ts, :],
+                    in_=scales[:].rearrange("p (m t) -> p t m", t=PACK)[:, ts, :],
+                )
             return dw, ds
 
         xsg = sb("xsg", [P, S], U8)
         xg = sb("xg", [P, S], U32)
         nc.vector.tensor_copy(out=xsg[:], in_=xs[:].indirect(offs_t[:]))
-        w1dw, w1ds = deal("w1d", w1w, w1s, nc.gpsimd)
+        w1dw, w1ds = deal("w1d", w1w, w1s, ((nc.gpsimd, slice(0, 1)), (nc.vector, slice(1, PACK))))
         for h in range(2):
             nc.vector.tensor_copy(out=xg[:, half(h)], in_=xw[:].indirect(offs_t[:, entries(h)]))
 
@@ -121,195 +138,150 @@ def tile_picked_mfield_none_po_kernel(
                 out=dst, lhsT=w1dw[:, blk(t)].bitcast(FP8X4), lhsT_scale=w1ds[:, blk(t)],
                 rhs=xg[:, js].bitcast(FP8X4), rhs_scale=xsg[:, js], start=True, stop=True,
             )
-            nc.scalar.activation(y[t][:, js], dst, ACT.Copy, scale=(1.0 if t in V_PLANES else 0.5))
+            nc.scalar.activation(y[t][:, js], dst, ACT.Copy, scale=(1.0 if t == LAST else 0.5))
 
         for h in range(2):
-            first_product(0, bank[(1, 2, 6, 7, 0)[h]][:, 0:HALF], half(h))
+            first_product(0, bank[Y_BANKS[h]][:, 0:HALF], half(h))
         for t in range(1, PACK):
-            first_product(t, bank[(1, 2, 6, 7, 0)[t + 1]][:], slice(0, S))
+            first_product(t, bank[Y_BANKS[t + 1]][:], slice(0, S))
 
         g = [[sb("g%d_%d" % (t, n), [P, S], F32) for n in range(2)] for t in range(PACK)]
         part = [sb("part%d" % t, [P, S], F32) for t in range(PACK)]
         a = [sb("a%d" % t, [P, S], F32) for t in range(PACK)]
-        sig = [sb("sig%d" % t, [P, 2, S], F32) for t in range(PACK)]
+        sig = [sb("sig%d" % t, [P, 2, S], F32) for t in range(LAST)]
         m = [sb("m%d" % t, [P, 2, S], F32) for t in range(PACK)]
-        zb = [bank[k] for k in ZB]
-        o_bank = [bank[k] for k in OB]
-        th = [sb("th%d" % k, [P, S], F32) for k in range(len(GROUPS))]
-        place = {}
-        left = {}
-        z16_pair = [keep.tile([P, HALF, PACK], BF16, name="z16_%d" % k, tag="pair16_%d" % k, align_bytes=64) for k in range(2)]
+        th = [sb("th%d" % k, [P, S], F32) for k in range(len(ROUND2))]
+        z16_pair = [sb("z16_%d" % k, [P, HALF, PACK], BF16, tag="pair16_%d" % k) for k in range(2)]
         z16 = [z16_pair[b // 2][:, blk(b % 2), :] for b in range(NJB)]
         zc = [sb("zc%d" % b, [P, JB], U32) for b in range(NJB)]
         zs = [sb("zs%d" % b, [P, JB], U8) for b in range(NJB)]
         ot = [sb("ot%d" % b, [P, PACK, JB], F32) for b in range(NJB)]
-        o16_pair = {}
         oc = sb("oc", [P, S], U32)
         osc = sb("osc", [P, S], U8)
+        h_last = sb("h_last", [P, S], F32)
         out_v = out_0.rearrange("(p t) j -> p t j", t=PACK)
-        out_w = out_1[0].rearrange("p n t -> p (n t)").bitcast(I32)
+        out_w = words_of(out_1)
 
         def turn(dst, src, start, stop):
             nc.tensor.matmul(out=dst, lhsT=src, rhs=ident[:], is_transpose=True, start=start, stop=stop)
 
-        def gather1(t, n, h):
-            nc.vector.tensor_tensor(out=g[t][n][:, half(h)], in0=y[t][:].indirect(lists[n][:, entries(h)]), in1=cpl[t][:, n, half(h)], op=ALU.mult)
-            if t in PE_PLANES:
-                dst = bank[SUM[t][h]]
-                if n == 0:
-                    for b in (2 * h, 2 * h + 1):
-                        turn(dst[:, blk(b)], y[t][:, blk(b)], b == 2 * h, False)
-                for b in (2 * h, 2 * h + 1):
-                    turn(dst[:, blk(b)], g[t][n][:, blk(b)], False, n == 1 and b == 2 * h + 1)
-
         def round1(t):
             for h in range(2):
+                first, second = blocks_of(h)
                 for n in range(2):
-                    gather1(t, n, h)
-            if t not in PE_PLANES:
+                    nc.vector.tensor_tensor(
+                        out=g[t][n][:, half(h)], in0=y[t][:].indirect(lists[n][:, entries(h)]),
+                        in1=cpl[t][:, n, half(h)], op=ALU.mult,
+                    )
+                    if t in TURNED:
+                        terms = (y[t], g[t][0]) if n == 0 else (g[t][1],)
+                        for term in terms:
+                            for b in (first, second):
+                                opens = term is y[t] and b == first
+                                turn(bank[SUM_BANKS[h]][:, blk(b)], term[:, blk(b)], opens, n == 1 and b == second)
+            if t in TURNED:
+                for h in range(2):
+                    nc.scalar.copy(out=part[t][:, half(h)], in_=bank[SUM_BANKS[h]][:, half(h)])
+                    back = bank[BACK_BANKS[t][h]]
+                    for b in blocks_of(h):
+                        turn(back[:, blk(b)], part[t][:, blk(b)], True, True)
+                    nc.scalar.copy(out=a[t][:, half(h)], in_=back[:, half(h)])
+            else:
                 for dst, lhs, rhs in ((part[t], y[t], g[t][0]), (a[t], part[t], g[t][1])):
                     for h in range(2):
                         nc.vector.tensor_tensor(out=dst[:, half(h)], in0=lhs[:, half(h)], in1=rhs[:, half(h)], op=ALU.add)
 
-        def sum_out(t, h):
-            if t in V_PLANES:
-                nc.scalar.activation(part[t][:, half(h)], bank[SUM[t][h]][:, half(h)], ACT.Tanh)
-            else:
-                nc.scalar.copy(out=part[t][:, half(h)], in_=bank[SUM[t][h]][:, half(h)])
-            for b in (2 * h, 2 * h + 1):
-                turn(bank[BACK[t][h]][:, blk(b)], part[t][:, blk(b)], True, True)
-
-        def sum_back(t, h):
-            nc.scalar.copy(out=a[t][:, half(h)], in_=bank[BACK[t][h]][:, half(h)])
-
-        def gather2(t, b0, b1):
+        def sigmoids(t, h):
             for n in range(2):
-                nc.scalar.activation(sig[t][:, n, b0 * JB : b1 * JB], a[t][:].indirect(lists[n][:, b0 * 8 : b1 * 8]), ACT.Sigmoid, scale=4.0)
+                nc.scalar.activation(sig[t][:, n, half(h)], a[t][:].indirect(lists[n][:, entries(h)]), ACT.Sigmoid, scale=4.0)
 
-        hw = {t: (a[t] if t in PE_PLANES else sb("h%d" % t, [P, S], F32)) for t in V_PLANES}
-
-        def state(t):
-            nc.scalar.activation(hw[t][:], a[t][:], ACT.Tanh)
-
-        def fused(t, b0, b1):
-            js = slice(b0 * JB, b1 * JB)
-            for n in range(2):
-                nc.vector.tensor_tensor(out=m[t][:, n, js], in0=hw[t][:].indirect(lists[n][:, b0 * 8 : b1 * 8]), in1=cpl[t][:, n, js], op=ALU.mult)
-                for b in range(b0, b1):
-                    k, i = place[(t, b)]
-                    left[k] = left[k] - 1
-                    turn(bank[GROUPS[k][0]][:, blk(i)], m[t][:, n, blk(b)], False, left[k] == 0)
-
-        def open_acc(k):
-            bk, slots = GROUPS[k]
-            left[k] = 2 * len(slots)
-            for i, (t, b) in enumerate(slots):
-                place[(t, b)] = (k, i)
+        def open_sum(k):
+            bk, t, bs = ROUND2[k]
+            for i, b in enumerate(bs):
                 turn(bank[bk][:, blk(i)], y[t][:, blk(b)], i == 0, False)
 
-        def couple(t, b0, b1):
-            js = slice(b0 * JB, b1 * JB)
-            nc.vector.scalar_tensor_tensor(out=m[t][:, :, js], in0=sig[t][:, :, js], scalar=-0.5, in1=cpl[t][:, :, js], op0=ALU.add, op1=ALU.mult)
-            for b in range(b0, b1):
-                k, i = place[(t, b)]
-                for n in range(2):
-                    left[k] = left[k] - 1
-                    turn(bank[GROUPS[k][0]][:, blk(i)], m[t][:, n, blk(b)], False, left[k] == 0)
+        def couple(t):
+            bk, bs = ROUND2[t][0], ROUND2[t][2]
+            for h in range(2):
+                nc.vector.scalar_tensor_tensor(
+                    out=m[t][:, :, half(h)], in0=sig[t][:, :, half(h)], scalar=-0.5, in1=cpl[t][:, :, half(h)],
+                    op0=ALU.add, op1=ALU.mult,
+                )
+                for b in blocks_of(h):
+                    for n in range(2):
+                        turn(bank[bk][:, blk(b)], m[t][:, n, blk(b)], False, b == bs[-1] and n == 1)
 
-        def tanh(k):
-            bk, slots = GROUPS[k]
-            for via in (False, True):
-                own = [i for i, (t, b) in enumerate(slots) if (t in V_PLANES) == via]
-                if own:
-                    js = slice(own[0] * JB, (own[-1] + 1) * JB)
-                    nc.scalar.activation(th[k][:, js], bank[bk][:, js], ACT.Tanh, scale=(1.0 if via else 2.0))
-            for i, (t, b) in enumerate(slots):
-                turn(zb[b][:, blk(t)], th[k][:, blk(i)], True, True)
+        def couple_last(h):
+            bk, t, bs = ROUND2[LAST + h]
+            for n in range(2):
+                nc.vector.tensor_tensor(
+                    out=m[t][:, n, half(h)], in0=h_last[:].indirect(lists[n][:, entries(h)]),
+                    in1=cpl[t][:, n, half(h)], op=ALU.mult,
+                )
+                for i, b in enumerate(bs):
+                    turn(bank[bk][:, blk(i)], m[t][:, n, blk(b)], False, b == bs[-1] and n == 1)
+
+        def close_sum(k):
+            bk, t, bs = ROUND2[k]
+            js = slice(0, len(bs) * JB)
+            nc.scalar.activation(th[k][:, js], bank[bk][:, js], ACT.Tanh, scale=(1.0 if t == LAST else 2.0))
+            for i, b in enumerate(bs):
+                turn(bank[Z_BANKS[b]][:, blk(t)], th[k][:, blk(i)], True, True)
+
+        round1(0)
+        round1(1)
+        for h in range(2):
+            sigmoids(0, h)
+        round1(2)
+        open_sum(0)
+        open_sum(1)
+        for h in range(2):
+            sigmoids(1, h)
+        couple(0)
+        round1(LAST)
+        sigmoids(2, 0)
+        close_sum(0)
+        sigmoids(2, 1)
+        nc.scalar.activation(h_last[:], a[LAST][:], ACT.Tanh)
+        for k in range(2, len(ROUND2)):
+            open_sum(k)
+        for t in (1, 2):
+            couple(t)
+            close_sum(t)
+        for h in range(2):
+            couple_last(h)
+            close_sum(LAST + h)
+        w2dw, w2ds = deal("w2d", w2w, w2s, ((nc.vector, slice(0, PACK)),))
 
         def gain(b):
             nc.vector.tensor_tensor(
-                out=z16[b], in0=zb[b][:].rearrange("p (t j) -> p j t", t=PACK),
+                out=z16[b], in0=bank[Z_BANKS[b]][:].rearrange("p (t j) -> p j t", t=PACK),
                 in1=gn_t[:].unsqueeze(1).to_broadcast([P, JB, PACK]), op=ALU.mult,
             )
 
         def second_product(b):
             nc.vector.quantize_mx(out=zc[b][:].bitcast(FP8X4), scales=zs[b][:], in_=z16[b].rearrange("p j t -> p (j t)"))
-            ob = o_bank[b][:].rearrange("p (t j) -> p t j", t=PACK)
             for t in range(PACK):
                 nc.tensor.matmul_mx(
-                    out=ob[:, t, :], lhsT=w2dw[:, blk(t)].bitcast(FP8X4), lhsT_scale=w2ds[:, blk(t)],
+                    out=bank[OUT_BANKS[b]][:, blk(t)], lhsT=w2dw[:, blk(t)].bitcast(FP8X4), lhsT_scale=w2ds[:, blk(t)],
                     rhs=zc[b][:].bitcast(FP8X4), rhs_scale=zs[b][:], start=True, stop=True,
                 )
 
-        def result(b):
-            nc.scalar.copy(out=ot[b][:], in_=o_bank[b][:].rearrange("p (t j) -> p t j", t=PACK))
+        for h in range(2):
+            for b in blocks_of(h):
+                gain(b)
+            for b in blocks_of(h):
+                second_product(b)
+        for b in range(NJB):
+            nc.scalar.copy(out=ot[b][:], in_=bank[OUT_BANKS[b]][:].rearrange("p (t j) -> p t j", t=PACK))
             nc.sync.dma_start(out=out_v[:, :, blk(b)], in_=ot[b][:])
 
-        def round_out(b):
-            if b % 2 == 0:
-                o16_pair[b // 2] = keep.tile([P, HALF, PACK], BF16, name="o16_%d" % (b // 2), tag="pair16_%d" % (1 - b // 2), align_bytes=64)
-            nc.vector.tensor_copy(out=o16_pair[b // 2][:, blk(b % 2), :], in_=ot[b][:].rearrange("p t j -> p j t"))
-
-        def planes(k):
-            nc.vector.quantize_mx(out=oc[:, half(k)].bitcast(FP8X4), scales=osc[:, half(k)], in_=o16_pair[k][:].rearrange("p j t -> p (j t)"))
-            nc.sync.dma_start(out=out_w[:, half(k)], in_=oc[:, half(k)].bitcast(I32))
-
-        round1(0)
-        sum_out(0, 0)
-        sum_back(0, 0)
-        sum_out(0, 1)
-        sum_back(0, 1)
-        round1(1)
-        gather2(0, 0, 2)
-        gather2(0, 2, 4)
-        round1(2)
-        sum_out(2, 0)
-        sum_back(2, 0)
-        sum_out(2, 1)
-        sum_back(2, 1)
-        open_acc(0)
-        open_acc(1)
-        gather2(1, 0, 2)
-        gather2(1, 2, 4)
-        couple(0, 0, 2)
-        couple(0, 2, 4)
-        round1(3)
-        gather2(2, 0, 2)
-        tanh(0)
-        gather2(2, 2, 4)
-        state(3)
-        open_acc(2)
-        open_acc(3)
-        open_acc(4)
-        couple(1, 0, 2)
-        couple(1, 2, 4)
-        tanh(1)
-        couple(2, 0, 2)
-        couple(2, 2, 4)
-        tanh(2)
-        fused(3, 0, 2)
-        tanh(3)
-        fused(3, 2, 4)
-        tanh(4)
-        w2dw, w2ds = deal("w2d", w2w, w2s, nc.vector)
-        gain(0)
-        gain(1)
-        second_product(0)
-        second_product(1)
-        gain(2)
-        gain(3)
-        second_product(2)
-        second_product(3)
-        result(0)
-        result(1)
-        result(2)
-        result(3)
-        round_out(0)
-        round_out(1)
-        planes(0)
-        round_out(2)
-        round_out(3)
-        planes(1)
-
-        for q in range(4):
-            (nc.scalar if q < 3 else nc.sync).dma_start(out=out_2[0][4 * q : 4 * q + 4, :].bitcast(I32), in_=osc[32 * q : 32 * q + 4, :].bitcast(I32))
+        for h, queue in enumerate((nc.sync, nc.scalar)):
+            o16 = sb("o16_%d" % h, [P, HALF, PACK], BF16, tag="pair16_%d" % (1 - h))
+            for i, b in enumerate(blocks_of(h)):
+                nc.vector.tensor_copy(out=o16[:, blk(i), :], in_=ot[b][:].rearrange("p t j -> p j t"))
+            nc.vector.quantize_mx(out=oc[:, half(h)].bitcast(FP8X4), scales=osc[:, half(h)], in_=o16[:].rearrange("p j t -> p (j t)"))
+            queue.dma_start(out=out_w[:, half(h)], in_=oc[:, half(h)].bitcast(I32))
+        for q in range(QUADS):
+            rows, target = scale_rows(osc, out_2, q)
+            (nc.scalar if q < QUADS // 2 else nc.sync).dma_start(out=target, in_=rows)

@@ -30,8 +30,8 @@ TURNED = (0, 2)
 SUM_BANKS = (4, 5)
 BACK_BANKS = {0: (0, 3), 2: (1, 2)}
 Z_BANKS = (4, 5, 6, 7)
-OUT_BANKS = (3, 0, 1, 2)
-ROUND2 = ((0, 0, (0, 1, 2, 3)), (3, 1, (0, 1, 2, 3)), (0, 2, (0, 1, 2, 3)), (1, LAST, (0, 1)), (2, LAST, (2, 3)))
+OUT_BANKS = (0, 3, 2, 1)
+ROUND2 = ((0, 0, (0, 1, 2, 3)), (3, 1, (0, 1, 2, 3)), (2, 2, (0, 1, 2, 3)), (1, LAST, (0, 1)))
 
 
 def tile_picked_mfield_none_po_kernel(
@@ -93,6 +93,7 @@ def tile_picked_mfield_none_po_kernel(
         nc.sync.dma_start(out=xw[:].bitcast(I32), in_=words_of(x_words))
         for q in range(1, QUADS):
             load_scales(w1s, w1_scales, q)
+        nc.sync.dma_start(out=w2w[:], in_=words_of(w2_words))
         for n, (tile, source) in enumerate(((p1_t, p1), (p2_t, p2))):
             nc.sync.dma_start(tile[:], source)
             nc.sync.dma_start(out=cpl[0][:, n, :], in_=cj_v[n][:, 0, :])
@@ -100,7 +101,6 @@ def tile_picked_mfield_none_po_kernel(
             for n in range(2):
                 nc.sync.dma_start(out=cpl[t][:, n, :], in_=cj_v[n][:, t, :])
         nc.sync.dma_start(out=gn_t[:], in_=gn.rearrange("(p t) o -> p (t o)", t=PACK))
-        nc.sync.dma_start(out=w2w[:], in_=words_of(w2_words))
         for q in range(QUADS):
             load_scales(w2s, w2_scales, q)
 
@@ -110,26 +110,31 @@ def tile_picked_mfield_none_po_kernel(
         warm = sb("warm", [P, 1], F32)
         nc.scalar.activation(warm[:], ident[:, 0:1], ACT.Sigmoid)
 
-        def deal(name, words, scales, pieces):
-            dw = sb(name + "_w", [P, S], I32)
-            ds = sb(name + "_s", [P, S], U8)
+        def deal_words(name, words, tag=None):
+            dw = sb(name, [P, S], I32, tag=tag)
             nc.vector.tensor_copy(
                 out=dw[:].rearrange("p (t c i) -> p c t i", t=PACK, i=4),
                 in_=words[:].rearrange("p (c i t) -> p c t i", t=PACK, i=4),
             )
+            return dw
+
+        def deal_scales(name, scales, pieces, tag=None):
+            ds = sb(name, [P, S], U8, tag=tag)
             for engine, ts in pieces:
                 engine.tensor_copy(
                     out=ds[:].rearrange("p (t m) -> p t m", t=PACK)[:, ts, :],
                     in_=scales[:].rearrange("p (m t) -> p t m", t=PACK)[:, ts, :],
                 )
-            return dw, ds
+            return ds
 
         xsg = sb("xsg", [P, S], U8)
         xg = sb("xg", [P, S], U32)
         nc.vector.tensor_copy(out=xsg[:], in_=xs[:].indirect(offs_t[:]))
-        w1dw, w1ds = deal("w1d", w1w, w1s, ((nc.gpsimd, slice(0, 1)), (nc.vector, slice(1, PACK))))
+        w1dw = deal_words("w1dw", w1w)
+        w1ds = deal_scales("w1ds", w1s, ((nc.gpsimd, slice(0, 1)), (nc.vector, slice(1, PACK))))
         for h in range(2):
             nc.vector.tensor_copy(out=xg[:, half(h)], in_=xw[:].indirect(offs_t[:, entries(h)]))
+        w2dw = deal_words("w2dw", w2w, tag="xw")
 
         y = [sb("y%d" % t, [P, S], F32) for t in range(PACK)]
 
@@ -211,15 +216,11 @@ def tile_picked_mfield_none_po_kernel(
                     for n in range(2):
                         turn(bank[bk][:, blk(b)], m[t][:, n, blk(b)], False, b == bs[-1] and n == 1)
 
-        def couple_last(h):
-            bk, t, bs = ROUND2[LAST + h]
-            for n in range(2):
-                nc.vector.tensor_tensor(
-                    out=m[t][:, n, half(h)], in0=h_last[:].indirect(lists[n][:, entries(h)]),
-                    in1=cpl[t][:, n, half(h)], op=ALU.mult,
-                )
-                for i, b in enumerate(bs):
-                    turn(bank[bk][:, blk(i)], m[t][:, n, blk(b)], False, b == bs[-1] and n == 1)
+        def gather_last(h, n):
+            nc.vector.tensor_tensor(
+                out=m[LAST][:, n, half(h)], in0=h_last[:].indirect(lists[n][:, entries(h)]),
+                in1=cpl[LAST][:, n, half(h)], op=ALU.mult,
+            )
 
         def close_sum(k):
             bk, t, bs = ROUND2[k]
@@ -248,16 +249,29 @@ def tile_picked_mfield_none_po_kernel(
         for t in (1, 2):
             couple(t)
             close_sum(t)
-        for h in range(2):
-            couple_last(h)
-            close_sum(LAST + h)
-        w2dw, w2ds = deal("w2d", w2w, w2s, ((nc.vector, slice(0, PACK)),))
+        bk, t, bs = ROUND2[LAST]
+        for n in range(2):
+            gather_last(0, n)
+            for i, b in enumerate(bs):
+                turn(bank[bk][:, blk(i)], m[t][:, n, blk(b)], False, b == bs[-1] and n == 1)
+        close_sum(LAST)
+        field = sb("field", [P, HALF], F32)
+        direct = sb("direct", [P, HALF], F32, tag="th2")
+        gather_last(1, 0)
+        gather_last(1, 1)
+        nc.vector.tensor_tensor(out=part[LAST][:, half(1)], in0=y[LAST][:, half(1)], in1=m[LAST][:, 0, half(1)], op=ALU.add)
+        nc.vector.tensor_tensor(out=field[:], in0=part[LAST][:, half(1)], in1=m[LAST][:, 1, half(1)], op=ALU.add)
+        nc.scalar.activation(direct[:], field[:], ACT.Tanh)
+        w2ds = deal_scales("w2ds", w2s, ((nc.vector, slice(0, PACK)),))
 
         def gain(b):
+            turned = PACK if b in ROUND2[LAST][2] else LAST
             nc.vector.tensor_tensor(
-                out=z16[b], in0=bank[Z_BANKS[b]][:].rearrange("p (t j) -> p j t", t=PACK),
-                in1=gn_t[:].unsqueeze(1).to_broadcast([P, JB, PACK]), op=ALU.mult,
+                out=z16[b][:, :, 0:turned], in0=bank[Z_BANKS[b]][:].rearrange("p (t j) -> p j t", t=PACK)[:, :, 0:turned],
+                in1=gn_t[:, 0:turned].unsqueeze(1).to_broadcast([P, JB, turned]), op=ALU.mult,
             )
+            if turned < PACK:
+                nc.vector.tensor_scalar(out=z16[b][:, :, LAST], in0=direct[:, blk(b % 2)], scalar1=gn_t[:, LAST:PACK], scalar2=None, op0=ALU.mult)
 
         def second_product(b):
             nc.vector.quantize_mx(out=zc[b][:].bitcast(FP8X4), scales=zs[b][:], in_=z16[b].rearrange("p j t -> p (j t)"))

@@ -107,9 +107,6 @@ def tile_picked_mfield_none_po_kernel(
         ident = sb("ident", [P, P], F32)
         make_identity(nc, ident[:])
 
-        warm = sb("warm", [P, 1], F32)
-        nc.scalar.activation(warm[:], ident[:, 0:1], ACT.Sigmoid)
-
         def deal_words(name, words, tag=None):
             dw = sb(name, [P, S], I32, tag=tag)
             nc.vector.tensor_copy(

@@ -17,7 +17,6 @@ P = 128
 T = 2048
 S = 512
 PACK = 4
-LAST = PACK - 1
 JB = 128
 NJB = S // JB
 HALF = S // 2
@@ -25,13 +24,16 @@ GROUP = 16
 QUADS = 4
 FLOPS = 2 * 2 * 512 * 512 * 512
 
-Y_BANKS = (1, 2, 6, 7, 0)
-TURNED = (0, 2)
-SUM_BANKS = (4, 5)
-BACK_BANKS = {0: (0, 3), 2: (1, 2)}
+LAST = 3
+ON_VECTOR = (0,)
+Y_BANKS = (4, 5, 6, 7, 3)
+SUM1_BANKS = {0: (0, 1), 2: (4, 5)}
+BACK1_BANKS = {0: (2, 3), 2: (6, 7)}
+SUM2 = ((0, [(0, 0), (0, 1), (1, 0), (1, 1)]), (1, [(2, 0), (2, 1), (3, 0), (3, 1)]), (2, [(0, 2), (0, 3), (1, 2), (1, 3)]), (3, [(2, 2), (2, 3)]))
+ADDED2 = ((3, 2), (3, 3))
 Z_BANKS = (4, 5, 6, 7)
-OUT_BANKS = (0, 3, 2, 1)
-ROUND2 = ((0, 0, (0, 1, 2, 3)), (3, 1, (0, 1, 2, 3)), (2, 2, (0, 1, 2, 3)), (1, LAST, (0, 1)))
+OUT_BANKS = (0, 1, 2, 3)
+ADDED1 = (1, 3)
 
 
 def tile_picked_mfield_none_po_kernel(
@@ -40,6 +42,7 @@ def tile_picked_mfield_none_po_kernel(
     nc = tc.nc
     with ExitStack() as ctx:
         keep = ctx.enter_context(tc.tile_pool(name="keep", bufs=1))
+        reused = ctx.enter_context(tc.tile_pool(name="reused", bufs=1))
         psum = ctx.enter_context(tc.psum_pool(name="psum", bufs=1))
 
         def sb(name, shape, dtype, tag=None):
@@ -56,91 +59,93 @@ def tile_picked_mfield_none_po_kernel(
         def blocks_of(h):
             return (2 * h, 2 * h + 1)
 
-        def entries(h):
-            return slice(h * HALF // GROUP, (h + 1) * HALF // GROUP)
+        def entries(js):
+            return slice(js.start // GROUP, js.stop // GROUP)
 
         def words_of(dram):
             return dram[0].rearrange("p n t -> p (n t)").bitcast(I32)
 
-        def scale_rows(tile, dram, q):
-            return tile[32 * q : 32 * q + 4, :].bitcast(I32), dram[0][4 * q : 4 * q + 4, :].bitcast(I32)
-
         def load_scales(tile, dram, q):
-            rows, source = scale_rows(tile, dram, q)
-            nc.sync.dma_start(out=rows, in_=source)
+            source = dram[0][4 * q : 4 * q + 4, :].bitcast(I32)
+            nc.sync.dma_start(
+                out=tile[32 * q : 32 * q + 32, :].bitcast(I32),
+                in_=source.unsqueeze(0).to_broadcast([32 // 4, 4, source.shape[1]]),
+            )
 
         xs = sb("xs", [P, T], U8)
         w1s = sb("w1s", [P, S], U8)
         w2s = sb("w2s", [P, S], U8)
-        for scales in (xs, w1s, w2s):
-            nc.gpsimd.memset(scales[:].bitcast(I32), 0)
-        xw = sb("xw", [P, T], U32)
+        xw = reused.tile([P, T], U32, name="xw", offset=0, align_bytes=64)
         w1w = sb("w1w", [P, S], I32)
         w2w = sb("w2w", [P, S], I32)
         offs_t = keep.tile([P, S // GROUP], U16, name="offs_t")
         p1_t = keep.tile([P, S // GROUP], U16, name="p1_t")
         p2_t = keep.tile([P, S // GROUP], U16, name="p2_t")
         lists = (p1_t, p2_t)
-        cpl = [sb("cpl%d" % t, [P, 2, S], F32) for t in range(PACK)]
+        window = {t: sb("y%d" % t, [P, 2 * S if t in ADDED1 else S], F32) for t in range(PACK)}
+        y = [window[t][:, 0:S] for t in range(PACK)]
+        pair = {t: sb("cpl%d" % t, [P, 2, S], F32) for t in range(1, PACK)}
+        cpl = {(t, n): pair[t][:, n, :] if t else window[ADDED1[n]][:, S : 2 * S] for t in range(PACK) for n in range(2)}
         gn_t = sb("gn_t", [P, PACK], F32)
         cj_v = [c.rearrange("(p t) j -> p t j", t=PACK) for c in (cj1, cj2)]
 
-        nc.sync.dma_start(offs_t[:], offs)
         for q in range(QUADS):
             load_scales(xs, x_scales, q)
-        nc.sync.dma_start(out=w1w[:], in_=words_of(w1_words))
-        load_scales(w1s, w1_scales, 0)
+        nc.sync.dma_start(offs_t[:], offs)
         nc.sync.dma_start(out=xw[:].bitcast(I32), in_=words_of(x_words))
-        for q in range(1, QUADS):
+        for q in range(QUADS):
             load_scales(w1s, w1_scales, q)
+        nc.sync.dma_start(out=w1w[:], in_=words_of(w1_words))
         nc.sync.dma_start(out=w2w[:], in_=words_of(w2_words))
-        for n, (tile, source) in enumerate(((p1_t, p1), (p2_t, p2))):
-            nc.sync.dma_start(tile[:], source)
-            nc.sync.dma_start(out=cpl[0][:, n, :], in_=cj_v[n][:, 0, :])
-        for t in range(1, PACK):
-            for n in range(2):
-                nc.sync.dma_start(out=cpl[t][:, n, :], in_=cj_v[n][:, t, :])
-        nc.sync.dma_start(out=gn_t[:], in_=gn.rearrange("(p t) o -> p (t o)", t=PACK))
         for q in range(QUADS):
             load_scales(w2s, w2_scales, q)
+        for n, (tile, source) in enumerate(((p1_t, p1), (p2_t, p2))):
+            nc.sync.dma_start(out=cpl[0, n], in_=cj_v[n][:, 0, :])
+            nc.sync.dma_start(tile[:], source)
+        for t in range(1, PACK):
+            for n in range(2):
+                nc.sync.dma_start(out=cpl[t, n], in_=cj_v[n][:, t, :])
+        nc.sync.dma_start(out=gn_t[:], in_=gn.rearrange("(p t) o -> p (t o)", t=PACK))
 
         ident = sb("ident", [P, P], F32)
         make_identity(nc, ident[:])
 
-        def deal_words(name, words, tag=None):
-            dw = sb(name, [P, S], I32, tag=tag)
+        def deal_words(dealt, words, ts):
             nc.vector.tensor_copy(
-                out=dw[:].rearrange("p (t c i) -> p c t i", t=PACK, i=4),
-                in_=words[:].rearrange("p (c i t) -> p c t i", t=PACK, i=4),
+                out=dealt[:].rearrange("p (t c i) -> p c t i", c=JB // 4, i=4),
+                in_=words[:].rearrange("p (c i t) -> p c t i", t=PACK, i=4)[:, :, ts, :],
             )
-            return dw
 
-        def deal_scales(name, scales, pieces, tag=None):
-            ds = sb(name, [P, S], U8, tag=tag)
-            for engine, ts in pieces:
-                engine.tensor_copy(
-                    out=ds[:].rearrange("p (t m) -> p t m", t=PACK)[:, ts, :],
-                    in_=scales[:].rearrange("p (m t) -> p t m", t=PACK)[:, ts, :],
-                )
-            return ds
+        def deal_scales(engine, dealt, scales, ts):
+            engine.tensor_copy(
+                out=dealt[:].rearrange("p (t m) -> p t m", m=JB),
+                in_=scales[:].rearrange("p (m t) -> p t m", t=PACK)[:, ts, :],
+            )
 
         xsg = sb("xsg", [P, S], U8)
         xg = sb("xg", [P, S], U32)
         nc.vector.tensor_copy(out=xsg[:], in_=xs[:].indirect(offs_t[:]))
-        w1dw = deal_words("w1dw", w1w)
-        w1ds = deal_scales("w1ds", w1s, ((nc.gpsimd, slice(0, 1)), (nc.vector, slice(1, PACK))))
         for h in range(2):
-            nc.vector.tensor_copy(out=xg[:, half(h)], in_=xw[:].indirect(offs_t[:, entries(h)]))
-        w2dw = deal_words("w2dw", w2w, tag="xw")
-
-        y = [sb("y%d" % t, [P, S], F32) for t in range(PACK)]
+            nc.vector.tensor_copy(out=xg[:, half(h)], in_=xw[:].indirect(offs_t[:, entries(half(h))]))
+        w1dw = [reused.tile([P, JB * k], I32, name="w1dw%d" % k, offset=at, align_bytes=64) for k, at in ((1, 0), (LAST, 4 * JB))]
+        w2dw = reused.tile([P, S], I32, name="w2dw", offset=8 * S, align_bytes=64)
+        w1ds = [sb("w1ds0", [P, JB], U8), sb("w1ds1", [P, LAST * JB], U8, tag="w1w")]
+        w2ds = sb("w2ds", [P, S], U8, tag="w1s")
+        first, rest, every = slice(0, 1), slice(1, PACK), slice(0, PACK)
+        deal_scales(nc.gpsimd, w1ds[0], w1s, first)
+        deal_words(w1dw[0], w1w, first)
+        deal_words(w1dw[1], w1w, rest)
+        deal_scales(nc.vector, w1ds[1], w1s, rest)
+        deal_words(w2dw, w2w, every)
+        deal_scales(nc.vector, w2ds, w2s, every)
 
         def first_product(t, dst, js):
+            k, ms = (0, blk(0)) if t == 0 else (1, blk(t - 1))
             nc.tensor.matmul_mx(
-                out=dst, lhsT=w1dw[:, blk(t)].bitcast(FP8X4), lhsT_scale=w1ds[:, blk(t)],
+                out=dst, lhsT=w1dw[k][:, ms].bitcast(FP8X4), lhsT_scale=w1ds[k][:, ms],
                 rhs=xg[:, js].bitcast(FP8X4), rhs_scale=xsg[:, js], start=True, stop=True,
             )
-            nc.scalar.activation(y[t][:, js], dst, ACT.Copy, scale=(1.0 if t == LAST else 0.5))
+            nc.scalar.activation(y[t][:, js], dst, ACT.Copy, scale=0.5)
 
         for h in range(2):
             first_product(0, bank[Y_BANKS[h]][:, 0:HALF], half(h))
@@ -150,149 +155,218 @@ def tile_picked_mfield_none_po_kernel(
         g = [[sb("g%d_%d" % (t, n), [P, S], F32) for n in range(2)] for t in range(PACK)]
         part = [sb("part%d" % t, [P, S], F32) for t in range(PACK)]
         a = [sb("a%d" % t, [P, S], F32) for t in range(PACK)]
-        sig = [sb("sig%d" % t, [P, 2, S], F32) for t in range(LAST)]
+        sig = {(t, h): sb("sig%d_%d" % (t, h), [P, 2, HALF], F32) for t in range(1, PACK) for h in range(2)}
         m = [sb("m%d" % t, [P, 2, S], F32) for t in range(PACK)]
-        th = [sb("th%d" % k, [P, S], F32) for k in range(len(ROUND2))]
-        z16_pair = [sb("z16_%d" % k, [P, HALF, PACK], BF16, tag="pair16_%d" % k) for k in range(2)]
-        z16 = [z16_pair[b // 2][:, blk(b % 2), :] for b in range(NJB)]
+        th = [sb("th%d" % t, [P, S], F32) for t in range(PACK)]
+        tt = [sb("tt%d" % k, [P, S], F32) for k in range(len(SUM2))]
+        z16 = [sb("z16_%d" % b, [P, JB, PACK], BF16) for b in range(NJB)]
         zc = [sb("zc%d" % b, [P, JB], U32) for b in range(NJB)]
         zs = [sb("zs%d" % b, [P, JB], U8) for b in range(NJB)]
         ot = [sb("ot%d" % b, [P, PACK, JB], F32) for b in range(NJB)]
+        o16_pair = [sb("o16_%d" % h, [P, HALF, PACK], BF16) for h in range(2)]
+        o16 = [o16_pair[b // 2][:, blk(b % 2), :] for b in range(NJB)]
         oc = sb("oc", [P, S], U32)
         osc = sb("osc", [P, S], U8)
-        h_last = sb("h_last", [P, S], F32)
         out_v = out_0.rearrange("(p t) j -> p t j", t=PACK)
         out_w = words_of(out_1)
 
         def turn(dst, src, start, stop):
             nc.tensor.matmul(out=dst, lhsT=src, rhs=ident[:], is_transpose=True, start=start, stop=stop)
 
-        def round1(t):
-            for h in range(2):
-                first, second = blocks_of(h)
-                for n in range(2):
-                    nc.vector.tensor_tensor(
-                        out=g[t][n][:, half(h)], in0=y[t][:].indirect(lists[n][:, entries(h)]),
-                        in1=cpl[t][:, n, half(h)], op=ALU.mult,
-                    )
-                    if t in TURNED:
-                        terms = (y[t], g[t][0]) if n == 0 else (g[t][1],)
-                        for term in terms:
-                            for b in (first, second):
-                                opens = term is y[t] and b == first
-                                turn(bank[SUM_BANKS[h]][:, blk(b)], term[:, blk(b)], opens, n == 1 and b == second)
-            if t in TURNED:
+        def gather1(t, js, n):
+            nc.vector.tensor_tensor(
+                out=g[t][n][:, js], in0=window[t][:].indirect(lists[n][:, entries(js)]), in1=cpl[t, n][:, js], op=ALU.mult
+            )
+
+        def round1_added(t):
+            for n in range(2):
+                gather1(t, slice(0, S), n)
+            add1(t)
+
+        def add1(t):
+            for o, lhs, rhs in ((part[t], y[t], g[t][0]), (a[t], part[t], g[t][1])):
                 for h in range(2):
-                    nc.scalar.copy(out=part[t][:, half(h)], in_=bank[SUM_BANKS[h]][:, half(h)])
-                    back = bank[BACK_BANKS[t][h]]
-                    for b in blocks_of(h):
-                        turn(back[:, blk(b)], part[t][:, blk(b)], True, True)
-                    nc.scalar.copy(out=a[t][:, half(h)], in_=back[:, half(h)])
+                    nc.vector.tensor_tensor(out=o[:, half(h)], in0=lhs[:, half(h)], in1=rhs[:, half(h)], op=ALU.add)
+
+        def tanh1(t, h):
+            nc.scalar.activation(a[t][:, half(h)], part[t][:, half(h)], ACT.Tanh)
+
+        def round1_turned(t):
+            for h in range(2):
+                bk = bank[SUM1_BANKS[t][h]]
+                for n in range(2):
+                    gather1(t, half(h), n)
+                    for i, b in enumerate(blocks_of(h)):
+                        turn(bk[:, blk(i)], g[t][n][:, blk(b)], False, n == 1 and i == 1)
+
+        def open1(t):
+            for h in range(2):
+                for i, b in enumerate(blocks_of(h)):
+                    turn(bank[SUM1_BANKS[t][h]][:, blk(i)], y[t][:, blk(b)], i == 0, False)
+
+        def out1(t, h):
+            src = bank[SUM1_BANKS[t][h]][:, 0:HALF]
+            if t in ON_VECTOR:
+                nc.scalar.activation(part[t][:, half(h)], src, ACT.Sigmoid, scale=4.0)
             else:
-                for dst, lhs, rhs in ((part[t], y[t], g[t][0]), (a[t], part[t], g[t][1])):
-                    for h in range(2):
-                        nc.vector.tensor_tensor(out=dst[:, half(h)], in0=lhs[:, half(h)], in1=rhs[:, half(h)], op=ALU.add)
+                nc.scalar.copy(out=part[t][:, half(h)], in_=src)
+            for i, b in enumerate(blocks_of(h)):
+                turn(bank[BACK1_BANKS[t][h]][:, blk(i)], part[t][:, blk(b)], True, True)
+
+        def back1(t, h):
+            src = bank[BACK1_BANKS[t][h]][:, 0:HALF]
+            nc.scalar.activation(a[t][:, half(h)], src, ACT.Copy, bias=(-0.5 if t in ON_VECTOR else 0.0))
 
         def sigmoids(t, h):
             for n in range(2):
-                nc.scalar.activation(sig[t][:, n, half(h)], a[t][:].indirect(lists[n][:, entries(h)]), ACT.Sigmoid, scale=4.0)
+                nc.scalar.activation(sig[t, h][:, n, :], a[t][:].indirect(lists[n][:, entries(half(h))]), ACT.Sigmoid, scale=4.0)
 
-        def open_sum(k):
-            bk, t, bs = ROUND2[k]
-            for i, b in enumerate(bs):
-                turn(bank[bk][:, blk(i)], y[t][:, blk(b)], i == 0, False)
+        added = [0] * len(SUM2)
 
-        def couple(t):
-            bk, bs = ROUND2[t][0], ROUND2[t][2]
-            for h in range(2):
+        def turn2(t, b, src):
+            k = [(t, b) in items for bk, items in SUM2].index(True)
+            bk, items = SUM2[k]
+            added[k] = added[k] + 1
+            turn(bank[bk][:, blk(items.index((t, b)))], src, added[k] == 1, added[k] == 3 * len(items))
+
+        def open2(k):
+            for t, b in SUM2[k][1]:
+                turn2(t, b, y[t][:, blk(b)])
+
+        def terms2(t, h):
+            if t in ON_VECTOR:
+                for n in range(2):
+                    nc.vector.tensor_tensor(
+                        out=m[t][:, n, half(h)], in0=a[t][:].indirect(lists[n][:, entries(half(h))]),
+                        in1=cpl[t, n][:, half(h)], op=ALU.mult,
+                    )
+            else:
                 nc.vector.scalar_tensor_tensor(
-                    out=m[t][:, :, half(h)], in0=sig[t][:, :, half(h)], scalar=-0.5, in1=cpl[t][:, :, half(h)],
+                    out=m[t][:, :, half(h)], in0=sig[t, h][:], scalar=-0.5, in1=pair[t][:, :, half(h)],
                     op0=ALU.add, op1=ALU.mult,
                 )
+            for n in range(2):
                 for b in blocks_of(h):
-                    for n in range(2):
-                        turn(bank[bk][:, blk(b)], m[t][:, n, blk(b)], False, b == bs[-1] and n == 1)
+                    if (t, b) not in ADDED2:
+                        turn2(t, b, m[t][:, n, blk(b)])
 
-        def gather_last(h, n):
-            nc.vector.tensor_tensor(
-                out=m[LAST][:, n, half(h)], in0=h_last[:].indirect(lists[n][:, entries(h)]),
-                in1=cpl[LAST][:, n, half(h)], op=ALU.mult,
-            )
+        def add2(k, js):
+            lhs = y[LAST] if k == 0 else part[LAST]
+            nc.vector.tensor_tensor(out=part[LAST][:, js], in0=lhs[:, js], in1=m[LAST][:, k, js], op=ALU.add)
 
-        def close_sum(k):
-            bk, t, bs = ROUND2[k]
-            js = slice(0, len(bs) * JB)
-            nc.scalar.activation(th[k][:, js], bank[bk][:, js], ACT.Tanh, scale=(1.0 if t == LAST else 2.0))
-            for i, b in enumerate(bs):
-                turn(bank[Z_BANKS[b]][:, blk(t)], th[k][:, blk(i)], True, True)
+        def tanh2(js):
+            nc.scalar.activation(th[LAST][:, js], part[LAST][:, js], ACT.Tanh, scale=2.0)
 
-        round1(0)
-        round1(1)
-        for h in range(2):
-            sigmoids(0, h)
-        round1(2)
-        open_sum(0)
-        open_sum(1)
-        for h in range(2):
-            sigmoids(1, h)
-        couple(0)
-        round1(LAST)
-        sigmoids(2, 0)
-        close_sum(0)
-        sigmoids(2, 1)
-        nc.scalar.activation(h_last[:], a[LAST][:], ACT.Tanh)
-        for k in range(2, len(ROUND2)):
-            open_sum(k)
-        for t in (1, 2):
-            couple(t)
-            close_sum(t)
-        bk, t, bs = ROUND2[LAST]
-        for n in range(2):
-            gather_last(0, n)
-            for i, b in enumerate(bs):
-                turn(bank[bk][:, blk(i)], m[t][:, n, blk(b)], False, b == bs[-1] and n == 1)
-        close_sum(LAST)
-        field = sb("field", [P, HALF], F32)
-        direct = sb("direct", [P, HALF], F32, tag="th2")
-        gather_last(1, 0)
-        gather_last(1, 1)
-        nc.vector.tensor_tensor(out=part[LAST][:, half(1)], in0=y[LAST][:, half(1)], in1=m[LAST][:, 0, half(1)], op=ALU.add)
-        nc.vector.tensor_tensor(out=field[:], in0=part[LAST][:, half(1)], in1=m[LAST][:, 1, half(1)], op=ALU.add)
-        nc.scalar.activation(direct[:], field[:], ACT.Tanh)
-        w2ds = deal_scales("w2ds", w2s, ((nc.vector, slice(0, PACK)),))
+        def gain_last(b):
+            nc.vector.tensor_scalar(out=z16[b][:, :, LAST], in0=th[LAST][:, blk(b)], scalar1=gn_t[:, LAST:PACK], scalar2=None, op0=ALU.mult)
+
+        def close2(k):
+            bk, items = SUM2[k]
+            js = slice(0, len(items) * JB)
+            nc.scalar.activation(tt[k][:, js], bank[bk][:, js], ACT.Tanh, scale=2.0)
+
+        def back2(k):
+            for i, (t, b) in enumerate(SUM2[k][1]):
+                turn(bank[Z_BANKS[b]][:, blk(t)], tt[k][:, blk(i)], True, True)
 
         def gain(b):
-            turned = PACK if b in ROUND2[LAST][2] else LAST
+            k = LAST if (LAST, b) in ADDED2 else PACK
             nc.vector.tensor_tensor(
-                out=z16[b][:, :, 0:turned], in0=bank[Z_BANKS[b]][:].rearrange("p (t j) -> p j t", t=PACK)[:, :, 0:turned],
-                in1=gn_t[:, 0:turned].unsqueeze(1).to_broadcast([P, JB, turned]), op=ALU.mult,
+                out=z16[b][:, :, 0:k], in0=bank[Z_BANKS[b]][:].rearrange("p (t j) -> p j t", t=PACK)[:, :, 0:k],
+                in1=gn_t[:, 0:k].unsqueeze(1).to_broadcast([P, JB, k]), op=ALU.mult,
             )
-            if turned < PACK:
-                nc.vector.tensor_scalar(out=z16[b][:, :, LAST], in0=direct[:, blk(b % 2)], scalar1=gn_t[:, LAST:PACK], scalar2=None, op0=ALU.mult)
+
+        def quantise(b):
+            nc.vector.quantize_mx(out=zc[b][:].bitcast(FP8X4), scales=zs[b][:], in_=z16[b][:].rearrange("p j t -> p (j t)"))
 
         def second_product(b):
-            nc.vector.quantize_mx(out=zc[b][:].bitcast(FP8X4), scales=zs[b][:], in_=z16[b].rearrange("p j t -> p (j t)"))
             for t in range(PACK):
                 nc.tensor.matmul_mx(
                     out=bank[OUT_BANKS[b]][:, blk(t)], lhsT=w2dw[:, blk(t)].bitcast(FP8X4), lhsT_scale=w2ds[:, blk(t)],
                     rhs=zc[b][:].bitcast(FP8X4), rhs_scale=zs[b][:], start=True, stop=True,
                 )
 
-        for h in range(2):
-            for b in blocks_of(h):
-                gain(b)
-            for b in blocks_of(h):
-                second_product(b)
-        for b in range(NJB):
+        def store(b):
             nc.scalar.copy(out=ot[b][:], in_=bank[OUT_BANKS[b]][:].rearrange("p (t j) -> p t j", t=PACK))
             nc.sync.dma_start(out=out_v[:, :, blk(b)], in_=ot[b][:])
 
-        for h, queue in enumerate((nc.sync, nc.scalar)):
-            o16 = sb("o16_%d" % h, [P, HALF, PACK], BF16, tag="pair16_%d" % (1 - h))
-            for i, b in enumerate(blocks_of(h)):
-                nc.vector.tensor_copy(out=o16[:, blk(i), :], in_=ot[b][:].rearrange("p t j -> p j t"))
-            nc.vector.quantize_mx(out=oc[:, half(h)].bitcast(FP8X4), scales=osc[:, half(h)], in_=o16[:].rearrange("p j t -> p (j t)"))
+        def rounded_s(b):
+            nc.scalar.copy(out=o16[b], in_=bank[OUT_BANKS[b]][:].rearrange("p (t j) -> p j t", t=PACK))
+
+        def rounded(b):
+            nc.vector.tensor_copy(out=o16[b], in_=ot[b][:].rearrange("p t j -> p j t"))
+
+        def planes(h, queue):
+            nc.vector.quantize_mx(out=oc[:, half(h)].bitcast(FP8X4), scales=osc[:, half(h)], in_=o16_pair[h][:].rearrange("p j t -> p (j t)"))
             queue.dma_start(out=out_w[:, half(h)], in_=oc[:, half(h)].bitcast(I32))
-        for q in range(QUADS):
-            rows, target = scale_rows(osc, out_2, q)
-            (nc.scalar if q < QUADS // 2 else nc.sync).dma_start(out=target, in_=rows)
+
+        def store_scales():
+            for q in range(QUADS):
+                (nc.scalar if q < QUADS // 2 else nc.sync).dma_start(
+                    out=out_2[0][4 * q : 4 * q + 4, :].bitcast(I32), in_=osc[32 * q : 32 * q + 4, :].bitcast(I32)
+                )
+
+        open1(0)
+        round1_turned(0)
+        out1(0, 0)
+        out1(0, 1)
+        back1(0, 0)
+        back1(0, 1)
+        open1(2)
+        round1_added(1)
+        round1_turned(2)
+        for k in range(len(SUM2)):
+            open2(k)
+        sigmoids(1, 0)
+        out1(2, 0)
+        out1(2, 1)
+        back1(2, 0)
+        back1(2, 1)
+        sigmoids(1, 1)
+        round1_added(3)
+        sigmoids(2, 0)
+        sigmoids(3, 0)
+        sigmoids(2, 1)
+        terms2(0, 0)
+        terms2(1, 0)
+        terms2(2, 0)
+        terms2(3, 0)
+        close2(0)
+        close2(1)
+        back2(0)
+        back2(1)
+        sigmoids(3, 1)
+        terms2(0, 1)
+        terms2(1, 1)
+        terms2(2, 1)
+        close2(2)
+        back2(2)
+        terms2(3, 1)
+        close2(3)
+        back2(3)
+        add2(0, half(1))
+        add2(1, half(1))
+        tanh2(half(1))
+        gain(0)
+        gain(1)
+        quantise(0)
+        second_product(0)
+        quantise(1)
+        second_product(1)
+        gain(2)
+        gain(3)
+        gain_last(2)
+        gain_last(3)
+        quantise(2)
+        second_product(2)
+        quantise(3)
+        second_product(3)
+        for b in range(NJB):
+            store(b)
+        rounded(0)
+        rounded(1)
+        rounded(2)
+        planes(0, nc.sync)
+        rounded(3)
+        planes(1, nc.scalar)
+        store_scales()

@@ -42,7 +42,6 @@ def tile_picked_mfield_none_po_kernel(
     nc = tc.nc
     with ExitStack() as ctx:
         keep = ctx.enter_context(tc.tile_pool(name="keep", bufs=1))
-        reused = ctx.enter_context(tc.tile_pool(name="reused", bufs=1))
         psum = ctx.enter_context(tc.psum_pool(name="psum", bufs=1))
 
         def sb(name, shape, dtype, tag=None):
@@ -66,16 +65,12 @@ def tile_picked_mfield_none_po_kernel(
             return dram[0].rearrange("p n t -> p (n t)").bitcast(I32)
 
         def load_scales(tile, dram, q):
-            source = dram[0][4 * q : 4 * q + 4, :].bitcast(I32)
-            nc.sync.dma_start(
-                out=tile[32 * q : 32 * q + 32, :].bitcast(I32),
-                in_=source.unsqueeze(0).to_broadcast([32 // 4, 4, source.shape[1]]),
-            )
+            nc.sync.dma_start(out=tile[32 * q : 32 * q + 4, :].bitcast(I32), in_=dram[0][4 * q : 4 * q + 4, :].bitcast(I32))
 
         xs = sb("xs", [P, T], U8)
         w1s = sb("w1s", [P, S], U8)
         w2s = sb("w2s", [P, S], U8)
-        xw = reused.tile([P, T], U32, name="xw", offset=0, align_bytes=64)
+        xw = sb("xw", [P, T], U32)
         w1w = sb("w1w", [P, S], I32)
         w2w = sb("w2w", [P, S], I32)
         offs_t = keep.tile([P, S // GROUP], U16, name="offs_t")
@@ -89,19 +84,22 @@ def tile_picked_mfield_none_po_kernel(
         gn_t = sb("gn_t", [P, PACK], F32)
         cj_v = [c.rearrange("(p t) j -> p t j", t=PACK) for c in (cj1, cj2)]
 
+        for scales in (xs, w1s, w2s):
+            nc.gpsimd.memset(scales[:].bitcast(I32), 0)
+        nc.sync.dma_start(offs_t[:], offs)
         for q in range(QUADS):
             load_scales(xs, x_scales, q)
-        nc.sync.dma_start(offs_t[:], offs)
-        nc.sync.dma_start(out=xw[:].bitcast(I32), in_=words_of(x_words))
-        for q in range(QUADS):
-            load_scales(w1s, w1_scales, q)
         nc.sync.dma_start(out=w1w[:], in_=words_of(w1_words))
+        load_scales(w1s, w1_scales, 0)
+        nc.sync.dma_start(out=xw[:].bitcast(I32), in_=words_of(x_words))
+        for q in range(1, QUADS):
+            load_scales(w1s, w1_scales, q)
         nc.sync.dma_start(out=w2w[:], in_=words_of(w2_words))
         for q in range(QUADS):
             load_scales(w2s, w2_scales, q)
         for n, (tile, source) in enumerate(((p1_t, p1), (p2_t, p2))):
-            nc.sync.dma_start(out=cpl[0, n], in_=cj_v[n][:, 0, :])
             nc.sync.dma_start(tile[:], source)
+            nc.sync.dma_start(out=cpl[0, n], in_=cj_v[n][:, 0, :])
         for t in range(1, PACK):
             for n in range(2):
                 nc.sync.dma_start(out=cpl[t, n], in_=cj_v[n][:, t, :])
@@ -125,24 +123,23 @@ def tile_picked_mfield_none_po_kernel(
         xsg = sb("xsg", [P, S], U8)
         xg = sb("xg", [P, S], U32)
         nc.vector.tensor_copy(out=xsg[:], in_=xs[:].indirect(offs_t[:]))
+        first, rest, every = slice(0, 1), slice(1, PACK), slice(0, PACK)
+        w1dw = sb("w1dw", [P, S], I32)
+        w1ds = [sb("w1ds0", [P, JB], U8), sb("w1ds1", [P, LAST * JB], U8)]
+        deal_words(w1dw, w1w, every)
+        deal_scales(nc.gpsimd, w1ds[0], w1s, first)
         for h in range(2):
             nc.vector.tensor_copy(out=xg[:, half(h)], in_=xw[:].indirect(offs_t[:, entries(half(h))]))
-        w1dw = [reused.tile([P, JB * k], I32, name="w1dw%d" % k, offset=at, align_bytes=64) for k, at in ((1, 0), (LAST, 4 * JB))]
-        w2dw = reused.tile([P, S], I32, name="w2dw", offset=8 * S, align_bytes=64)
-        w1ds = [sb("w1ds0", [P, JB], U8), sb("w1ds1", [P, LAST * JB], U8, tag="w1w")]
-        w2ds = sb("w2ds", [P, S], U8, tag="w1s")
-        first, rest, every = slice(0, 1), slice(1, PACK), slice(0, PACK)
-        deal_scales(nc.gpsimd, w1ds[0], w1s, first)
-        deal_words(w1dw[0], w1w, first)
-        deal_words(w1dw[1], w1w, rest)
         deal_scales(nc.vector, w1ds[1], w1s, rest)
+        w2dw = sb("w2dw", [P, S], I32, tag="xw")
+        w2ds = sb("w2ds", [P, S], U8, tag="w1s")
         deal_words(w2dw, w2w, every)
         deal_scales(nc.vector, w2ds, w2s, every)
 
         def first_product(t, dst, js):
             k, ms = (0, blk(0)) if t == 0 else (1, blk(t - 1))
             nc.tensor.matmul_mx(
-                out=dst, lhsT=w1dw[k][:, ms].bitcast(FP8X4), lhsT_scale=w1ds[k][:, ms],
+                out=dst, lhsT=w1dw[:, blk(t)].bitcast(FP8X4), lhsT_scale=w1ds[k][:, ms],
                 rhs=xg[:, js].bitcast(FP8X4), rhs_scale=xsg[:, js], start=True, stop=True,
             )
             nc.scalar.activation(y[t][:, js], dst, ACT.Copy, scale=0.5)

@@ -156,7 +156,8 @@ def tile_picked_mfield_none_po_kernel(
         m = [sb("m%d" % t, [P, 2, S], F32) for t in range(PACK)]
         th = [sb("th%d" % t, [P, S], F32) for t in range(PACK)]
         tt = [sb("tt%d" % k, [P, S], F32) for k in range(len(SUM2))]
-        z16 = [sb("z16_%d" % b, [P, JB, PACK], BF16) for b in range(NJB)]
+        z16_end = sb("z16_end", [P, HALF, PACK], BF16)
+        z16 = {b: z16_end[:, blk(b % 2), :] for b in blocks_of(1)}
         zc = [sb("zc%d" % b, [P, JB], U32) for b in range(NJB)]
         zs = [sb("zs%d" % b, [P, JB], U8) for b in range(NJB)]
         ot = [sb("ot%d" % b, [P, PACK, JB], F32) for b in range(NJB)]
@@ -247,15 +248,22 @@ def tile_picked_mfield_none_po_kernel(
                     if (t, b) not in ADDED2:
                         turn2(t, b, m[t][:, n, blk(b)])
 
+        end = [sb("end%d" % n, [P, HALF], F32) for n in range(2)]
+
+        def term_end(n):
+            nc.vector.scalar_tensor_tensor(
+                out=end[n][:], in0=sig[LAST, 1][:, n, :], scalar=-0.5, in1=cpl[LAST, n][:, half(1)], op0=ALU.add, op1=ALU.mult
+            )
+
         def add2(k, js):
             lhs = y[LAST] if k == 0 else part[LAST]
-            nc.vector.tensor_tensor(out=part[LAST][:, js], in0=lhs[:, js], in1=m[LAST][:, k, js], op=ALU.add)
+            nc.vector.tensor_tensor(out=part[LAST][:, js], in0=lhs[:, js], in1=end[k][:], op=ALU.add)
 
         def tanh2(js):
             nc.scalar.activation(th[LAST][:, js], part[LAST][:, js], ACT.Tanh, scale=2.0)
 
-        def gain_last(b):
-            nc.vector.tensor_scalar(out=z16[b][:, :, LAST], in0=th[LAST][:, blk(b)], scalar1=gn_t[:, LAST:PACK], scalar2=None, op0=ALU.mult)
+        def gain_last():
+            nc.vector.tensor_scalar(out=z16_end[:, :, LAST], in0=th[LAST][:, half(1)], scalar1=gn_t[:, LAST:PACK], scalar2=None, op0=ALU.mult)
 
         def close2(k):
             bk, items = SUM2[k]
@@ -274,7 +282,7 @@ def tile_picked_mfield_none_po_kernel(
             )
 
         def quantise(b):
-            nc.vector.quantize_mx(out=zc[b][:].bitcast(FP8X4), scales=zs[b][:], in_=z16[b][:].rearrange("p j t -> p (j t)"))
+            nc.vector.quantize_mx(out=zc[b][:].bitcast(FP8X4), scales=zs[b][:], in_=z16[b].rearrange("p j t -> p (j t)"))
 
         def second_product(b):
             for t in range(PACK):
@@ -335,32 +343,35 @@ def tile_picked_mfield_none_po_kernel(
         sigmoids(3, 1)
         terms2(0, 1)
         terms2(1, 1)
+        term_end(0)
         terms2(2, 1)
         close2(2)
         back2(2)
-        terms2(3, 1)
         close2(3)
         back2(3)
         add2(0, half(1))
+        term_end(1)
+        z16[0] = sb("z16_0", [P, JB, PACK], BF16, tag="end0")[:]
+        gain(0)
         add2(1, half(1))
         tanh2(half(1))
-        gain(0)
-        gain(1)
         quantise(0)
         second_product(0)
+        z16[1] = sb("z16_1", [P, JB, PACK], BF16, tag="end1")[:]
+        gain(1)
+        gain(2)
         quantise(1)
         second_product(1)
-        gain(2)
         gain(3)
-        gain_last(2)
-        gain_last(3)
+        gain_last()
+        store(0)
+        rounded(0)
         quantise(2)
         second_product(2)
         quantise(3)
         second_product(3)
-        for b in range(NJB):
+        for b in range(1, NJB):
             store(b)
-        rounded(0)
         rounded(1)
         rounded(2)
         planes(0, nc.sync)

@@ -64,8 +64,8 @@ def tile_picked_mfield_none_po_kernel(
         def words_of(dram):
             return dram[0].rearrange("p n t -> p (n t)").bitcast(I32)
 
-        def load_scales(tile, dram, q):
-            nc.sync.dma_start(out=tile[32 * q : 32 * q + 4, :].bitcast(I32), in_=dram[0][4 * q : 4 * q + 4, :].bitcast(I32))
+        def load_scales(tile, dram, q, queue=nc.sync):
+            queue.dma_start(out=tile[32 * q : 32 * q + 4, :].bitcast(I32), in_=dram[0][4 * q : 4 * q + 4, :].bitcast(I32))
 
         xs = sb("xs", [P, T], U8)
         w1s = sb("w1s", [P, S], U8)
@@ -84,12 +84,13 @@ def tile_picked_mfield_none_po_kernel(
         gn_t = sb("gn_t", [P, PACK], F32)
         cj_v = [c.rearrange("(p t) j -> p t j", t=PACK) for c in (cj1, cj2)]
 
-        for scales in (xs, w1s, w2s):
+        nc.vector.memset(xs[:].bitcast(I32), 0)
+        for scales in (w1s, w2s):
             nc.gpsimd.memset(scales[:].bitcast(I32), 0)
         nc.sync.dma_start(offs_t[:], offs)
-        for q in range(QUADS):
-            load_scales(xs, x_scales, q)
         nc.sync.dma_start(out=w1w[:], in_=words_of(w1_words))
+        for q in range(QUADS):
+            load_scales(xs, x_scales, q, nc.scalar if q % 2 else nc.sync)
         load_scales(w1s, w1_scales, 0)
         nc.sync.dma_start(out=xw[:].bitcast(I32), in_=words_of(x_words))
         for q in range(1, QUADS):

@@ -32,7 +32,7 @@ BACK1_BANKS = {0: (2, 3), 2: (6, 7)}
 SUM2 = ((0, [(0, 0), (0, 1), (1, 0), (1, 1)]), (1, [(2, 0), (2, 1), (3, 0), (3, 1)]), (2, [(0, 2), (0, 3), (1, 2), (1, 3)]), (3, [(2, 2), (2, 3)]))
 ADDED2 = ((3, 2), (3, 3))
 Z_BANKS = (4, 5, 6, 7)
-OUT_BANKS = (0, 1, 2, 3)
+OUT_BANKS = (0, 1, 2, 3, 4)
 ADDED1 = (1, 3)
 
 
@@ -157,13 +157,12 @@ def tile_picked_mfield_none_po_kernel(
         m = [sb("m%d" % t, [P, 2, S], F32) for t in range(PACK)]
         th = [sb("th%d" % t, [P, S], F32) for t in range(PACK)]
         tt = [sb("tt%d" % k, [P, S], F32) for k in range(len(SUM2))]
-        z16_end = sb("z16_end", [P, HALF, PACK], BF16)
-        z16 = {b: z16_end[:, blk(b % 2), :] for b in blocks_of(1)}
+        z16 = {b: sb("z16_%d" % b, [P, JB, PACK], BF16)[:] for b in blocks_of(1)}
         zc = [sb("zc%d" % b, [P, JB], U32) for b in range(NJB)]
         zs = [sb("zs%d" % b, [P, JB], U8) for b in range(NJB)]
         ot = [sb("ot%d" % b, [P, PACK, JB], F32) for b in range(NJB)]
-        o16_pair = [sb("o16_%d" % h, [P, HALF, PACK], BF16) for h in range(2)]
-        o16 = [o16_pair[b // 2][:, blk(b % 2), :] for b in range(NJB)]
+        o16_all = sb("o16", [P, S, PACK], BF16)
+        o16 = [o16_all[:, blk(b), :] for b in range(NJB)]
         oc = sb("oc", [P, S], U32)
         osc = sb("osc", [P, S], U8)
         out_v = out_0.rearrange("(p t) j -> p t j", t=PACK)
@@ -263,8 +262,8 @@ def tile_picked_mfield_none_po_kernel(
         def tanh2(js):
             nc.scalar.activation(th[LAST][:, js], part[LAST][:, js], ACT.Tanh, scale=2.0)
 
-        def gain_last():
-            nc.vector.tensor_scalar(out=z16_end[:, :, LAST], in0=th[LAST][:, half(1)], scalar1=gn_t[:, LAST:PACK], scalar2=None, op0=ALU.mult)
+        def gain_last(b):
+            nc.vector.tensor_scalar(out=z16[b][:, :, LAST], in0=th[LAST][:, blk(b)], scalar1=gn_t[:, LAST:PACK], scalar2=None, op0=ALU.mult)
 
         def close2(k):
             bk, items = SUM2[k]
@@ -285,15 +284,20 @@ def tile_picked_mfield_none_po_kernel(
         def quantise(b):
             nc.vector.quantize_mx(out=zc[b][:].bitcast(FP8X4), scales=zs[b][:], in_=z16[b].rearrange("p j t -> p (j t)"))
 
+        def out_bank(b, t):
+            return bank[OUT_BANKS[NJB if b == NJB - 1 and t >= 2 else b]]
+
         def second_product(b):
             for t in range(PACK):
                 nc.tensor.matmul_mx(
-                    out=bank[OUT_BANKS[b]][:, blk(t)], lhsT=w2dw[:, blk(t)].bitcast(FP8X4), lhsT_scale=w2ds[:, blk(t)],
+                    out=out_bank(b, t)[:, blk(t)], lhsT=w2dw[:, blk(t)].bitcast(FP8X4), lhsT_scale=w2ds[:, blk(t)],
                     rhs=zc[b][:].bitcast(FP8X4), rhs_scale=zs[b][:], start=True, stop=True,
                 )
 
         def store(b):
-            nc.scalar.copy(out=ot[b][:], in_=bank[OUT_BANKS[b]][:].rearrange("p (t j) -> p t j", t=PACK))
+            for ts in (slice(0, 2), slice(2, PACK)) if b == NJB - 1 else (slice(0, PACK),):
+                copy = nc.vector.tensor_copy if ts.start else nc.scalar.copy
+                copy(out=ot[b][:, ts, :], in_=out_bank(b, ts.start)[:].rearrange("p (t j) -> p t j", t=PACK)[:, ts, :])
             nc.sync.dma_start(out=out_v[:, :, blk(b)], in_=ot[b][:])
 
         def rounded_s(b):
@@ -302,9 +306,11 @@ def tile_picked_mfield_none_po_kernel(
         def rounded(b):
             nc.vector.tensor_copy(out=o16[b], in_=ot[b][:].rearrange("p t j -> p j t"))
 
-        def planes(h, queue):
-            nc.vector.quantize_mx(out=oc[:, half(h)].bitcast(FP8X4), scales=osc[:, half(h)], in_=o16_pair[h][:].rearrange("p j t -> p (j t)"))
-            queue.dma_start(out=out_w[:, half(h)], in_=oc[:, half(h)].bitcast(I32))
+        def planes(js, queue=None, stored=None):
+            source = o16_all[:, js, :]
+            nc.vector.quantize_mx(out=oc[:, js].bitcast(FP8X4), scales=osc[:, js], in_=source.rearrange("p j t -> p (j t)"))
+            if queue is not None:
+                queue.dma_start(out=out_w[:, stored], in_=oc[:, stored].bitcast(I32))
 
         def store_scales():
             for q in range(QUADS):
@@ -363,19 +369,22 @@ def tile_picked_mfield_none_po_kernel(
         gain(2)
         quantise(1)
         second_product(1)
+        gain_last(2)
         gain(3)
-        gain_last()
-        store(0)
-        rounded(0)
         quantise(2)
         second_product(2)
+        gain_last(3)
+        store(0)
+        rounded(0)
         quantise(3)
         second_product(3)
-        for b in range(1, NJB):
-            store(b)
+        store(1)
+        store(2)
         rounded(1)
+        planes(half(0))
+        store(3)
         rounded(2)
-        planes(0, nc.sync)
+        planes(blk(2), nc.sync, slice(0, LAST * JB))
         rounded(3)
-        planes(1, nc.scalar)
+        planes(blk(3), nc.scalar, blk(3))
         store_scales()

@@ -23,17 +23,15 @@ HALF = S // 2
 GROUP = 16
 QUADS = 4
 FLOPS = 2 * 2 * 512 * 512 * 512
+LAST = PACK - 1
 
-LAST = 3
-ON_VECTOR = (0,)
-Y_BANKS = (4, 5, 6, 7, 3)
-SUM1_BANKS = {0: (0, 1), 2: (4, 5)}
-BACK1_BANKS = {0: (2, 3), 2: (6, 7)}
-SUM2 = ((0, [(0, 0), (0, 1), (1, 0), (1, 1)]), (1, [(2, 0), (2, 1), (3, 0), (3, 1)]), (2, [(0, 2), (0, 3), (1, 2), (1, 3)]), (3, [(2, 2), (2, 3)]))
+Y_BANKS = (0, 1, 2, 3, 0)
+SUM1 = {0: 4, 1: 5}
+BACK1 = {0: 6, 1: 7}
 ADDED2 = ((3, 2), (3, 3))
-Z_BANKS = (4, 5, 6, 7)
-OUT_BANKS = (0, 1, 2, 3, 4)
-ADDED1 = (1, 3)
+SUM2 = tuple((4 + b, [(t, b) for t in range(PACK) if (t, b) not in ADDED2]) for b in range(NJB))
+Z_BANKS = (0, 1, 2, 3)
+OUT_BANKS = (4, 5, 6, 7, 0)
 
 
 def tile_picked_mfield_none_po_kernel(
@@ -55,8 +53,10 @@ def tile_picked_mfield_none_po_kernel(
         def half(h):
             return slice(h * HALF, (h + 1) * HALF)
 
-        def blocks_of(h):
-            return (2 * h, 2 * h + 1)
+        whole = slice(0, S)
+
+        def blocks_in(js):
+            return range(js.start // JB, js.stop // JB)
 
         def entries(js):
             return slice(js.start // GROUP, js.stop // GROUP)
@@ -77,10 +77,9 @@ def tile_picked_mfield_none_po_kernel(
         p1_t = keep.tile([P, S // GROUP], U16, name="p1_t")
         p2_t = keep.tile([P, S // GROUP], U16, name="p2_t")
         lists = (p1_t, p2_t)
-        window = {t: sb("y%d" % t, [P, 2 * S if t in ADDED1 else S], F32) for t in range(PACK)}
-        y = [window[t][:, 0:S] for t in range(PACK)]
-        pair = {t: sb("cpl%d" % t, [P, 2, S], F32) for t in range(1, PACK)}
-        cpl = {(t, n): pair[t][:, n, :] if t else window[ADDED1[n]][:, S : 2 * S] for t in range(PACK) for n in range(2)}
+        ywin = [sb("y%d" % t, [P, S], F32) for t in range(PACK)]
+        y = [ywin[t][:, 0:S] for t in range(PACK)]
+        c1, c2 = [[sb("c%d_%d" % (n, t), [P, S], F32)[:] for t in range(PACK)] for n in range(2)]
         gn_t = sb("gn_t", [P, PACK], F32)
         cj_v = [c.rearrange("(p t) j -> p t j", t=PACK) for c in (cj1, cj2)]
 
@@ -98,12 +97,11 @@ def tile_picked_mfield_none_po_kernel(
         nc.sync.dma_start(out=w2w[:], in_=words_of(w2_words))
         for q in range(QUADS):
             load_scales(w2s, w2_scales, q)
-        for n, (tile, source) in enumerate(((p1_t, p1), (p2_t, p2))):
-            nc.sync.dma_start(tile[:], source)
-            nc.sync.dma_start(out=cpl[0, n], in_=cj_v[n][:, 0, :])
-        for t in range(1, PACK):
-            for n in range(2):
-                nc.sync.dma_start(out=cpl[t, n], in_=cj_v[n][:, t, :])
+        nc.sync.dma_start(p2_t[:], p2)
+        nc.sync.dma_start(p1_t[:], p1)
+        for t in range(PACK):
+            for c, v in ((c1, cj_v[0]), (c2, cj_v[1])):
+                nc.sync.dma_start(out=c[t], in_=v[:, t, :])
         nc.sync.dma_start(out=gn_t[:], in_=gn.rearrange("(p t) o -> p (t o)", t=PACK))
 
         ident = sb("ident", [P, P], F32)
@@ -137,149 +135,119 @@ def tile_picked_mfield_none_po_kernel(
         deal_words(w2dw, w2w, every)
         deal_scales(nc.vector, w2ds, w2s, every)
 
-        def first_product(t, dst, js):
+        def y_bank(t, js):
+            return bank[Y_BANKS[t + 1]][:] if t else bank[Y_BANKS[js.start // HALF]][:, 0:HALF]
+
+        def first_product(t, js):
             k, ms = (0, blk(0)) if t == 0 else (1, blk(t - 1))
             nc.tensor.matmul_mx(
-                out=dst, lhsT=w1dw[:, blk(t)].bitcast(FP8X4), lhsT_scale=w1ds[k][:, ms],
+                out=y_bank(t, js), lhsT=w1dw[:, blk(t)].bitcast(FP8X4), lhsT_scale=w1ds[k][:, ms],
                 rhs=xg[:, js].bitcast(FP8X4), rhs_scale=xsg[:, js], start=True, stop=True,
             )
-            nc.scalar.activation(y[t][:, js], dst, ACT.Copy, scale=0.5)
 
-        for h in range(2):
-            first_product(0, bank[Y_BANKS[h]][:, 0:HALF], half(h))
-        for t in range(1, PACK):
-            first_product(t, bank[Y_BANKS[t + 1]][:], slice(0, S))
+        def field(t, js):
+            nc.scalar.activation(y[t][:, js], y_bank(t, js), ACT.Copy)
 
-        g = [[sb("g%d_%d" % (t, n), [P, S], F32) for n in range(2)] for t in range(PACK)]
-        part = [sb("part%d" % t, [P, S], F32) for t in range(PACK)]
-        a = [sb("a%d" % t, [P, S], F32) for t in range(PACK)]
-        sig = {(t, h): sb("sig%d_%d" % (t, h), [P, 2, HALF], F32) for t in range(1, PACK) for h in range(2)}
-        m = [sb("m%d" % t, [P, 2, S], F32) for t in range(PACK)]
-        th = [sb("th%d" % t, [P, S], F32) for t in range(PACK)]
+        hwin = [sb("h%d" % t, [P, S], F32) for t in range(PACK)]
+        hh = [hwin[t][:, 0:S] for t in range(PACK)]
+        win = (ywin, hwin)
+        m1 = [[sb("m1_%d" % t, [P, S], F32)[:] for t in range(PACK)]]
+        g2 = [[sb("g2_%d" % t, [P, S], F32)[:] for t in range(PACK)]]
+        m2 = [[sb("m2_%d" % t, [P, S], F32)[:] for t in range(PACK)]]
+        part = [sb("part%d" % t, [P, S], F32)[:] for t in range(PACK)]
+        g1 = [sb("g1_%d" % t, [P, S], F32)[:] for t in range(PACK)]
+        g1[LAST], g2[0][LAST] = m2[0][0], m2[0][1]
+        ring = {(0, i): g1[LAST][:, half(i)] for i in range(2)}
+        ring[1, 0], ring[1, 1], ring[1, 2] = g2[0][LAST][:, half(0)], g2[0][LAST][:, half(1)], sb("ring", [P, HALF], F32)[:]
+
+        def buf(n, r, t, js):
+            if r == 0:
+                return (m1, g2, m2)[n][0][t][:, js]
+            h = js.start // HALF
+            return ring[min(n, 1), (PACK * h + t) % (3 if n else 2)][:, js.start - h * HALF : js.stop - h * HALF]
+
         tt = [sb("tt%d" % k, [P, S], F32) for k in range(len(SUM2))]
-        z16 = {b: sb("z16_%d" % b, [P, JB, PACK], BF16)[:] for b in blocks_of(1)}
+        z16 = [sb("z16_%d" % b, [P, JB, PACK], BF16)[:] for b in range(NJB)]
         zc = [sb("zc%d" % b, [P, JB], U32) for b in range(NJB)]
         zs = [sb("zs%d" % b, [P, JB], U8) for b in range(NJB)]
         ot = [sb("ot%d" % b, [P, PACK, JB], F32) for b in range(NJB)]
-        o16_all = sb("o16", [P, S, PACK], BF16)
-        o16 = [o16_all[:, blk(b), :] for b in range(NJB)]
+        o16 = sb("o16", [P, S, PACK], BF16)
         oc = sb("oc", [P, S], U32)
         osc = sb("osc", [P, S], U8)
         out_v = out_0.rearrange("(p t) j -> p t j", t=PACK)
         out_w = words_of(out_1)
 
+        groups = {(0, t): (SUM1[t], [(t, b) for b in range(NJB)]) for t in SUM1}
+        for k, (bk, items) in enumerate(SUM2):
+            groups[1, k] = (bk, items)
+        count = {key: 0 for key in groups}
+
         def turn(dst, src, start, stop):
             nc.tensor.matmul(out=dst, lhsT=src, rhs=ident[:], is_transpose=True, start=start, stop=stop)
 
-        def gather1(t, js, n):
-            nc.vector.tensor_tensor(
-                out=g[t][n][:, js], in0=window[t][:].indirect(lists[n][:, entries(js)]), in1=cpl[t, n][:, js], op=ALU.mult
-            )
+        def add_turned(r, t, src, js):
+            for b in blocks_in(js):
+                for key in groups:
+                    bk, items = groups[key]
+                    if key[0] == r and (t, b) in items:
+                        count[key] = count[key] + 1
+                        turn(bank[bk][:, blk(items.index((t, b)))], src[:, blk(b - js.start // JB)], count[key] == 1, count[key] == 3 * len(items))
 
-        def round1_added(t):
-            for n in range(2):
-                gather1(t, slice(0, S), n)
-            add1(t)
+        def fused(n, r, t, js):
+            o = buf(2 * n, r, t, js)
+            nc.vector.tensor_tensor(out=o, in0=win[r][t][:].indirect(lists[n][:, entries(js)]), in1=(c1, c2)[n][t][:, js], op=ALU.mult)
+            add_turned(r, t, o, js)
 
-        def add1(t):
-            for o, lhs, rhs in ((part[t], y[t], g[t][0]), (a[t], part[t], g[t][1])):
-                for h in range(2):
-                    nc.vector.tensor_tensor(out=o[:, half(h)], in0=lhs[:, half(h)], in1=rhs[:, half(h)], op=ALU.add)
+        def fetch(n, r, t, js):
+            o = buf(1, r, t, js) if n else g1[t][:, js]
+            nc.scalar.activation(o, win[r][t][:].indirect(lists[n][:, entries(js)]), ACT.Copy)
 
-        def tanh1(t, h):
-            nc.scalar.activation(a[t][:, half(h)], part[t][:, half(h)], ACT.Tanh)
+        def term(n, r, t, js):
+            o = buf(2 * n, r, t, js)
+            nc.vector.tensor_tensor(out=o, in0=buf(1, r, t, js) if n else g1[t][:, js], in1=(c1, c2)[n][t][:, js], op=ALU.mult)
+            add_turned(r, t, o, js)
 
-        def round1_turned(t):
-            for h in range(2):
-                bk = bank[SUM1_BANKS[t][h]]
-                for n in range(2):
-                    gather1(t, half(h), n)
-                    for i, b in enumerate(blocks_of(h)):
-                        turn(bk[:, blk(i)], g[t][n][:, blk(b)], False, n == 1 and i == 1)
+        def add(o, a, b):
+            nc.vector.tensor_tensor(out=o, in0=a, in1=b, op=ALU.add)
 
-        def open1(t):
-            for h in range(2):
-                for i, b in enumerate(blocks_of(h)):
-                    turn(bank[SUM1_BANKS[t][h]][:, blk(i)], y[t][:, blk(b)], i == 0, False)
+        def tanh1(t):
+            nc.scalar.activation(hh[t], part[t], ACT.Tanh)
 
-        def out1(t, h):
-            src = bank[SUM1_BANKS[t][h]][:, 0:HALF]
-            if t in ON_VECTOR:
-                nc.scalar.activation(part[t][:, half(h)], src, ACT.Sigmoid, scale=4.0)
-            else:
-                nc.scalar.copy(out=part[t][:, half(h)], in_=src)
-            for i, b in enumerate(blocks_of(h)):
-                turn(bank[BACK1_BANKS[t][h]][:, blk(i)], part[t][:, blk(b)], True, True)
+        def tanh1_turned(t):
+            nc.scalar.activation(part[t], bank[SUM1[t]][:], ACT.Tanh)
+            for b in range(NJB):
+                turn(bank[BACK1[t]][:, blk(b)], part[t][:, blk(b)], True, True)
 
-        def back1(t, h):
-            src = bank[BACK1_BANKS[t][h]][:, 0:HALF]
-            nc.scalar.activation(a[t][:, half(h)], src, ACT.Copy, bias=(-0.5 if t in ON_VECTOR else 0.0))
+        def back1(t):
+            nc.scalar.activation(hh[t], bank[BACK1[t]][:], ACT.Copy)
 
-        def sigmoids(t, h):
-            for n in range(2):
-                nc.scalar.activation(sig[t, h][:, n, :], a[t][:].indirect(lists[n][:, entries(half(h))]), ACT.Sigmoid, scale=4.0)
-
-        added = [0] * len(SUM2)
-
-        def turn2(t, b, src):
-            k = [(t, b) in items for bk, items in SUM2].index(True)
-            bk, items = SUM2[k]
-            added[k] = added[k] + 1
-            turn(bank[bk][:, blk(items.index((t, b)))], src, added[k] == 1, added[k] == 3 * len(items))
-
-        def open2(k):
-            for t, b in SUM2[k][1]:
-                turn2(t, b, y[t][:, blk(b)])
-
-        def terms2(t, h):
-            if t in ON_VECTOR:
-                for n in range(2):
-                    nc.vector.tensor_tensor(
-                        out=m[t][:, n, half(h)], in0=a[t][:].indirect(lists[n][:, entries(half(h))]),
-                        in1=cpl[t, n][:, half(h)], op=ALU.mult,
-                    )
-            else:
-                nc.vector.scalar_tensor_tensor(
-                    out=m[t][:, :, half(h)], in0=sig[t, h][:], scalar=-0.5, in1=pair[t][:, :, half(h)],
-                    op0=ALU.add, op1=ALU.mult,
-                )
-            for n in range(2):
-                for b in blocks_of(h):
-                    if (t, b) not in ADDED2:
-                        turn2(t, b, m[t][:, n, blk(b)])
-
-        end = [sb("end%d" % n, [P, HALF], F32) for n in range(2)]
-
-        def term_end(n):
-            nc.vector.scalar_tensor_tensor(
-                out=end[n][:], in0=sig[LAST, 1][:, n, :], scalar=-0.5, in1=cpl[LAST, n][:, half(1)], op0=ALU.add, op1=ALU.mult
-            )
-
-        def add2(k, js):
-            lhs = y[LAST] if k == 0 else part[LAST]
-            nc.vector.tensor_tensor(out=part[LAST][:, js], in0=lhs[:, js], in1=end[k][:], op=ALU.add)
-
-        def tanh2(js):
-            nc.scalar.activation(th[LAST][:, js], part[LAST][:, js], ACT.Tanh, scale=2.0)
-
-        def gain_last(b):
-            nc.vector.tensor_scalar(out=z16[b][:, :, LAST], in0=th[LAST][:, blk(b)], scalar1=gn_t[:, LAST:PACK], scalar2=None, op0=ALU.mult)
-
-        def close2(k):
+        def tanh2(k):
             bk, items = SUM2[k]
             js = slice(0, len(items) * JB)
-            nc.scalar.activation(tt[k][:, js], bank[bk][:, js], ACT.Tanh, scale=2.0)
-
-        def back2(k):
-            for i, (t, b) in enumerate(SUM2[k][1]):
+            nc.scalar.activation(tt[k][:, js], bank[bk][:, js], ACT.Tanh)
+            for i, (t, b) in enumerate(items):
                 turn(bank[Z_BANKS[b]][:, blk(t)], tt[k][:, blk(i)], True, True)
 
         def gain(b):
-            k = LAST if (LAST, b) in ADDED2 else PACK
+            k = len(SUM2[b][1])
             nc.vector.tensor_tensor(
                 out=z16[b][:, :, 0:k], in0=bank[Z_BANKS[b]][:].rearrange("p (t j) -> p j t", t=PACK)[:, :, 0:k],
                 in1=gn_t[:, 0:k].unsqueeze(1).to_broadcast([P, JB, k]), op=ALU.mult,
             )
+
+        end = sb("end", [P, S], F32)[:]
+
+        def add_end(k, js):
+            add(end[:, js], (y[LAST], end)[k][:, js], buf(2 * k, 1, LAST, js))
+
+        def tanh_end(js):
+            nc.scalar.activation(part[LAST][:, js], end[:, js], ACT.Tanh)
+
+        def gain_end(b):
+            nc.vector.tensor_scalar(out=z16[b][:, :, LAST], in0=part[LAST][:, blk(b)], scalar1=gn_t[:, LAST:PACK], scalar2=None, op0=ALU.mult)
+
+        def rounded_s(b):
+            nc.scalar.copy(out=o16[:, blk(b), :], in_=bank[OUT_BANKS[b]][:].rearrange("p (t j) -> p j t", t=PACK))
 
         def quantise(b):
             nc.vector.quantize_mx(out=zc[b][:].bitcast(FP8X4), scales=zs[b][:], in_=z16[b].rearrange("p j t -> p (j t)"))
@@ -300,15 +268,11 @@ def tile_picked_mfield_none_po_kernel(
                 copy(out=ot[b][:, ts, :], in_=out_bank(b, ts.start)[:].rearrange("p (t j) -> p t j", t=PACK)[:, ts, :])
             nc.sync.dma_start(out=out_v[:, :, blk(b)], in_=ot[b][:])
 
-        def rounded_s(b):
-            nc.scalar.copy(out=o16[b], in_=bank[OUT_BANKS[b]][:].rearrange("p (t j) -> p j t", t=PACK))
-
         def rounded(b):
-            nc.vector.tensor_copy(out=o16[b], in_=ot[b][:].rearrange("p t j -> p j t"))
+            nc.vector.tensor_copy(out=o16[:, blk(b), :], in_=ot[b][:].rearrange("p t j -> p j t"))
 
         def planes(js, queue=None, stored=None):
-            source = o16_all[:, js, :]
-            nc.vector.quantize_mx(out=oc[:, js].bitcast(FP8X4), scales=osc[:, js], in_=source.rearrange("p j t -> p (j t)"))
+            nc.vector.quantize_mx(out=oc[:, js].bitcast(FP8X4), scales=osc[:, js], in_=o16[:, js, :].rearrange("p j t -> p (j t)"))
             if queue is not None:
                 queue.dma_start(out=out_w[:, stored], in_=oc[:, stored].bitcast(I32))
 
@@ -318,69 +282,96 @@ def tile_picked_mfield_none_po_kernel(
                     out=out_2[0][4 * q : 4 * q + 4, :].bitcast(I32), in_=osc[32 * q : 32 * q + 4, :].bitcast(I32)
                 )
 
-        open1(0)
-        round1_turned(0)
-        out1(0, 0)
-        out1(0, 1)
-        back1(0, 0)
-        back1(0, 1)
-        open1(2)
-        round1_added(1)
-        round1_turned(2)
-        for k in range(len(SUM2)):
-            open2(k)
-        sigmoids(1, 0)
-        out1(2, 0)
-        out1(2, 1)
-        back1(2, 0)
-        back1(2, 1)
-        sigmoids(1, 1)
-        round1_added(3)
-        sigmoids(2, 0)
-        sigmoids(3, 0)
-        sigmoids(2, 1)
-        terms2(0, 0)
-        terms2(1, 0)
-        terms2(2, 0)
-        terms2(3, 0)
-        close2(0)
-        close2(1)
-        back2(0)
-        back2(1)
-        sigmoids(3, 1)
-        terms2(0, 1)
-        terms2(1, 1)
-        term_end(0)
-        terms2(2, 1)
-        close2(2)
-        back2(2)
-        close2(3)
-        back2(3)
-        add2(0, half(1))
-        term_end(1)
-        z16[0] = sb("z16_0", [P, JB, PACK], BF16, tag="end0")[:]
+        for h in range(2):
+            first_product(0, half(h))
+            field(0, half(h))
+        for t in range(1, PACK):
+            first_product(t, whole)
+            field(t, whole)
+        add_turned(0, 0, y[0], whole)
+        add_turned(0, 1, y[1], whole)
+        for h in range(2):
+            fused(0, 0, 0, half(h))
+        for h in range(2):
+            fused(1, 0, 0, half(h))
+        for h in range(2):
+            fetch(1, 0, 1, half(h))
+        for h in range(2):
+            fused(0, 0, 1, half(h))
+        for h in range(2):
+            fetch(1, 0, 2, half(h))
+        tanh1_turned(0)
+        term(1, 0, 1, whole)
+        for h in range(2):
+            fetch(0, 0, 3, half(h))
+        for h in range(2):
+            fused(0, 0, 2, half(h))
+        tanh1_turned(1)
+        back1(0)
+        term(1, 0, 2, whole)
+        add(part[2], y[2], m1[0][2])
+        for h in range(2):
+            fetch(1, 0, 3, half(h))
+        term(0, 0, 3, whole)
+        add(part[2], part[2], m2[0][2])
+        back1(1)
+        add(part[3], y[3], m1[0][3])
+        tanh1(2)
+        term(1, 0, 3, whole)
+        for t in range(PACK):
+            add_turned(1, t, y[t], whole)
+        fused(0, 1, 0, half(0))
+        fetch(1, 1, 0, half(0))
+        add(part[3], part[3], m2[0][3])
+        fetch(1, 1, 1, half(0))
+        fused(0, 1, 1, half(0))
+        tanh1(3)
+        term(1, 1, 0, half(0))
+        fetch(1, 1, 2, half(0))
+        fused(0, 1, 2, half(0))
+        term(1, 1, 1, half(0))
+        fetch(1, 1, 3, half(0))
+        fused(0, 1, 3, half(0))
+        term(1, 1, 2, half(0))
+        fetch(1, 1, 0, half(1))
+        fused(0, 1, 0, half(1))
+        term(1, 1, 3, half(0))
+        fetch(1, 1, 1, half(1))
+        fused(0, 1, 1, half(1))
+        tanh2(0)
+        term(1, 1, 0, half(1))
+        fetch(1, 1, 2, half(1))
+        fused(0, 1, 2, half(1))
+        tanh2(1)
+        term(1, 1, 1, half(1))
+        fetch(1, 1, 3, half(1))
+        term(1, 1, 2, half(1))
+        fused(0, 1, 3, half(1))
         gain(0)
-        add2(1, half(1))
-        tanh2(half(1))
+        add_end(0, half(1))
+        term(1, 1, 3, half(1))
+        tanh2(2)
         quantise(0)
         second_product(0)
-        z16[1] = sb("z16_1", [P, JB, PACK], BF16, tag="end1")[:]
+        add_end(1, half(1))
+        tanh2(3)
         gain(1)
+        tanh_end(half(1))
         gain(2)
         quantise(1)
         second_product(1)
-        gain_last(2)
+        gain_end(2)
         gain(3)
         quantise(2)
         second_product(2)
-        gain_last(3)
+        gain_end(3)
         store(0)
-        rounded(0)
+        rounded_s(0)
         quantise(3)
         second_product(3)
         store(1)
-        store(2)
         rounded(1)
+        store(2)
         planes(half(0))
         store(3)
         rounded(2)

@@ -72,14 +72,15 @@ def tile_picked_mfield_none_po_kernel(
         w2s = sb("w2s", [P, S], U8)
         xw = sb("xw", [P, T], U32)
         w1w = sb("w1w", [P, S], I32)
-        w2w = sb("w2w", [P, S], I32)
+        w2w = sb("w2w", [P, S], U32)
         offs_t = keep.tile([P, S // GROUP], U16, name="offs_t")
         p1_t = keep.tile([P, S // GROUP], U16, name="p1_t")
         p2_t = keep.tile([P, S // GROUP], U16, name="p2_t")
         lists = (p1_t, p2_t)
-        ywin = [sb("y%d" % t, [P, S], F32) for t in range(PACK)]
+        ywin = [sb("y%d" % t, [P, 2 * S if t else S], F32) for t in range(PACK)]
         y = [ywin[t][:, 0:S] for t in range(PACK)]
-        c1, c2 = [[sb("c%d_%d" % (n, t), [P, S], F32)[:] for t in range(PACK)] for n in range(2)]
+        spare = {(0, 0): 1, (1, 0): 2, (0, 1): 3}
+        c1, c2 = [[ywin[spare[n, t]][:, S : 2 * S] if (n, t) in spare else sb("c%d_%d" % (n, t), [P, S], F32)[:] for t in range(PACK)] for n in range(2)]
         gn_t = sb("gn_t", [P, PACK], F32)
         cj_v = [c.rearrange("(p t) j -> p t j", t=PACK) for c in (cj1, cj2)]
 
@@ -94,21 +95,21 @@ def tile_picked_mfield_none_po_kernel(
         nc.sync.dma_start(out=xw[:].bitcast(I32), in_=words_of(x_words))
         for q in range(1, QUADS):
             load_scales(w1s, w1_scales, q)
-        nc.sync.dma_start(out=w2w[:], in_=words_of(w2_words))
+        nc.sync.dma_start(out=w2w[:].bitcast(I32), in_=words_of(w2_words))
         for q in range(QUADS):
             load_scales(w2s, w2_scales, q)
-        nc.sync.dma_start(p2_t[:], p2)
-        nc.sync.dma_start(p1_t[:], p1)
         for t in range(PACK):
-            for c, v in ((c1, cj_v[0]), (c2, cj_v[1])):
+            for tile, source, c, v in ((p1_t, p1, c1, cj_v[0]), (p2_t, p2, c2, cj_v[1])):
+                if t == 0:
+                    nc.sync.dma_start(tile[:], source)
                 nc.sync.dma_start(out=c[t], in_=v[:, t, :])
         nc.sync.dma_start(out=gn_t[:], in_=gn.rearrange("(p t) o -> p (t o)", t=PACK))
 
         ident = sb("ident", [P, P], F32)
         make_identity(nc, ident[:])
 
-        def deal_words(dealt, words, ts):
-            nc.vector.tensor_copy(
+        def deal_words(copy, dealt, words, ts):
+            copy(
                 out=dealt[:].rearrange("p (t c i) -> p c t i", c=JB // 4, i=4),
                 in_=words[:].rearrange("p (c i t) -> p c t i", t=PACK, i=4)[:, :, ts, :],
             )
@@ -125,14 +126,14 @@ def tile_picked_mfield_none_po_kernel(
         first, rest, every = slice(0, 1), slice(1, PACK), slice(0, PACK)
         w1dw = sb("w1dw", [P, S], I32)
         w1ds = [sb("w1ds0", [P, JB], U8), sb("w1ds1", [P, LAST * JB], U8)]
-        deal_words(w1dw, w1w, every)
+        deal_words(nc.vector.tensor_copy, w1dw, w1w, every)
         deal_scales(nc.gpsimd, w1ds[0], w1s, first)
         for h in range(2):
             nc.vector.tensor_copy(out=xg[:, half(h)], in_=xw[:].indirect(offs_t[:, entries(half(h))]))
         deal_scales(nc.vector, w1ds[1], w1s, rest)
-        w2dw = sb("w2dw", [P, S], I32, tag="xw")
+        w2dw = sb("w2dw", [P, S], U32, tag="xw")
         w2ds = sb("w2ds", [P, S], U8, tag="w1s")
-        deal_words(w2dw, w2w, every)
+        deal_words(nc.vector.tensor_copy, w2dw, w2w, every)
         deal_scales(nc.vector, w2ds, w2s, every)
 
         def y_bank(t, js):
@@ -157,14 +158,19 @@ def tile_picked_mfield_none_po_kernel(
         part = [sb("part%d" % t, [P, S], F32)[:] for t in range(PACK)]
         g1 = [sb("g1_%d" % t, [P, S], F32)[:] for t in range(PACK)]
         g1[LAST], g2[0][LAST] = m2[0][0], m2[0][1]
-        ring = {(0, i): g1[LAST][:, half(i)] for i in range(2)}
-        ring[1, 0], ring[1, 1], ring[1, 2] = g2[0][LAST][:, half(0)], g2[0][LAST][:, half(1)], sb("ring", [P, HALF], F32)[:]
+        g1[0] = part[LAST]
+        spare_buf = [sb("ring%d" % i, [P, HALF], F32)[:] for i in range(3)]
+        own = [g1[LAST][:, half(0)], g1[LAST][:, half(1)], spare_buf[0]]
+        fetched = [g2[0][LAST][:, half(0)], g2[0][LAST][:, half(1)], spare_buf[1], spare_buf[2]]
 
         def buf(n, r, t, js):
             if r == 0:
                 return (m1, g2, m2)[n][0][t][:, js]
             h = js.start // HALF
-            return ring[min(n, 1), (PACK * h + t) % (3 if n else 2)][:, js.start - h * HALF : js.stop - h * HALF]
+            i = PACK * h + t
+            if (n, i) == (0, 2 * PACK - 1):
+                return tt[0][:, js.start - HALF : js.stop - HALF]
+            return (fetched[(0, 1, 2, 3, 0, 2, 3, 0)[i]] if n else own[i % 3])[:, js.start - h * HALF : js.stop - h * HALF]
 
         tt = [sb("tt%d" % k, [P, S], F32) for k in range(len(SUM2))]
         z16 = [sb("z16_%d" % b, [P, JB, PACK], BF16)[:] for b in range(NJB)]
@@ -209,6 +215,9 @@ def tile_picked_mfield_none_po_kernel(
 
         def add(o, a, b):
             nc.vector.tensor_tensor(out=o, in0=a, in1=b, op=ALU.add)
+
+        def add1(k, t, h):
+            add(part[t][:, half(h)], (y, part)[k][t][:, half(h)], (m1, m2)[k][0][t][:, half(h)])
 
         def tanh1(t):
             nc.scalar.activation(hh[t], part[t], ACT.Tanh)
@@ -294,38 +303,37 @@ def tile_picked_mfield_none_po_kernel(
             fused(0, 0, 0, half(h))
         for h in range(2):
             fused(1, 0, 0, half(h))
-        for h in range(2):
-            fetch(1, 0, 1, half(h))
-        for h in range(2):
-            fused(0, 0, 1, half(h))
-        for h in range(2):
-            fetch(1, 0, 2, half(h))
+        fetch(1, 0, 1, whole)
+        fused(0, 0, 1, whole)
+        fetch(1, 0, 2, whole)
         tanh1_turned(0)
         term(1, 0, 1, whole)
-        for h in range(2):
-            fetch(0, 0, 3, half(h))
-        for h in range(2):
-            fused(0, 0, 2, half(h))
+        fetch(0, 0, 3, whole)
+        fused(0, 0, 2, whole)
         tanh1_turned(1)
         back1(0)
+        add1(0, 2, 0)
         term(1, 0, 2, whole)
-        add(part[2], y[2], m1[0][2])
-        for h in range(2):
-            fetch(1, 0, 3, half(h))
+        add1(0, 2, 1)
+        fetch(1, 0, 3, whole)
+        add1(1, 2, 0)
         term(0, 0, 3, whole)
-        add(part[2], part[2], m2[0][2])
+        add1(1, 2, 1)
         back1(1)
-        add(part[3], y[3], m1[0][3])
+        for h in range(2):
+            add1(0, 3, h)
         tanh1(2)
-        term(1, 0, 3, whole)
+        for h in range(2):
+            term(1, 0, 3, half(h))
+        for h in range(2):
+            add1(1, 3, h)
         for t in range(PACK):
             add_turned(1, t, y[t], whole)
-        fused(0, 1, 0, half(0))
         fetch(1, 1, 0, half(0))
-        add(part[3], part[3], m2[0][3])
+        fused(0, 1, 0, half(0))
+        tanh1(3)
         fetch(1, 1, 1, half(0))
         fused(0, 1, 1, half(0))
-        tanh1(3)
         term(1, 1, 0, half(0))
         fetch(1, 1, 2, half(0))
         fused(0, 1, 2, half(0))
@@ -334,42 +342,43 @@ def tile_picked_mfield_none_po_kernel(
         fused(0, 1, 3, half(0))
         term(1, 1, 2, half(0))
         fetch(1, 1, 0, half(1))
-        fused(0, 1, 0, half(1))
+        fetch(0, 1, 0, half(1))
         term(1, 1, 3, half(0))
         fetch(1, 1, 1, half(1))
         fused(0, 1, 1, half(1))
         tanh2(0)
         term(1, 1, 0, half(1))
+        term(0, 1, 0, half(1))
         fetch(1, 1, 2, half(1))
         fused(0, 1, 2, half(1))
         tanh2(1)
         term(1, 1, 1, half(1))
         fetch(1, 1, 3, half(1))
-        term(1, 1, 2, half(1))
-        fused(0, 1, 3, half(1))
         gain(0)
-        add_end(0, half(1))
-        term(1, 1, 3, half(1))
-        tanh2(2)
+        term(1, 1, 2, half(1))
         quantise(0)
         second_product(0)
-        add_end(1, half(1))
-        tanh2(3)
+        fused(0, 1, 3, half(1))
+        tanh2(2)
+        term(1, 1, 3, half(1))
+        add_end(0, half(1))
         gain(1)
-        tanh_end(half(1))
-        gain(2)
+        tanh2(3)
+        add_end(1, half(1))
         quantise(1)
         second_product(1)
+        tanh_end(half(1))
+        store(0)
+        gain(2)
         gain_end(2)
         gain(3)
         quantise(2)
         second_product(2)
         gain_end(3)
-        store(0)
-        rounded_s(0)
+        store(1)
+        rounded(0)
         quantise(3)
         second_product(3)
-        store(1)
         rounded(1)
         store(2)
         planes(half(0))

@@ -25,7 +25,8 @@ QUADS = 4
 FLOPS = 2 * 2 * 512 * 512 * 512
 LAST = PACK - 1
 
-Y_BANKS = (0, 1, 2, 3, 0)
+Y_BANKS = (0, 1, 2, 6, 7, 3)
+PIECES = (slice(0, HALF), slice(HALF, HALF + JB), slice(HALF + JB, S))
 SUM1 = {0: 4, 1: 5}
 BACK1 = {0: 6, 1: 7}
 ADDED2 = ((3, 2), (3, 3))
@@ -96,12 +97,13 @@ def tile_picked_mfield_none_po_kernel(
         for q in range(1, QUADS):
             load_scales(w1s, w1_scales, q)
         nc.sync.dma_start(out=w2w[:].bitcast(I32), in_=words_of(w2_words))
+        nc.sync.dma_start(p1_t[:], p1)
+        nc.sync.dma_start(out=c1[0], in_=cj_v[0][:, 0, :])
+        nc.sync.dma_start(p2_t[:], p2)
         for q in range(QUADS):
             load_scales(w2s, w2_scales, q)
         for t in range(PACK):
-            for tile, source, c, v in ((p1_t, p1, c1, cj_v[0]), (p2_t, p2, c2, cj_v[1])):
-                if t == 0:
-                    nc.sync.dma_start(tile[:], source)
+            for c, v in ((c1, cj_v[0]), (c2, cj_v[1]))[0 if t else 1 :]:
                 nc.sync.dma_start(out=c[t], in_=v[:, t, :])
         nc.sync.dma_start(out=gn_t[:], in_=gn.rearrange("(p t) o -> p (t o)", t=PACK))
 
@@ -128,8 +130,8 @@ def tile_picked_mfield_none_po_kernel(
         w1ds = [sb("w1ds0", [P, JB], U8), sb("w1ds1", [P, LAST * JB], U8)]
         deal_words(nc.vector.tensor_copy, w1dw, w1w, every)
         deal_scales(nc.gpsimd, w1ds[0], w1s, first)
-        for h in range(2):
-            nc.vector.tensor_copy(out=xg[:, half(h)], in_=xw[:].indirect(offs_t[:, entries(half(h))]))
+        for js in PIECES:
+            nc.vector.tensor_copy(out=xg[:, js], in_=xw[:].indirect(offs_t[:, entries(js)]))
         deal_scales(nc.vector, w1ds[1], w1s, rest)
         w2dw = sb("w2dw", [P, S], U32, tag="xw")
         w2ds = sb("w2ds", [P, S], U8, tag="w1s")
@@ -137,7 +139,7 @@ def tile_picked_mfield_none_po_kernel(
         deal_scales(nc.vector, w2ds, w2s, every)
 
         def y_bank(t, js):
-            return bank[Y_BANKS[t + 1]][:] if t else bank[Y_BANKS[js.start // HALF]][:, 0:HALF]
+            return bank[Y_BANKS[t + 2]][:] if t else bank[Y_BANKS[PIECES.index(js)]][:, 0 : js.stop - js.start]
 
         def first_product(t, js):
             k, ms = (0, blk(0)) if t == 0 else (1, blk(t - 1))
@@ -291,9 +293,9 @@ def tile_picked_mfield_none_po_kernel(
                     out=out_2[0][4 * q : 4 * q + 4, :].bitcast(I32), in_=osc[32 * q : 32 * q + 4, :].bitcast(I32)
                 )
 
-        for h in range(2):
-            first_product(0, half(h))
-            field(0, half(h))
+        for js in PIECES:
+            first_product(0, js)
+            field(0, js)
         for t in range(1, PACK):
             first_product(t, whole)
             field(t, whole)
@@ -376,7 +378,7 @@ def tile_picked_mfield_none_po_kernel(
         second_product(2)
         gain_end(3)
         store(1)
-        rounded(0)
+        rounded_s(0)
         quantise(3)
         second_product(3)
         rounded(1)

@@ -175,6 +175,7 @@ def tile_picked_mfield_none_po_kernel(
             return (fetched[(0, 1, 2, 3, 0, 2, 3, 0)[i]] if n else own[i % 3])[:, js.start - h * HALF : js.stop - h * HALF]
 
         tt = [sb("tt%d" % k, [P, S], F32) for k in range(len(SUM2))]
+        late = tt[0][:]
         z16 = [sb("z16_%d" % b, [P, JB, PACK], BF16)[:] for b in range(NJB)]
         zc = [sb("zc%d" % b, [P, JB], U32) for b in range(NJB)]
         zs = [sb("zs%d" % b, [P, JB], U8) for b in range(NJB)]
@@ -207,12 +208,12 @@ def tile_picked_mfield_none_po_kernel(
             add_turned(r, t, o, js)
 
         def fetch(n, r, t, js):
-            o = buf(1, r, t, js) if n else g1[t][:, js]
+            o = buf(1, r, t, js) if n else (late if (r, t) == (1, LAST) else g1[t])[:, js]
             nc.scalar.activation(o, win[r][t][:].indirect(lists[n][:, entries(js)]), ACT.Copy)
 
         def term(n, r, t, js):
             o = buf(2 * n, r, t, js)
-            nc.vector.tensor_tensor(out=o, in0=buf(1, r, t, js) if n else g1[t][:, js], in1=(c1, c2)[n][t][:, js], op=ALU.mult)
+            nc.vector.tensor_tensor(out=o, in0=buf(1, r, t, js) if n else (late if (r, t) == (1, LAST) else g1[t])[:, js], in1=(c1, c2)[n][t][:, js], op=ALU.mult)
             add_turned(r, t, o, js)
 
         def add(o, a, b):
@@ -249,7 +250,7 @@ def tile_picked_mfield_none_po_kernel(
         end = sb("end", [P, S], F32)[:]
 
         def add_end(k, js):
-            add(end[:, js], (y[LAST], end)[k][:, js], buf(2 * k, 1, LAST, js))
+            add(end[:, js], (y[LAST], end)[k][:, js], buf(2 - 2 * k, 1, LAST, js))
 
         def tanh_end(js):
             nc.scalar.activation(part[LAST][:, js], end[:, js], ACT.Tanh)
@@ -356,19 +357,20 @@ def tile_picked_mfield_none_po_kernel(
         tanh2(1)
         term(1, 1, 1, half(1))
         fetch(1, 1, 3, half(1))
+        fetch(0, 1, 3, half(1))
         gain(0)
         term(1, 1, 2, half(1))
         quantise(0)
         second_product(0)
-        fused(0, 1, 3, half(1))
-        tanh2(2)
         term(1, 1, 3, half(1))
-        add_end(0, half(1))
+        tanh2(2)
         gain(1)
+        add_end(0, half(1))
+        term(0, 1, 3, half(1))
         tanh2(3)
-        add_end(1, half(1))
         quantise(1)
         second_product(1)
+        add_end(1, half(1))
         tanh_end(half(1))
         store(0)
         gain(2)

@@ -175,7 +175,13 @@ def tile_picked_mfield_none_po_kernel(
             return (fetched[(0, 1, 2, 3, 0, 2, 3, 0)[i]] if n else own[i % 3])[:, js.start - h * HALF : js.stop - h * HALF]
 
         tt = [sb("tt%d" % k, [P, S], F32) for k in range(len(SUM2))]
-        late = tt[0][:]
+
+        def fetched1(r, t, js):
+            if r == 0:
+                return g1[t][:, js]
+            if js.start < HALF:
+                return g2[0][2][:, half(t // LAST)]
+            return (part[LAST] if t == 0 else tt[0][:])[:, js]
         z16 = [sb("z16_%d" % b, [P, JB, PACK], BF16)[:] for b in range(NJB)]
         zc = [sb("zc%d" % b, [P, JB], U32) for b in range(NJB)]
         zs = [sb("zs%d" % b, [P, JB], U8) for b in range(NJB)]
@@ -208,12 +214,12 @@ def tile_picked_mfield_none_po_kernel(
             add_turned(r, t, o, js)
 
         def fetch(n, r, t, js):
-            o = buf(1, r, t, js) if n else (late if (r, t) == (1, LAST) else g1[t])[:, js]
+            o = buf(1, r, t, js) if n else fetched1(r, t, js)
             nc.scalar.activation(o, win[r][t][:].indirect(lists[n][:, entries(js)]), ACT.Copy)
 
         def term(n, r, t, js):
             o = buf(2 * n, r, t, js)
-            nc.vector.tensor_tensor(out=o, in0=buf(1, r, t, js) if n else (late if (r, t) == (1, LAST) else g1[t])[:, js], in1=(c1, c2)[n][t][:, js], op=ALU.mult)
+            nc.vector.tensor_tensor(out=o, in0=buf(1, r, t, js) if n else fetched1(r, t, js), in1=(c1, c2)[n][t][:, js], op=ALU.mult)
             add_turned(r, t, o, js)
 
         def add(o, a, b):
@@ -332,11 +338,12 @@ def tile_picked_mfield_none_po_kernel(
             add1(1, 3, h)
         for t in range(PACK):
             add_turned(1, t, y[t], whole)
+        fetch(0, 1, 0, half(0))
         fetch(1, 1, 0, half(0))
-        fused(0, 1, 0, half(0))
+        fused(0, 1, 1, half(0))
         tanh1(3)
         fetch(1, 1, 1, half(0))
-        fused(0, 1, 1, half(0))
+        term(0, 1, 0, half(0))
         term(1, 1, 0, half(0))
         fetch(1, 1, 2, half(0))
         fused(0, 1, 2, half(0))

@@ -87,7 +87,7 @@ def tile_picked_mfield_none_po_kernel(
 
         nc.vector.memset(xs[:].bitcast(I32), 0)
         for scales in (w1s, w2s):
-            nc.gpsimd.memset(scales[:].bitcast(I32), 0)
+            nc.vector.memset(scales[:].bitcast(I32), 0)
         nc.sync.dma_start(offs_t[:], offs)
         nc.sync.dma_start(out=w1w[:], in_=words_of(w1_words))
         for q in range(QUADS):
@@ -108,7 +108,8 @@ def tile_picked_mfield_none_po_kernel(
         nc.sync.dma_start(out=gn_t[:], in_=gn.rearrange("(p t) o -> p (t o)", t=PACK))
 
         ident = sb("ident", [P, P], F32)
-        make_identity(nc, ident[:])
+        nc.vector.memset(ident[:], 0.0)
+        make_identity(nc, ident[:], nomemset=True)
 
         def deal_words(copy, dealt, words, ts):
             copy(

@@ -135,9 +135,7 @@ def tile_picked_mfield_none_po_kernel(
             nc.vector.tensor_copy(out=xg[:, js], in_=xw[:].indirect(offs_t[:, entries(js)]))
         deal_scales(nc.vector, w1ds[1], w1s, rest)
         w2dw = sb("w2dw", [P, S], U32, tag="xw")
-        w2ds = sb("w2ds", [P, S], U8, tag="w1s")
         deal_words(nc.vector.tensor_copy, w2dw, w2w, every)
-        deal_scales(nc.vector, w2ds, w2s, every)
 
         def y_bank(t, js):
             return bank[Y_BANKS[t + 2]][:] if t else bank[Y_BANKS[PIECES.index(js)]][:, 0 : js.stop - js.start]
@@ -368,6 +366,8 @@ def tile_picked_mfield_none_po_kernel(
         fetch(0, 1, 3, half(1))
         gain(0)
         term(1, 1, 2, half(1))
+        w2ds = sb("w2ds", [P, S], U8, tag="h2")
+        deal_scales(nc.vector, w2ds, w2s, every)
         quantise(0)
         second_product(0)
         term(1, 1, 3, half(1))

@@ -337,12 +337,11 @@ def tile_picked_mfield_none_po_kernel(
             add1(1, 3, h)
         for t in range(PACK):
             add_turned(1, t, y[t], whole)
-        fetch(0, 1, 0, half(0))
         fetch(1, 1, 0, half(0))
         fused(0, 1, 1, half(0))
         tanh1(3)
         fetch(1, 1, 1, half(0))
-        term(0, 1, 0, half(0))
+        fused(0, 1, 0, half(0))
         term(1, 1, 0, half(0))
         fetch(1, 1, 2, half(0))
         fused(0, 1, 2, half(0))

@@ -388,14 +388,14 @@ def tile_picked_mfield_none_po_kernel(
         gain_end(3)
         store(1)
         rounded_s(0)
+        rounded_s(1)
         quantise(3)
         second_product(3)
-        rounded(1)
         store(2)
-        planes(half(0))
+        planes(half(0), nc.sync, half(0))
         store(3)
         rounded(2)
-        planes(blk(2), nc.sync, slice(0, LAST * JB))
+        planes(blk(2))
         rounded(3)
-        planes(blk(3), nc.scalar, blk(3))
+        planes(blk(3), nc.sync, half(1))
         store_scales()

from contextlib import ExitStack

import concourse.mybir as mybir
from concourse.masks import make_identity

F32 = mybir.dt.float32
BF16 = mybir.dt.bfloat16
I32 = mybir.dt.int32
U32 = mybir.dt.uint32
U16 = mybir.dt.uint16
U8 = mybir.dt.uint8
FP8X4 = mybir.dt.float8_e4m3fn_x4
ACT = mybir.ActivationFunctionType
ALU = mybir.AluOpType

P = 128
T = 2048
S = 512
PACK = 4
JB = 128
NJB = S // JB
HALF = S // 2
GROUP = 16
QUADS = 4
FLOPS = 2 * 2 * 512 * 512 * 512
LAST = PACK - 1

Y_BANKS = (0, 1, 2, 6, 7, 3)
PIECES = (slice(0, HALF), slice(HALF, HALF + JB), slice(HALF + JB, S))
SUM1 = {0: 4, 1: 5}
BACK1 = {0: 6, 1: 7}
ADDED2 = ((3, 2), (3, 3))
SUM2 = tuple((4 + b, [(t, b) for t in range(PACK) if (t, b) not in ADDED2]) for b in range(NJB))
Z_BANKS = (0, 1, 2, 3)
OUT_BANKS = (4, 5, 6, 7, 0)


def tile_picked_mfield_none_po_kernel(
    tc, x_words, x_scales, w1_words, w1_scales, cj1, cj2, gn, w2_words, w2_scales, offs, p1, p2, out_0, out_1, out_2
):
    nc = tc.nc
    with ExitStack() as ctx:
        keep = ctx.enter_context(tc.tile_pool(name="keep", bufs=1))
        psum = ctx.enter_context(tc.psum_pool(name="psum", bufs=1))

        def sb(name, shape, dtype, tag=None):
            return keep.tile(shape, dtype, name=name, tag=tag or name, align_bytes=64)

        bank = [psum.tile([P, S], F32, name="bank%d" % k) for k in range(8)]

        def blk(b):
            return slice(b * JB, (b + 1) * JB)

        def half(h):
            return slice(h * HALF, (h + 1) * HALF)

        whole = slice(0, S)

        def blocks_in(js):
            return range(js.start // JB, js.stop // JB)

        def entries(js):
            return slice(js.start // GROUP, js.stop // GROUP)

        def words_of(dram):
            return dram[0].rearrange("p n t -> p (n t)").bitcast(I32)

        def load_scales(tile, dram, q, queue=nc.sync):
            queue.dma_start(out=tile[32 * q : 32 * q + 4, :].bitcast(I32), in_=dram[0][4 * q : 4 * q + 4, :].bitcast(I32))

        xs = sb("xs", [P, T], U8)
        w1s = sb("w1s", [P, S], U8)
        w2s = sb("w2s", [P, S], U8)
        xw = sb("xw", [P, T], U32)
        w1w = sb("w1w", [P, S], I32)
        w2w = sb("w2w", [P, S], U32)
        offs_t = keep.tile([P, S // GROUP], U16, name="offs_t")
        p1_t = keep.tile([P, S // GROUP], U16, name="p1_t")
        p2_t = keep.tile([P, S // GROUP], U16, name="p2_t")
        lists = (p1_t, p2_t)
        ywin = [sb("y%d" % t, [P, 2 * S if t else S], F32) for t in range(PACK)]
        y = [ywin[t][:, 0:S] for t in range(PACK)]
        spare = {(0, 0): 1, (1, 0): 2, (0, 1): 3}
        c1, c2 = [[ywin[spare[n, t]][:, S : 2 * S] if (n, t) in spare else sb("c%d_%d" % (n, t), [P, S], F32)[:] for t in range(PACK)] for n in range(2)]
        gn_t = sb("gn_t", [P, PACK], F32)
        cj_v = [c.rearrange("(p t) j -> p t j", t=PACK) for c in (cj1, cj2)]

        nc.vector.memset(xs[:].bitcast(I32), 0)
        for scales in (w1s, w2s):
            nc.vector.memset(scales[:].bitcast(I32), 0)
        nc.sync.dma_start(offs_t[:], offs)
        nc.sync.dma_start(out=w1w[:], in_=words_of(w1_words))
        for q in range(QUADS):
            load_scales(xs, x_scales, q, nc.scalar if q % 2 else nc.sync)
        load_scales(w1s, w1_scales, 0)
        nc.sync.dma_start(out=xw[:].bitcast(I32), in_=words_of(x_words))
        for q in range(1, QUADS):
            load_scales(w1s, w1_scales, q)
        nc.sync.dma_start(out=w2w[:].bitcast(I32), in_=words_of(w2_words))
        nc.sync.dma_start(p1_t[:], p1)
        nc.sync.dma_start(out=c1[0], in_=cj_v[0][:, 0, :])
        nc.sync.dma_start(p2_t[:], p2)
        for q in range(QUADS):
            load_scales(w2s, w2_scales, q)
        for t in range(PACK):
            for c, v in ((c1, cj_v[0]), (c2, cj_v[1]))[0 if t else 1 :]:
                nc.sync.dma_start(out=c[t], in_=v[:, t, :])
        nc.sync.dma_start(out=gn_t[:], in_=gn.rearrange("(p t) o -> p (t o)", t=PACK))

        ident = sb("ident", [P, P], F32)
        nc.vector.memset(ident[:], 0.0)
        make_identity(nc, ident[:], nomemset=True)

        def deal_words(copy, dealt, words, ts):
            copy(
                out=dealt[:].rearrange("p (t c i) -> p c t i", c=JB // 4, i=4),
                in_=words[:].rearrange("p (c i t) -> p c t i", t=PACK, i=4)[:, :, ts, :],
            )

        def deal_scales(engine, dealt, scales, ts):
            engine.tensor_copy(
                out=dealt[:].rearrange("p (t m) -> p t m", m=JB),
                in_=scales[:].rearrange("p (m t) -> p t m", t=PACK)[:, ts, :],
            )

        xsg = sb("xsg", [P, S], U8)
        xg = sb("xg", [P, S], U32)
        nc.vector.tensor_copy(out=xsg[:], in_=xs[:].indirect(offs_t[:]))
        first, rest, every = slice(0, 1), slice(1, PACK), slice(0, PACK)
        w1dw = sb("w1dw", [P, S], I32)
        w1ds = [sb("w1ds0", [P, JB], U8), sb("w1ds1", [P, LAST * JB], U8)]
        deal_words(nc.vector.tensor_copy, w1dw, w1w, every)
        deal_scales(nc.gpsimd, w1ds[0], w1s, first)
        for js in PIECES:
            nc.vector.tensor_copy(out=xg[:, js], in_=xw[:].indirect(offs_t[:, entries(js)]))
        deal_scales(nc.vector, w1ds[1], w1s, rest)
        w2dw = sb("w2dw", [P, S], U32, tag="xw")
        deal_words(nc.vector.tensor_copy, w2dw, w2w, every)

        def y_bank(t, js):
            return bank[Y_BANKS[t + 2]][:] if t else bank[Y_BANKS[PIECES.index(js)]][:, 0 : js.stop - js.start]

        def first_product(t, js):
            k, ms = (0, blk(0)) if t == 0 else (1, blk(t - 1))
            nc.tensor.matmul_mx(
                out=y_bank(t, js), lhsT=w1dw[:, blk(t)].bitcast(FP8X4), lhsT_scale=w1ds[k][:, ms],
                rhs=xg[:, js].bitcast(FP8X4), rhs_scale=xsg[:, js], start=True, stop=True,
            )

        def field(t, js):
            nc.scalar.activation(y[t][:, js], y_bank(t, js), ACT.Copy)

        hwin = [sb("h%d" % t, [P, S], F32) for t in range(PACK)]
        hh = [hwin[t][:, 0:S] for t in range(PACK)]
        win = (ywin, hwin)
        m1 = [[sb("m1_%d" % t, [P, S], F32)[:] for t in range(PACK)]]
        g2 = [[sb("g2_%d" % t, [P, S], F32)[:] for t in range(PACK)]]
        m2 = [[sb("m2_%d" % t, [P, S], F32)[:] for t in range(PACK)]]
        part = [sb("part%d" % t, [P, S], F32)[:] for t in range(PACK)]
        g1 = [sb("g1_%d" % t, [P, S], F32)[:] for t in range(PACK)]
        g1[LAST], g2[0][LAST] = m2[0][0], m2[0][1]
        g1[0] = part[LAST]
        spare_buf = [sb("ring%d" % i, [P, HALF], F32)[:] for i in range(3)]
        own = [g1[LAST][:, half(0)], g1[LAST][:, half(1)], spare_buf[0]]
        fetched = [g2[0][LAST][:, half(0)], g2[0][LAST][:, half(1)], spare_buf[1], spare_buf[2]]

        def buf(n, r, t, js):
            if r == 0:
                return (m1, g2, m2)[n][0][t][:, js]
            h = js.start // HALF
            i = PACK * h + t
            if (n, i) == (0, 2 * PACK - 1):
                return tt[0][:, js.start - HALF : js.stop - HALF]
            return (fetched[(0, 1, 2, 3, 0, 2, 3, 0)[i]] if n else own[i % 3])[:, js.start - h * HALF : js.stop - h * HALF]

        tt = [sb("tt%d" % k, [P, S], F32) for k in range(len(SUM2))]

        def fetched1(r, t, js):
            if r == 0:
                return g1[t][:, js]
            if js.start < HALF:
                return g2[0][2][:, half(t // LAST)]
            return (part[LAST] if t == 0 else tt[0][:])[:, js]
        z16 = [sb("z16_%d" % b, [P, JB, PACK], BF16)[:] for b in range(NJB)]
        zc = [sb("zc%d" % b, [P, JB], U32) for b in range(NJB)]
        zs = [sb("zs%d" % b, [P, JB], U8) for b in range(NJB)]
        ot = [sb("ot%d" % b, [P, PACK, JB], F32) for b in range(NJB)]
        o16 = sb("o16", [P, S, PACK], BF16)
        oc = sb("oc", [P, S], U32)
        osc = sb("osc", [P, S], U8)
        out_v = out_0.rearrange("(p t) j -> p t j", t=PACK)
        out_w = words_of(out_1)

        groups = {(0, t): (SUM1[t], [(t, b) for b in range(NJB)]) for t in SUM1}
        for k, (bk, items) in enumerate(SUM2):
            groups[1, k] = (bk, items)
        count = {key: 0 for key in groups}

        def turn(dst, src, start, stop):
            nc.tensor.matmul(out=dst, lhsT=src, rhs=ident[:], is_transpose=True, start=start, stop=stop)

        def add_turned(r, t, src, js):
            for b in blocks_in(js):
                for key in groups:
                    bk, items = groups[key]
                    if key[0] == r and (t, b) in items:
                        count[key] = count[key] + 1
                        turn(bank[bk][:, blk(items.index((t, b)))], src[:, blk(b - js.start // JB)], count[key] == 1, count[key] == 3 * len(items))

        def fused(n, r, t, js):
            o = buf(2 * n, r, t, js)
            nc.vector.tensor_tensor(out=o, in0=win[r][t][:].indirect(lists[n][:, entries(js)]), in1=(c1, c2)[n][t][:, js], op=ALU.mult)
            add_turned(r, t, o, js)

        def fetch(n, r, t, js):
            o = buf(1, r, t, js) if n else fetched1(r, t, js)
            nc.scalar.activation(o, win[r][t][:].indirect(lists[n][:, entries(js)]), ACT.Copy)

        def term(n, r, t, js):
            o = buf(2 * n, r, t, js)
            nc.vector.tensor_tensor(out=o, in0=buf(1, r, t, js) if n else fetched1(r, t, js), in1=(c1, c2)[n][t][:, js], op=ALU.mult)
            add_turned(r, t, o, js)

        def add(o, a, b):
            nc.vector.tensor_tensor(out=o, in0=a, in1=b, op=ALU.add)

        def add1(k, t, h):
            add(part[t][:, half(h)], (y, part)[k][t][:, half(h)], (m1, m2)[k][0][t][:, half(h)])

        def tanh1(t):
            nc.scalar.activation(hh[t], part[t], ACT.Tanh)

        def tanh1_turned(t):
            nc.scalar.activation(part[t], bank[SUM1[t]][:], ACT.Tanh)
            for b in range(NJB):
                turn(bank[BACK1[t]][:, blk(b)], part[t][:, blk(b)], True, True)

        def back1(t):
            nc.scalar.activation(hh[t], bank[BACK1[t]][:], ACT.Copy)

        def tanh2(k):
            bk, items = SUM2[k]
            js = slice(0, len(items) * JB)
            nc.scalar.activation(tt[k][:, js], bank[bk][:, js], ACT.Tanh)
            for i, (t, b) in enumerate(items):
                turn(bank[Z_BANKS[b]][:, blk(t)], tt[k][:, blk(i)], True, True)

        def gain(b):
            k = len(SUM2[b][1])
            nc.vector.tensor_tensor(
                out=z16[b][:, :, 0:k], in0=bank[Z_BANKS[b]][:].rearrange("p (t j) -> p j t", t=PACK)[:, :, 0:k],
                in1=gn_t[:, 0:k].unsqueeze(1).to_broadcast([P, JB, k]), op=ALU.mult,
            )

        end = sb("end", [P, S], F32)[:]

        def add_end(k, js):
            add(end[:, js], (y[LAST], end)[k][:, js], buf(2 - 2 * k, 1, LAST, js))

        def tanh_end(js):
            nc.scalar.activation(part[LAST][:, js], end[:, js], ACT.Tanh)

        def gain_end(b):
            nc.vector.tensor_scalar(out=z16[b][:, :, LAST], in0=part[LAST][:, blk(b)], scalar1=gn_t[:, LAST:PACK], scalar2=None, op0=ALU.mult)

        def rounded_s(b):
            nc.scalar.copy(out=o16[:, blk(b), :], in_=bank[OUT_BANKS[b]][:].rearrange("p (t j) -> p j t", t=PACK))

        def quantise(b):
            nc.vector.quantize_mx(out=zc[b][:].bitcast(FP8X4), scales=zs[b][:], in_=z16[b].rearrange("p j t -> p (j t)"))

        def out_bank(b, t):
            return bank[OUT_BANKS[NJB if b == NJB - 1 and t >= 2 else b]]

        def second_product(b):
            for t in range(PACK):
                nc.tensor.matmul_mx(
                    out=out_bank(b, t)[:, blk(t)], lhsT=w2dw[:, blk(t)].bitcast(FP8X4), lhsT_scale=w2ds[:, blk(t)],
                    rhs=zc[b][:].bitcast(FP8X4), rhs_scale=zs[b][:], start=True, stop=True,
                )

        def store(b):
            for ts in (slice(0, 2), slice(2, PACK)) if b == NJB - 1 else (slice(0, PACK),):
                copy = nc.vector.tensor_copy if ts.start else nc.scalar.copy
                copy(out=ot[b][:, ts, :], in_=out_bank(b, ts.start)[:].rearrange("p (t j) -> p t j", t=PACK)[:, ts, :])
            nc.sync.dma_start(out=out_v[:, :, blk(b)], in_=ot[b][:])

        def rounded(b):
            nc.vector.tensor_copy(out=o16[:, blk(b), :], in_=ot[b][:].rearrange("p t j -> p j t"))

        def planes(js, queue=None, stored=None):
            nc.vector.quantize_mx(out=oc[:, js].bitcast(FP8X4), scales=osc[:, js], in_=o16[:, js, :].rearrange("p j t -> p (j t)"))
            if queue is not None:
                queue.dma_start(out=out_w[:, stored], in_=oc[:, stored].bitcast(I32))

        def store_scales():
            for q in range(QUADS):
                (nc.scalar if q < QUADS // 2 else nc.sync).dma_start(
                    out=out_2[0][4 * q : 4 * q + 4, :].bitcast(I32), in_=osc[32 * q : 32 * q + 4, :].bitcast(I32)
                )

        for js in PIECES:
            first_product(0, js)
            field(0, js)
        for t in range(1, PACK):
            first_product(t, whole)
            field(t, whole)
        add_turned(0, 0, y[0], whole)
        add_turned(0, 1, y[1], whole)
        for h in range(2):
            fused(0, 0, 0, half(h))
        for h in range(2):
            fused(1, 0, 0, half(h))
        fetch(1, 0, 1, whole)
        fused(0, 0, 1, whole)
        fetch(1, 0, 2, whole)
        tanh1_turned(0)
        term(1, 0, 1, whole)
        fetch(0, 0, 3, whole)
        fused(0, 0, 2, whole)
        tanh1_turned(1)
        back1(0)
        add1(0, 2, 0)
        term(1, 0, 2, whole)
        add1(0, 2, 1)
        fetch(1, 0, 3, whole)
        add1(1, 2, 0)
        term(0, 0, 3, whole)
        add1(1, 2, 1)
        back1(1)
        for h in range(2):
            add1(0, 3, h)
        tanh1(2)
        for h in range(2):
            term(1, 0, 3, half(h))
        for h in range(2):
            add1(1, 3, h)
        for t in range(PACK):
            add_turned(1, t, y[t], whole)
        fetch(1, 1, 0, half(0))
        fused(0, 1, 1, half(0))
        tanh1(3)
        fetch(1, 1, 1, half(0))
        fused(0, 1, 0, half(0))
        term(1, 1, 0, half(0))
        fetch(1, 1, 2, half(0))
        fused(0, 1, 2, half(0))
        term(1, 1, 1, half(0))
        fetch(1, 1, 3, half(0))
        fused(0, 1, 3, half(0))
        term(1, 1, 2, half(0))
        fetch(1, 1, 0, half(1))
        fetch(0, 1, 0, half(1))
        term(1, 1, 3, half(0))
        fetch(1, 1, 1, half(1))
        fused(0, 1, 1, half(1))
        tanh2(0)
        term(1, 1, 0, half(1))
        term(0, 1, 0, half(1))
        fetch(1, 1, 2, half(1))
        fused(0, 1, 2, half(1))
        tanh2(1)
        term(1, 1, 1, half(1))
        fetch(1, 1, 3, half(1))
        fetch(0, 1, 3, half(1))
        gain(0)
        term(1, 1, 2, half(1))
        w2ds = sb("w2ds", [P, S], U8, tag="h2")
        deal_scales(nc.vector, w2ds, w2s, every)
        quantise(0)
        second_product(0)
        term(1, 1, 3, half(1))
        tanh2(2)
        gain(1)
        add_end(0, half(1))
        term(0, 1, 3, half(1))
        tanh2(3)
        quantise(1)
        second_product(1)
        add_end(1, half(1))
        tanh_end(half(1))
        store(0)
        gain(2)
        gain_end(2)
        gain(3)
        quantise(2)
        second_product(2)
        gain_end(3)
        store(1)
        rounded_s(0)
        rounded_s(1)
        quantise(3)
        second_product(3)
        store(2)
        planes(half(0), nc.sync, half(0))
        store(3)
        rounded(2)
        planes(blk(2))
        rounded(3)
        planes(blk(3), nc.sync, half(1))
        store_scales()
